import numpy as np
import ml_dtypes


def mxq(x, axis, fmt="e4m3"):
    dtype, down = {"e4m3": (ml_dtypes.float8_e4m3fn, 7), "e5m2": (ml_dtypes.float8_e5m2, 14)}[fmt]
    v = np.moveaxis(np.asarray(x, np.float32).astype(ml_dtypes.bfloat16).astype(np.float64), axis, -1)
    blocks = v.reshape(v.shape[:-1] + (-1, 32))
    amax = np.abs(blocks).max(-1, keepdims=True)
    byte = np.maximum(np.where(amax > 0, np.frexp(amax)[1] - 1 + 127, 0) - down, 1)
    scale = np.exp2(byte - 127.0)
    codes = (blocks / scale).astype(np.float32).astype(dtype).astype(np.float64)
    return np.moveaxis((codes * scale).reshape(v.shape), -1, axis)


WIDE = False


def mx_kscale(k):
    if not WIDE:
        return np.ones(k)
    levels = np.array([24, -24, 12, -12, 0])
    if k % 512:
        return np.exp2(np.random.permutation(np.resize(levels, k // 32))).repeat(32)
    a = np.empty((k // 512, 16))
    for p in range(k // 512):
        a[p, :8] = np.random.permutation(np.resize(levels, 8))
        for g in range(8):
            far = levels[np.abs(levels - a[p, g]) >= 10]
            a[p, g + 8] = far[np.random.randint(len(far))]
    return np.exp2(a.ravel()).repeat(32)


def f64(x):
    return np.asarray(x).astype(np.float64)


def striped(idx):
    return np.tile(idx.reshape(-1, 16).T, (8, 1)).astype(np.uint16)


def unstriped(offs):
    return offs[:16].T.reshape(-1).astype(np.int64)


E2M1 = np.array([0.0, 0.5, 1.0, 1.5, 2.0, 3.0, 4.0, 6.0, -0.0, -0.5, -1.0, -1.5, -2.0, -3.0, -4.0, -6.0])


def pack_weight(w, fmt):
    k, n = w.shape
    w = f64(np.asarray(w, np.float32).astype(ml_dtypes.bfloat16)).reshape(k // 32, 32, n)
    amax = np.abs(w).max(1)
    if fmt == "e4m3":
        byte = np.frexp(amax)[1] - 1 + 127 - 7
    else:
        mant, ex = np.frexp(amax / 6.0)
        byte = np.where(mant > 0.5, ex, ex - 1) + 127
    byte = np.clip(np.where(amax > 0, byte, 1), 1, 254)
    scaled = (w * np.exp2(127.0 - byte)[:, None, :]).reshape(k, n).astype(np.float32)
    by_word = np.ascontiguousarray(scaled.reshape(k // 512, 128, 4, n).transpose(0, 1, 3, 2))
    if fmt == "e4m3":
        words = by_word.astype(ml_dtypes.float8_e4m3fn).view(np.uint8)
    else:
        c = by_word.astype(ml_dtypes.float4_e2m1fn).view(np.uint8) & 0xF
        words = (c[..., 0::2] | (c[..., 1::2] << 4)).reshape(k // 512, 128, 2 * n)
    return np.ascontiguousarray(words), np.ascontiguousarray(byte.astype(np.uint8).reshape(k // 512, 16, n))


def unpack_weight(words, scales, fmt):
    g, _, n = scales.shape
    words = np.ascontiguousarray(words).reshape(g, 128, n, -1)
    if fmt == "e4m3":
        vals = words.view(ml_dtypes.float8_e4m3fn).astype(np.float64)
    else:
        nib = np.empty((g, 128, n, 4), np.uint8)
        nib[..., 0::2] = words & 0xF
        nib[..., 1::2] = words >> 4
        vals = E2M1[nib]
    vals = vals * np.repeat(np.exp2(scales.astype(np.float64) - 127.0), 8, axis=1)[..., None]
    return vals.transpose(0, 1, 3, 2).reshape(g * 512, n)


def pack_table4(v):
    words, scales = pack_weight(v, "e2m1")
    g, t = words.shape[0] // 2, v.shape[1]
    return np.ascontiguousarray(words.reshape(g, 2, 128, t, 2).transpose(0, 2, 3, 1, 4).reshape(g, 128, t, 4)), scales


def unpack_table4(words, scales):
    g, _, t, _ = words.shape
    return unpack_weight(words.reshape(g, 128, t, 2, 2).transpose(0, 3, 1, 2, 4).reshape(2 * g, 128, 2 * t), scales, "e2m1")


def planes(y):
    n, m = y.shape
    v = y.astype(np.float32).astype(ml_dtypes.bfloat16).astype(np.float64).reshape(n // 32, 32, m)
    top = np.abs(v).max(1)
    byte = np.clip(np.where(top > 0, np.frexp(top)[1] - 1 + 127 - 7, 1), 1, 254)
    codes = (v * np.exp2(127.0 - byte)[:, None, :]).reshape(n, m).astype(np.float32).astype(ml_dtypes.float8_e4m3fn).view(np.uint8)
    words = codes.reshape(n // 512, 128, 4, m).transpose(0, 1, 3, 2)
    return np.ascontiguousarray(words), np.ascontiguousarray(byte.astype(np.uint8).reshape(n // 512, 16, m))


def sigm(f):
    return 1.0 / (1.0 + np.exp(-np.maximum(f, -700.0)))


K, N, T, J = 1024, 512, 2048, 1024


def setup_inputs():
    n = np.random.standard_normal
    s = mx_kscale(K)[:, None]
    p_tab = pack_table4(n((K, T)) * s)
    p_wa = pack_weight(n((K, N)) / np.sqrt(2 * K) / s, "e4m3")
    p_wc = pack_weight(n((K, N)) / np.sqrt(K) / s, "e2m1")
    return {
        "tab_words": p_tab[0],
        "tab_scales": p_tab[1],
        "wa_words": p_wa[0],
        "wa_scales": p_wa[1],
        "wb": (n((K, N)) / np.sqrt(2 * K) / s).astype(np.float32),
        "wc_words": p_wc[0],
        "wc_scales": p_wc[1],
        "wgo": np.tile(np.random.uniform(0.5, 2.0, J), (128, 1)).astype(np.float32),
        "offs": striped(np.random.permutation(T)[:J]),
        "offs2": striped(np.random.permutation(T)[:J]),
    }


def reference(tab_words, tab_scales, wa_words, wa_scales, wb, wc_words, wc_scales, wgo, offs, offs2):
    idx = unstriped(offs)
    idx2 = unstriped(offs2)
    tab_ = unpack_table4(tab_words, tab_scales)[:, idx]
    tabb_ = unpack_table4(tab_words, tab_scales)[:, idx2]
    wa_ = unpack_weight(wa_words, wa_scales, "e4m3")
    wb_ = mxq(f64(wb), 0, "e4m3")
    za = wa_.T @ tabb_ + wb_.T @ tab_
    eta = sigm(za)
    wc_ = unpack_weight(wc_words, wc_scales, "e2m1")
    ms = wc_.T @ tab_
    out = np.zeros((N, T))
    out[:, idx2] = f64(wgo)[0] * (np.maximum(eta * ms, 0.0))
    return (out,) + planes(out)

@@ -1,0 +1,235 @@
+from contextlib import ExitStack
+
+import concourse.mybir as mybir
+
+K, N, T, J = 1024, 512, 2048, 1024
+FLOPS = 3 * 2 * K * N * J
+
+F32 = mybir.dt.float32
+BF16 = mybir.dt.bfloat16
+I32 = mybir.dt.int32
+U32 = mybir.dt.uint32
+U16 = mybir.dt.uint16
+U8 = mybir.dt.uint8
+FP8X4 = mybir.dt.float8_e4m3fn_x4
+FP4X4 = mybir.dt.float4_e2m1fn_x4
+MULT = mybir.AluOpType.mult
+MAX = mybir.AluOpType.max
+SIGMOID = mybir.ActivationFunctionType.Sigmoid
+
+P = 128
+PACK = 4
+PASSES = K // (P * PACK)
+HALF = 512
+HALVES = J // HALF
+QUADS = 4
+ROWS = 4
+CHUNK = 512
+CHUNKS = T // CHUNK
+SLICE_ORDER = (2, 0, 1, 3)
+WINDOWS = 3
+
+
+def tile_list_rgg_reluP_kernel(
+    tc, tab_words, tab_scales, wa_words, wa_scales, wb, wc_words, wc_scales, wgo, offs, offs2, out_0, out_1, out_2
+):
+    nc = tc.nc
+    with ExitStack() as ctx:
+        held = ctx.enter_context(tc.tile_pool(name="held", bufs=1))
+        keep = ctx.enter_context(tc.tile_pool(name="keep", bufs=1))
+        psum = ctx.enter_context(tc.psum_pool(name="psum", bufs=1))
+
+        src_list = held.tile([P, J // 16], U16, name="src_list")
+        dst_list = held.tile([P, J // 16], U16, name="dst_list")
+        lists = (src_list, dst_list)
+        nc.sync.dma_start(src_list[:], offs)
+        nc.sync.dma_start(dst_list[:], offs2)
+
+        tab_sc = keep.tile([P, T], U8, name="tab_sc", align_bytes=64)
+        nc.vector.memset(tab_sc[:].bitcast(I32), 0)
+        for q in range(QUADS):
+            nc.scalar.dma_start(
+                tab_sc[32 * q : 32 * q + PASSES * ROWS, :].bitcast(I32),
+                tab_scales[:, ROWS * q : ROWS * (q + 1), :].bitcast(I32),
+            )
+        tab_w = keep.tile([P, T], I32, name="tab_w", align_bytes=64)
+        nc.sync.dma_start(tab_w[:], tab_words[0].rearrange("p t i -> p (t i)").bitcast(I32))
+
+        wb_raw = [keep.tile([P, PACK, N], F32, name="wb_raw%d" % a) for a in range(PASSES)]
+        wb_rows = wb.rearrange("(a p i) n -> a p i n", p=P, i=PACK)
+        nc.sync.dma_start(wb_raw[0][:], wb_rows[0])
+        wc_raw = keep.tile([P, PASSES, 2 * N], U8, name="wc_raw")
+        nc.sync.dma_start(wc_raw[:].bitcast(I32), wc_words.rearrange("a p b -> p a b").bitcast(I32))
+        wa_raw = keep.tile([P, PASSES, N], I32, name="wa_raw")
+        nc.sync.dma_start(wa_raw[:], wa_words.rearrange("a p n i -> p a (n i)").bitcast(I32))
+
+        nc.sync.dma_start(wb_raw[1][:], wb_rows[1])
+
+        w_sc_raw = keep.tile([P, PASSES, N], U8, name="w_sc_raw")
+        nc.vector.memset(w_sc_raw[:].bitcast(I32), 0)
+        for w, scales in enumerate((wa_scales, wc_scales)):
+            for q in range(QUADS):
+                first = 32 * q + ROWS * w
+                nc.scalar.dma_start(
+                    w_sc_raw[first : first + ROWS, :, :].bitcast(I32),
+                    scales[:, ROWS * q : ROWS * (q + 1), :].rearrange("a r n -> r a n").bitcast(I32),
+                )
+        edge_w = keep.tile([P, J], F32, name="edge_w")
+        nc.sync.dma_start(edge_w[:], wgo)
+
+        wc_sc = keep.tile([P, PASSES, N], U8, name="wc_sc", align_bytes=64)
+        nc.vector.memset(wc_sc[:].bitcast(I32), 0)
+        late_sc = keep.tile([P, 2, J], U8, name="late_sc", align_bytes=64)
+        nc.vector.memset(late_sc[:].bitcast(I32), 0)
+        windows = [keep.tile([P, T], F32, name="window0")]
+        nc.vector.memset(windows[0][:], 0.0)
+
+        picked_sc = keep.tile([P, 2, J], U8, name="picked_sc", align_bytes=64)
+        picked = [
+            [keep.tile([P, PASSES, 2 * HALF], U8, name="picked%d_%d" % (l, h), align_bytes=64) for h in range(HALVES)]
+            for l in range(2)
+        ]
+
+        def cols(h):
+            return slice(h * HALF // 16, (h + 1) * HALF // 16)
+
+        def gather_scales():
+            for l in range(2):
+                nc.vector.tensor_copy(picked_sc[:, l, :], tab_sc[:].indirect(lists[l][:]))
+            nc.sync.dma_start(late_sc[0 : P - ROWS, :, :].bitcast(I32), picked_sc[ROWS:P, :, :].bitcast(I32))
+
+        def gather_words(h):
+            both = []
+            for l in range(2):
+                pair = keep.tile([P, HALF], U32, name="pair%d_%d" % (l, h), tag="pair%d" % l if h == 0 else "stage%d" % l, align_bytes=64)
+                nc.vector.tensor_copy(pair[:], tab_w[:].bitcast(U32).indirect(lists[l][:, cols(h)]))
+                both.append(pair)
+            for l in range(2):
+                nc.vector.tensor_copy(
+                    picked[l][h][:].bitcast(U16), both[l][:].bitcast(U16).rearrange("p (j a) -> p a j", a=PASSES)
+                )
+
+        wa_q = keep.tile([P, PASSES, N], I32, name="wa_q", tag="gate0", align_bytes=64)
+        wa_sc = keep.tile([P, PASSES, N], U8, name="wa_sc", tag="gate1", align_bytes=64)
+        wc_q = keep.tile([P, PASSES, 2 * N], U8, name="wc_q", align_bytes=64)
+        wb_q = [keep.tile([P, N], U32, name="wb_q%d" % a, tag="gate%d" % (2 + a), align_bytes=64) for a in range(PASSES)]
+        wb_sc = [keep.tile([P, N], U8, name="wb_sc%d" % a, align_bytes=64) for a in range(PASSES)]
+
+        def deal_packed_weights():
+            nc.vector.tensor_copy(
+                wa_sc[:].rearrange("p a (t m) -> p a t m", t=PACK), w_sc_raw[:].rearrange("p a (m t) -> p a t m", t=PACK)
+            )
+            nc.sync.dma_start(wc_sc[0 : P - ROWS, :, :].bitcast(I32), wa_sc[ROWS:P, :, :].bitcast(I32))
+            nc.vector.tensor_copy(
+                wc_q[:].bitcast(U16).rearrange("p a (t m) -> p a t m", t=PACK),
+                wc_raw[:].bitcast(U16).rearrange("p a (m t) -> p a t m", t=PACK),
+            )
+            nc.vector.tensor_copy(
+                wa_q[:].rearrange("p a (t m e) -> p a m t e", t=PACK, e=4),
+                wa_raw[:].rearrange("p a (m e t) -> p a m t e", t=PACK, e=4),
+            )
+
+        def quantise_wb():
+            for a in range(PASSES):
+                grouped = keep.tile([P, N * PACK], BF16, name="wb_grouped%d" % a, tag="stage%d" % a, align_bytes=64)
+                nc.scalar.copy(
+                    grouped[:].rearrange("p (t m i) -> p m i t", t=PACK, i=PACK),
+                    wb_raw[a][:].rearrange("p i (m t) -> p m i t", t=PACK),
+                )
+                nc.vector.quantize_mx(out=wb_q[a][:].bitcast(FP8X4), scales=wb_sc[a][:], in_=grouped[:])
+
+        gather_scales()
+        gather_words(0)
+        deal_packed_weights()
+        quantise_wb()
+        gather_words(1)
+        for l in range(2):
+            window = keep.tile([P, T], F32, name="window%d" % (l + 1), tag="stage%d" % l, align_bytes=64)
+            nc.gpsimd.memset(window[:], 0.0)
+            windows.append(window)
+
+        def moving(l, h, a):
+            plane = picked_sc if a == 0 else late_sc
+            return dict(rhs=picked[l][h][:, a, :].bitcast(FP4X4), rhs_scale=plane[:, l, h * HALF : (h + 1) * HALF])
+
+        def gate(t, h):
+            m = slice(t * P, (t + 1) * P)
+            za = psum.tile([P, HALF], F32, name="za", bufs=3)
+            for a in range(PASSES):
+                nc.tensor.matmul_mx(
+                    out=za[:], lhsT=wa_q[:, a, m].bitcast(FP8X4), lhsT_scale=wa_sc[:, a, m],
+                    start=(a == 0), stop=False, **moving(1, h, a),
+                )
+            for a in range(PASSES):
+                nc.tensor.matmul_mx(
+                    out=za[:], lhsT=wb_q[a][:, m].bitcast(FP8X4), lhsT_scale=wb_sc[a][:, m],
+                    start=False, stop=(a == PASSES - 1), **moving(0, h, a),
+                )
+            eta = keep.tile([P, HALF], F32, name="eta%d_%d" % (t, h))
+            nc.scalar.activation(eta[:], za[:], SIGMOID)
+            return eta
+
+        def message(t, h):
+            ms = psum.tile([P, HALF], F32, name="ms", bufs=5)
+            for a in range(PASSES):
+                nc.tensor.matmul_mx(
+                    out=ms[:],
+                    lhsT=wc_q[:, a, 2 * t * P : 2 * (t + 1) * P].bitcast(FP4X4),
+                    lhsT_scale=wc_sc[:, a, t * P : (t + 1) * P],
+                    start=(a == 0),
+                    stop=(a == PASSES - 1),
+                    **moving(0, h, a),
+                )
+            return ms
+
+        steps = [(s, h) for s in range(PACK) for h in range(HALVES)]
+        etas = []
+
+        def gated_message(i):
+            while len(etas) < min(max(2 * i, 1), len(steps)):
+                s, h = steps[len(etas)]
+                etas.append(gate(SLICE_ORDER[s], h))
+            s, h = steps[i]
+            ms = message(SLICE_ORDER[s], h)
+            nc.vector.scalar_tensor_tensor(gated[s][:, h * HALF : (h + 1) * HALF], ms[:], 0.0, etas[i][:], MAX, MULT)
+
+        gated = [keep.tile([P, J], F32, name="gated%d" % s) for s in range(PACK)]
+        for i in range(len(steps)):
+            gated_message(i)
+        y_bf = [
+            keep.tile([P, CHUNK, PACK], BF16, name="y_bf%d" % c, tag="gate%d" % c, align_bytes=64) for c in range(CHUNKS)
+        ]
+        y_sc = keep.tile([P, T], U8, name="y_sc", align_bytes=64)
+        out_rows = out_0.rearrange("(p t) c -> t p c", t=PACK)
+        out_words = out_1[0].rearrange("p c i -> p (c i)").bitcast(I32)
+
+        for s, t in enumerate(SLICE_ORDER):
+            window = windows[s % WINDOWS]
+            width = HALF if s == 0 else J
+            for j in range(0, J, width):
+                nc.vector.tensor_tensor(
+                    window[:].indirect(dst_list[:, j // 16 : (j + width) // 16]),
+                    gated[s][:, j : j + width],
+                    edge_w[:, j : j + width],
+                    MULT,
+                )
+            nc.sync.dma_start(out_rows[t], window[:])
+            for c in range(CHUNKS):
+                part = window[:, c * CHUNK : (c + 1) * CHUNK]
+                if s == PACK - 1 and c < CHUNKS // 2:
+                    nc.vector.tensor_copy(y_bf[c][:, :, t], part)
+                else:
+                    nc.scalar.copy(y_bf[c][:, :, t], part)
+
+        for c in range(CHUNKS):
+            codes = keep.tile([P, CHUNK], I32, name="y_codes%d" % c, align_bytes=64)
+            nc.vector.quantize_mx(
+                out=codes[:].bitcast(FP8X4),
+                scales=y_sc[:, c * CHUNK : (c + 1) * CHUNK],
+                in_=y_bf[c][:].rearrange("p c i -> p (c i)"),
+            )
+            nc.sync.dma_start(out_words[:, c * CHUNK : (c + 1) * CHUNK], codes[:])
+        for q in range(QUADS):
+            (nc.scalar if q % 2 else nc.sync).dma_start(
+                out_2[0, ROWS * q : ROWS * (q + 1), :].bitcast(I32), y_sc[32 * q : 32 * q + ROWS, :].bitcast(I32)
+            )

@@ -16,6 +16,7 @@ FP4X4 = mybir.dt.float4_e2m1fn_x4
 MULT = mybir.AluOpType.mult
 MAX = mybir.AluOpType.max
 SIGMOID = mybir.ActivationFunctionType.Sigmoid
+RELU = mybir.ActivationFunctionType.Relu
 
 P = 128
 PACK = 4
@@ -26,8 +27,9 @@ QUADS = 4
 ROWS = 4
 CHUNK = 512
 CHUNKS = T // CHUNK
-SLICE_ORDER = (2, 0, 1, 3)
-WINDOWS = 3
+SLICE_ORDER = (0, 1, 2, 3)
+WINDOWS = 4
+LIVE = 32 - PASSES * ROWS
 
 
 def tile_list_rgg_reluP_kernel(
@@ -45,44 +47,45 @@ def tile_list_rgg_reluP_kernel(
         nc.sync.dma_start(src_list[:], offs)
         nc.sync.dma_start(dst_list[:], offs2)
 
+        w_sc_raw = keep.tile([P, PASSES, N], U8, name="w_sc_raw")
+        nc.gpsimd.memset(w_sc_raw[:].bitcast(I32), 0)
         tab_sc = keep.tile([P, T], U8, name="tab_sc", align_bytes=64)
-        nc.vector.memset(tab_sc[:].bitcast(I32), 0)
         for q in range(QUADS):
-            nc.scalar.dma_start(
-                tab_sc[32 * q : 32 * q + PASSES * ROWS, :].bitcast(I32),
+            nc.gpsimd.memset(tab_sc[32 * q : 32 * q + LIVE, :].bitcast(I32), 0)
+            nc.sync.dma_start(
+                tab_sc[32 * q + LIVE : 32 * (q + 1), :].bitcast(I32),
                 tab_scales[:, ROWS * q : ROWS * (q + 1), :].bitcast(I32),
             )
         tab_w = keep.tile([P, T], I32, name="tab_w", align_bytes=64)
-        nc.sync.dma_start(tab_w[:], tab_words[0].rearrange("p t i -> p (t i)").bitcast(I32))
 
         wb_raw = [keep.tile([P, PACK, N], F32, name="wb_raw%d" % a) for a in range(PASSES)]
         wb_rows = wb.rearrange("(a p i) n -> a p i n", p=P, i=PACK)
         nc.sync.dma_start(wb_raw[0][:], wb_rows[0])
+        nc.sync.dma_start(tab_w[:], tab_words[0].rearrange("p t i -> p (t i)").bitcast(I32))
+        for w, scales in enumerate((wa_scales, wc_scales)):
+            for q in range(QUADS):
+                first = 32 * q + ROWS * w
+                nc.sync.dma_start(
+                    w_sc_raw[first : first + ROWS, :, :].bitcast(I32),
+                    scales[:, ROWS * q : ROWS * (q + 1), :].rearrange("a r n -> r a n").bitcast(I32),
+                )
+        nc.sync.dma_start(wb_raw[1][:], wb_rows[1])
         wc_raw = keep.tile([P, PASSES, 2 * N], U8, name="wc_raw")
         nc.sync.dma_start(wc_raw[:].bitcast(I32), wc_words.rearrange("a p b -> p a b").bitcast(I32))
         wa_raw = keep.tile([P, PASSES, N], I32, name="wa_raw")
         nc.sync.dma_start(wa_raw[:], wa_words.rearrange("a p n i -> p a (n i)").bitcast(I32))
 
-        nc.sync.dma_start(wb_raw[1][:], wb_rows[1])
 
-        w_sc_raw = keep.tile([P, PASSES, N], U8, name="w_sc_raw")
-        nc.vector.memset(w_sc_raw[:].bitcast(I32), 0)
-        for w, scales in enumerate((wa_scales, wc_scales)):
-            for q in range(QUADS):
-                first = 32 * q + ROWS * w
-                nc.scalar.dma_start(
-                    w_sc_raw[first : first + ROWS, :, :].bitcast(I32),
-                    scales[:, ROWS * q : ROWS * (q + 1), :].rearrange("a r n -> r a n").bitcast(I32),
-                )
         edge_w = keep.tile([P, J], F32, name="edge_w")
         nc.sync.dma_start(edge_w[:], wgo)
 
-        wc_sc = keep.tile([P, PASSES, N], U8, name="wc_sc", align_bytes=64)
-        nc.vector.memset(wc_sc[:].bitcast(I32), 0)
-        late_sc = keep.tile([P, 2, J], U8, name="late_sc", align_bytes=64)
-        nc.vector.memset(late_sc[:].bitcast(I32), 0)
-        windows = [keep.tile([P, T], F32, name="window0")]
-        nc.vector.memset(windows[0][:], 0.0)
+        wc_sc = keep.tile([P, PASSES, N], U8, name="wc_sc", tag="gate1", align_bytes=64)
+        nc.gpsimd.memset(wc_sc[:].bitcast(I32), 0)
+        late_sc = keep.tile([P, PASSES, 2, J], U8, name="late_sc", align_bytes=64)
+        nc.gpsimd.memset(late_sc[:].bitcast(I32), 0)
+        windows = [keep.tile([P, T], F32, name="window%d" % i) for i in range(WINDOWS - 1)]
+        for window in windows:
+            nc.gpsimd.memset(window[:], 0.0)
 
         picked_sc = keep.tile([P, 2, J], U8, name="picked_sc", align_bytes=64)
         picked = [
@@ -96,7 +99,9 @@ def tile_list_rgg_reluP_kernel(
         def gather_scales():
             for l in range(2):
                 nc.vector.tensor_copy(picked_sc[:, l, :], tab_sc[:].indirect(lists[l][:]))
-            nc.sync.dma_start(late_sc[0 : P - ROWS, :, :].bitcast(I32), picked_sc[ROWS:P, :, :].bitcast(I32))
+            for a in range(PASSES):
+                shift = LIVE + ROWS * a
+                nc.sync.dma_start(late_sc[0 : P - shift, a, :, :].bitcast(I32), picked_sc[shift:P, :, :].bitcast(I32))
 
         def gather_words(h):
             both = []
@@ -109,10 +114,10 @@ def tile_list_rgg_reluP_kernel(
                     picked[l][h][:].bitcast(U16), both[l][:].bitcast(U16).rearrange("p (j a) -> p a j", a=PASSES)
                 )
 
-        wa_q = keep.tile([P, PASSES, N], I32, name="wa_q", tag="gate0", align_bytes=64)
-        wa_sc = keep.tile([P, PASSES, N], U8, name="wa_sc", tag="gate1", align_bytes=64)
-        wc_q = keep.tile([P, PASSES, 2 * N], U8, name="wc_q", align_bytes=64)
-        wb_q = [keep.tile([P, N], U32, name="wb_q%d" % a, tag="gate%d" % (2 + a), align_bytes=64) for a in range(PASSES)]
+        wa_q = keep.tile([P, PASSES, N], I32, name="wa_q", align_bytes=64)
+        wa_sc = keep.tile([P, PASSES, N], U8, name="wa_sc", align_bytes=64)
+        wc_q = keep.tile([P, PASSES, 2 * N], U8, name="wc_q", tag="gate0", align_bytes=64)
+        wb_q = [keep.tile([P, N], U32, name="wb_q%d" % a, align_bytes=64) for a in range(PASSES)]
         wb_sc = [keep.tile([P, N], U8, name="wb_sc%d" % a, align_bytes=64) for a in range(PASSES)]
 
         def deal_packed_weights():
@@ -143,18 +148,16 @@ def tile_list_rgg_reluP_kernel(
         deal_packed_weights()
         quantise_wb()
         gather_words(1)
-        for l in range(2):
-            window = keep.tile([P, T], F32, name="window%d" % (l + 1), tag="stage%d" % l, align_bytes=64)
-            nc.gpsimd.memset(window[:], 0.0)
-            windows.append(window)
+        window = keep.tile([P, T], F32, name="window3", tag="stage1", align_bytes=64)
+        nc.gpsimd.memset(window[:], 0.0)
+        windows.append(window)
 
         def moving(l, h, a):
-            plane = picked_sc if a == 0 else late_sc
-            return dict(rhs=picked[l][h][:, a, :].bitcast(FP4X4), rhs_scale=plane[:, l, h * HALF : (h + 1) * HALF])
+            return dict(rhs=picked[l][h][:, a, :].bitcast(FP4X4), rhs_scale=late_sc[:, a, l, h * HALF : (h + 1) * HALF])
 
         def gate(t, h):
             m = slice(t * P, (t + 1) * P)
-            za = psum.tile([P, HALF], F32, name="za", bufs=3)
+            za = psum.tile([P, HALF], F32, name="za", bufs=4)
             for a in range(PASSES):
                 nc.tensor.matmul_mx(
                     out=za[:], lhsT=wa_q[:, a, m].bitcast(FP8X4), lhsT_scale=wa_sc[:, a, m],
@@ -165,12 +168,13 @@ def tile_list_rgg_reluP_kernel(
                     out=za[:], lhsT=wb_q[a][:, m].bitcast(FP8X4), lhsT_scale=wb_sc[a][:, m],
                     start=False, stop=(a == PASSES - 1), **moving(0, h, a),
                 )
-            eta = keep.tile([P, HALF], F32, name="eta%d_%d" % (t, h))
+            last = (t, h) == (SLICE_ORDER[-1], HALVES - 1)
+            eta = keep.tile([P, HALF], F32, name="eta", tag="gate2" if last else "eta%d_%d" % (t, h), align_bytes=64)
             nc.scalar.activation(eta[:], za[:], SIGMOID)
             return eta
 
         def message(t, h):
-            ms = psum.tile([P, HALF], F32, name="ms", bufs=5)
+            ms = psum.tile([P, HALF], F32, name="ms", bufs=4)
             for a in range(PASSES):
                 nc.tensor.matmul_mx(
                     out=ms[:],
@@ -183,19 +187,20 @@ def tile_list_rgg_reluP_kernel(
             return ms
 
         steps = [(s, h) for s in range(PACK) for h in range(HALVES)]
-        etas = []
-
-        def gated_message(i):
-            while len(etas) < min(max(2 * i, 1), len(steps)):
-                s, h = steps[len(etas)]
-                etas.append(gate(SLICE_ORDER[s], h))
-            s, h = steps[i]
+        values = [keep.tile([P, J], F32, name="values%d" % s) for s in range(PACK)]
+        for i, (s, h) in enumerate(steps):
+            js = slice(h * HALF, (h + 1) * HALF)
+            eta = gate(SLICE_ORDER[s], h)
             ms = message(SLICE_ORDER[s], h)
-            nc.vector.scalar_tensor_tensor(gated[s][:, h * HALF : (h + 1) * HALF], ms[:], 0.0, etas[i][:], MAX, MULT)
-
-        gated = [keep.tile([P, J], F32, name="gated%d" % s) for s in range(PACK)]
-        for i in range(len(steps)):
-            gated_message(i)
+            part = keep.tile([P, HALF], F32, name="part%d" % i)
+            if i == 0:
+                nc.vector.scalar_tensor_tensor(part[:], ms[:], 0.0, eta[:], MAX, MULT)
+                nc.vector.tensor_tensor(values[s][:, js], part[:], edge_w[:, js], MULT)
+            else:
+                kept = keep.tile([P, HALF], F32, name="kept", tag="gate3" if i == len(steps) - 1 else "kept%d" % i, align_bytes=64)
+                nc.scalar.activation(kept[:], ms[:], RELU)
+                nc.gpsimd.tensor_tensor(part[:], eta[:], edge_w[:, js], MULT)
+                nc.gpsimd.tensor_tensor(values[s][:, js], part[:], kept[:], MULT)
         y_bf = [
             keep.tile([P, CHUNK, PACK], BF16, name="y_bf%d" % c, tag="gate%d" % c, align_bytes=64) for c in range(CHUNKS)
         ]
@@ -205,19 +210,20 @@ def tile_list_rgg_reluP_kernel(
 
         for s, t in enumerate(SLICE_ORDER):
             window = windows[s % WINDOWS]
-            width = HALF if s == 0 else J
+            width = HALF if s < 2 else J
             for j in range(0, J, width):
-                nc.vector.tensor_tensor(
-                    window[:].indirect(dst_list[:, j // 16 : (j + width) // 16]),
-                    gated[s][:, j : j + width],
-                    edge_w[:, j : j + width],
-                    MULT,
+                nc.vector.tensor_copy(
+                    window[:].indirect(dst_list[:, j // 16 : (j + width) // 16]), values[s][:, j : j + width]
                 )
             nc.sync.dma_start(out_rows[t], window[:])
             for c in range(CHUNKS):
                 part = window[:, c * CHUNK : (c + 1) * CHUNK]
                 if s == PACK - 1 and c < CHUNKS // 2:
                     nc.vector.tensor_copy(y_bf[c][:, :, t], part)
+                elif t < 2 and c >= CHUNKS // 2:
+                    nc.gpsimd.tensor_copy(y_bf[c][:, :, t], part)
+                elif t == 2 and c < CHUNKS // 2:
+                    nc.scalar.copy(y_bf[c][:, :, 2:4], part.unsqueeze(2).to_broadcast([P, CHUNK, 2]))
                 else:
                     nc.scalar.copy(y_bf[c][:, :, t], part)
 

@@ -21,15 +21,18 @@ RELU = mybir.ActivationFunctionType.Relu
 P = 128
 PACK = 4
 PASSES = K // (P * PACK)
+LISTS = 2
 HALF = 512
 HALVES = J // HALF
-QUADS = 4
+QUAD = 32
+QUADS = P // QUAD
 ROWS = 4
+SPARE = QUAD - PASSES * ROWS
+LINE = 4
 CHUNK = 512
 CHUNKS = T // CHUNK
-SLICE_ORDER = (0, 1, 2, 3)
-WINDOWS = 4
-LIVE = 32 - PASSES * ROWS
+SHARED = CHUNKS // 2
+BANKS = 4
 
 
 def tile_list_rgg_reluP_kernel(
@@ -51,9 +54,9 @@ def tile_list_rgg_reluP_kernel(
         nc.gpsimd.memset(w_sc_raw[:].bitcast(I32), 0)
         tab_sc = keep.tile([P, T], U8, name="tab_sc", align_bytes=64)
         for q in range(QUADS):
-            nc.gpsimd.memset(tab_sc[32 * q : 32 * q + LIVE, :].bitcast(I32), 0)
+            nc.gpsimd.memset(tab_sc[QUAD * q : QUAD * q + SPARE, :].bitcast(I32), 0)
             nc.sync.dma_start(
-                tab_sc[32 * q + LIVE : 32 * (q + 1), :].bitcast(I32),
+                tab_sc[QUAD * q + SPARE : QUAD * (q + 1), :].bitcast(I32),
                 tab_scales[:, ROWS * q : ROWS * (q + 1), :].bitcast(I32),
             )
         tab_w = keep.tile([P, T], I32, name="tab_w", align_bytes=64)
@@ -64,7 +67,7 @@ def tile_list_rgg_reluP_kernel(
         nc.sync.dma_start(tab_w[:], tab_words[0].rearrange("p t i -> p (t i)").bitcast(I32))
         for w, scales in enumerate((wa_scales, wc_scales)):
             for q in range(QUADS):
-                first = 32 * q + ROWS * w
+                first = QUAD * q + ROWS * w
                 nc.sync.dma_start(
                     w_sc_raw[first : first + ROWS, :, :].bitcast(I32),
                     scales[:, ROWS * q : ROWS * (q + 1), :].rearrange("a r n -> r a n").bitcast(I32),
@@ -74,44 +77,41 @@ def tile_list_rgg_reluP_kernel(
         nc.sync.dma_start(wc_raw[:].bitcast(I32), wc_words.rearrange("a p b -> p a b").bitcast(I32))
         wa_raw = keep.tile([P, PASSES, N], I32, name="wa_raw")
         nc.sync.dma_start(wa_raw[:], wa_words.rearrange("a p n i -> p a (n i)").bitcast(I32))
-
-
         edge_w = keep.tile([P, J], F32, name="edge_w")
         nc.sync.dma_start(edge_w[:], wgo)
 
         wc_sc = keep.tile([P, PASSES, N], U8, name="wc_sc", tag="gate1", align_bytes=64)
         nc.gpsimd.memset(wc_sc[:].bitcast(I32), 0)
-        late_sc = keep.tile([P, PASSES, 2, J], U8, name="late_sc", align_bytes=64)
-        nc.gpsimd.memset(late_sc[:].bitcast(I32), 0)
-        windows = [keep.tile([P, T], F32, name="window%d" % i) for i in range(WINDOWS - 1)]
+        edge_sc = keep.tile([P, PASSES, LISTS, J], U8, name="edge_sc", align_bytes=64)
+        nc.gpsimd.memset(edge_sc[:].bitcast(I32), 0)
+        windows = [keep.tile([P, T], F32, name="window%d" % t) for t in range(PACK - 1)]
         for window in windows:
             nc.gpsimd.memset(window[:], 0.0)
 
-        picked_sc = keep.tile([P, 2, J], U8, name="picked_sc", align_bytes=64)
+        picked_sc = keep.tile([P, LISTS, J], U8, name="picked_sc", align_bytes=64)
         picked = [
             [keep.tile([P, PASSES, 2 * HALF], U8, name="picked%d_%d" % (l, h), align_bytes=64) for h in range(HALVES)]
-            for l in range(2)
+            for l in range(LISTS)
         ]
 
-        def cols(h):
-            return slice(h * HALF // 16, (h + 1) * HALF // 16)
-
         def gather_scales():
-            for l in range(2):
+            for l in range(LISTS):
                 nc.vector.tensor_copy(picked_sc[:, l, :], tab_sc[:].indirect(lists[l][:]))
             for a in range(PASSES):
-                shift = LIVE + ROWS * a
-                nc.sync.dma_start(late_sc[0 : P - shift, a, :, :].bitcast(I32), picked_sc[shift:P, :, :].bitcast(I32))
+                shift = SPARE + ROWS * a
+                nc.sync.dma_start(edge_sc[0 : P - shift, a, :, :].bitcast(I32), picked_sc[shift:P, :, :].bitcast(I32))
 
         def gather_words(h):
-            both = []
-            for l in range(2):
-                pair = keep.tile([P, HALF], U32, name="pair%d_%d" % (l, h), tag="pair%d" % l if h == 0 else "stage%d" % l, align_bytes=64)
-                nc.vector.tensor_copy(pair[:], tab_w[:].bitcast(U32).indirect(lists[l][:, cols(h)]))
-                both.append(pair)
-            for l in range(2):
+            pairs = []
+            for l in range(LISTS):
+                tag = "pair%d" % l if h == 0 else "stage%d" % l
+                pair = keep.tile([P, HALF], U32, name="pair%d_%d" % (l, h), tag=tag, align_bytes=64)
+                offsets = lists[l][:, h * HALF // 16 : (h + 1) * HALF // 16]
+                nc.vector.tensor_copy(pair[:], tab_w[:].bitcast(U32).indirect(offsets))
+                pairs.append(pair)
+            for l in range(LISTS):
                 nc.vector.tensor_copy(
-                    picked[l][h][:].bitcast(U16), both[l][:].bitcast(U16).rearrange("p (j a) -> p a j", a=PASSES)
+                    picked[l][h][:].bitcast(U16), pairs[l][:].bitcast(U16).rearrange("p (j a) -> p a j", a=PASSES)
                 )
 
         wa_q = keep.tile([P, PASSES, N], I32, name="wa_q", align_bytes=64)
@@ -130,16 +130,16 @@ def tile_list_rgg_reluP_kernel(
                 wc_raw[:].bitcast(U16).rearrange("p a (m t) -> p a t m", t=PACK),
             )
             nc.vector.tensor_copy(
-                wa_q[:].rearrange("p a (t m e) -> p a m t e", t=PACK, e=4),
-                wa_raw[:].rearrange("p a (m e t) -> p a m t e", t=PACK, e=4),
+                wa_q[:].rearrange("p a (t m e) -> p a m t e", t=PACK, e=LINE),
+                wa_raw[:].rearrange("p a (m e t) -> p a m t e", t=PACK, e=LINE),
             )
 
         def quantise_wb():
             for a in range(PASSES):
                 grouped = keep.tile([P, N * PACK], BF16, name="wb_grouped%d" % a, tag="stage%d" % a, align_bytes=64)
                 nc.scalar.copy(
-                    grouped[:].rearrange("p (t m i) -> p m i t", t=PACK, i=PACK),
-                    wb_raw[a][:].rearrange("p i (m t) -> p m i t", t=PACK),
+                    grouped[:].rearrange("p (t m i) -> p m t i", t=PACK, i=PACK),
+                    wb_raw[a][:].rearrange("p i (m t) -> p m t i", t=PACK),
                 )
                 nc.vector.quantize_mx(out=wb_q[a][:].bitcast(FP8X4), scales=wb_sc[a][:], in_=grouped[:])
 
@@ -148,16 +148,16 @@ def tile_list_rgg_reluP_kernel(
         deal_packed_weights()
         quantise_wb()
         gather_words(1)
-        window = keep.tile([P, T], F32, name="window3", tag="stage1", align_bytes=64)
-        nc.gpsimd.memset(window[:], 0.0)
-        windows.append(window)
+        last_window = keep.tile([P, T], F32, name="window3", tag="stage1", align_bytes=64)
+        nc.gpsimd.memset(last_window[:], 0.0)
+        windows.append(last_window)
 
         def moving(l, h, a):
-            return dict(rhs=picked[l][h][:, a, :].bitcast(FP4X4), rhs_scale=late_sc[:, a, l, h * HALF : (h + 1) * HALF])
+            return dict(rhs=picked[l][h][:, a, :].bitcast(FP4X4), rhs_scale=edge_sc[:, a, l, h * HALF : (h + 1) * HALF])
 
         def gate(t, h):
             m = slice(t * P, (t + 1) * P)
-            za = psum.tile([P, HALF], F32, name="za", bufs=4)
+            za = psum.tile([P, HALF], F32, name="za", bufs=BANKS)
             for a in range(PASSES):
                 nc.tensor.matmul_mx(
                     out=za[:], lhsT=wa_q[:, a, m].bitcast(FP8X4), lhsT_scale=wa_sc[:, a, m],
@@ -168,13 +168,12 @@ def tile_list_rgg_reluP_kernel(
                     out=za[:], lhsT=wb_q[a][:, m].bitcast(FP8X4), lhsT_scale=wb_sc[a][:, m],
                     start=False, stop=(a == PASSES - 1), **moving(0, h, a),
                 )
-            last = (t, h) == (SLICE_ORDER[-1], HALVES - 1)
-            eta = keep.tile([P, HALF], F32, name="eta", tag="gate2" if last else "eta%d_%d" % (t, h), align_bytes=64)
+            eta = keep.tile([P, HALF], F32, name="eta", tag="eta%d_%d" % (t, h), align_bytes=64)
             nc.scalar.activation(eta[:], za[:], SIGMOID)
             return eta
 
         def message(t, h):
-            ms = psum.tile([P, HALF], F32, name="ms", bufs=4)
+            ms = psum.tile([P, HALF], F32, name="ms", bufs=BANKS)
             for a in range(PASSES):
                 nc.tensor.matmul_mx(
                     out=ms[:],
@@ -186,21 +185,25 @@ def tile_list_rgg_reluP_kernel(
                 )
             return ms
 
-        steps = [(s, h) for s in range(PACK) for h in range(HALVES)]
-        values = [keep.tile([P, J], F32, name="values%d" % s) for s in range(PACK)]
-        for i, (s, h) in enumerate(steps):
+        steps = [(t, h) for h in range(HALVES) for t in range(2)] + [(t, h) for t in range(2, PACK) for h in range(HALVES)]
+        last_step = len(steps) - 1
+        values = [keep.tile([P, J], F32, name="values%d" % t) for t in range(PACK)]
+        for i, (t, h) in enumerate(steps):
             js = slice(h * HALF, (h + 1) * HALF)
-            eta = gate(SLICE_ORDER[s], h)
-            ms = message(SLICE_ORDER[s], h)
-            part = keep.tile([P, HALF], F32, name="part%d" % i)
+            eta = gate(t, h)
+            ms = message(t, h)
+            tag = {1: "eta0_0", last_step: "gate3"}.get(i, "weighted%d" % i)
+            weighted = keep.tile([P, HALF], F32, name="weighted", tag=tag, align_bytes=64)
             if i == 0:
-                nc.vector.scalar_tensor_tensor(part[:], ms[:], 0.0, eta[:], MAX, MULT)
-                nc.vector.tensor_tensor(values[s][:, js], part[:], edge_w[:, js], MULT)
+                nc.vector.tensor_tensor(weighted[:], eta[:], edge_w[:, js], MULT)
+                nc.vector.scalar_tensor_tensor(values[t][:, js], ms[:], 0.0, weighted[:], MAX, MULT)
             else:
-                kept = keep.tile([P, HALF], F32, name="kept", tag="gate3" if i == len(steps) - 1 else "kept%d" % i, align_bytes=64)
+                tag = "gate2" if i == last_step else "kept%d" % i
+                kept = keep.tile([P, HALF], F32, name="kept", tag=tag, align_bytes=64)
                 nc.scalar.activation(kept[:], ms[:], RELU)
-                nc.gpsimd.tensor_tensor(part[:], eta[:], edge_w[:, js], MULT)
-                nc.gpsimd.tensor_tensor(values[s][:, js], part[:], kept[:], MULT)
+                nc.gpsimd.tensor_tensor(weighted[:], eta[:], edge_w[:, js], MULT)
+                nc.gpsimd.tensor_tensor(values[t][:, js], weighted[:], kept[:], MULT)
+
         y_bf = [
             keep.tile([P, CHUNK, PACK], BF16, name="y_bf%d" % c, tag="gate%d" % c, align_bytes=64) for c in range(CHUNKS)
         ]
@@ -208,34 +211,35 @@ def tile_list_rgg_reluP_kernel(
         out_rows = out_0.rearrange("(p t) c -> t p c", t=PACK)
         out_words = out_1[0].rearrange("p c i -> p (c i)").bitcast(I32)
 
-        for s, t in enumerate(SLICE_ORDER):
-            window = windows[s % WINDOWS]
-            width = HALF if s < 2 else J
-            for j in range(0, J, width):
-                nc.vector.tensor_copy(
-                    window[:].indirect(dst_list[:, j // 16 : (j + width) // 16]), values[s][:, j : j + width]
-                )
+        pieces = [(t, h * HALF, HALF) for t, h in steps[:-HALVES]] + [(PACK - 1, 0, J)]
+        for t, j, width in pieces:
+            window = windows[t]
+            nc.vector.tensor_copy(window[:].indirect(dst_list[:, j // 16 : (j + width) // 16]), values[t][:, j : j + width])
+            if j + width < J:
+                continue
             nc.sync.dma_start(out_rows[t], window[:])
             for c in range(CHUNKS):
                 part = window[:, c * CHUNK : (c + 1) * CHUNK]
-                if s == PACK - 1 and c < CHUNKS // 2:
+                if t == PACK - 1 and c < SHARED:
                     nc.vector.tensor_copy(y_bf[c][:, :, t], part)
-                elif t < 2 and c >= CHUNKS // 2:
+                elif t < 2 and c >= SHARED:
                     nc.gpsimd.tensor_copy(y_bf[c][:, :, t], part)
-                elif t == 2 and c < CHUNKS // 2:
+                elif t == 2 and c < SHARED:
                     nc.scalar.copy(y_bf[c][:, :, 2:4], part.unsqueeze(2).to_broadcast([P, CHUNK, 2]))
                 else:
                     nc.scalar.copy(y_bf[c][:, :, t], part)
 
+        codes = keep.tile([P, T], I32, name="y_codes", align_bytes=64)
         for c in range(CHUNKS):
-            codes = keep.tile([P, CHUNK], I32, name="y_codes%d" % c, align_bytes=64)
             nc.vector.quantize_mx(
-                out=codes[:].bitcast(FP8X4),
+                out=codes[:, c * CHUNK : (c + 1) * CHUNK].bitcast(FP8X4),
                 scales=y_sc[:, c * CHUNK : (c + 1) * CHUNK],
                 in_=y_bf[c][:].rearrange("p c i -> p (c i)"),
             )
-            nc.sync.dma_start(out_words[:, c * CHUNK : (c + 1) * CHUNK], codes[:])
+            if c > 0:
+                first = 0 if c == 1 else c * CHUNK
+                nc.sync.dma_start(out_words[:, first : (c + 1) * CHUNK], codes[:, first : (c + 1) * CHUNK])
         for q in range(QUADS):
             (nc.scalar if q % 2 else nc.sync).dma_start(
-                out_2[0, ROWS * q : ROWS * (q + 1), :].bitcast(I32), y_sc[32 * q : 32 * q + ROWS, :].bitcast(I32)
+                out_2[0, ROWS * q : ROWS * (q + 1), :].bitcast(I32), y_sc[QUAD * q : QUAD * q + ROWS, :].bitcast(I32)
             )

@@ -28,6 +28,7 @@ QUAD = 32
 QUADS = P // QUAD
 ROWS = 4
 SPARE = QUAD - PASSES * ROWS
+MOVED = 112
 LINE = 4
 CHUNK = 512
 CHUNKS = T // CHUNK
@@ -42,6 +43,7 @@ def tile_list_rgg_reluP_kernel(
     with ExitStack() as ctx:
         held = ctx.enter_context(tc.tile_pool(name="held", bufs=1))
         keep = ctx.enter_context(tc.tile_pool(name="keep", bufs=1))
+        laid = ctx.enter_context(tc.tile_pool(name="laid", bufs=1))
         psum = ctx.enter_context(tc.psum_pool(name="psum", bufs=1))
 
         src_list = held.tile([P, J // 16], U16, name="src_list")
@@ -61,58 +63,67 @@ def tile_list_rgg_reluP_kernel(
             )
         tab_w = keep.tile([P, T], I32, name="tab_w", align_bytes=64)
 
+        nc.sync.dma_start(tab_w[:], tab_words[0].rearrange("p t i -> p (t i)").bitcast(I32))
         wb_raw = [keep.tile([P, PACK, N], F32, name="wb_raw%d" % a) for a in range(PASSES)]
         wb_rows = wb.rearrange("(a p i) n -> a p i n", p=P, i=PACK)
         nc.sync.dma_start(wb_raw[0][:], wb_rows[0])
-        nc.sync.dma_start(tab_w[:], tab_words[0].rearrange("p t i -> p (t i)").bitcast(I32))
-        for w, scales in enumerate((wa_scales, wc_scales)):
-            for q in range(QUADS):
-                first = QUAD * q + ROWS * w
-                nc.sync.dma_start(
-                    w_sc_raw[first : first + ROWS, :, :].bitcast(I32),
-                    scales[:, ROWS * q : ROWS * (q + 1), :].rearrange("a r n -> r a n").bitcast(I32),
-                )
-        nc.sync.dma_start(wb_raw[1][:], wb_rows[1])
-        wc_raw = keep.tile([P, PASSES, 2 * N], U8, name="wc_raw")
-        nc.sync.dma_start(wc_raw[:].bitcast(I32), wc_words.rearrange("a p b -> p a b").bitcast(I32))
-        wa_raw = keep.tile([P, PASSES, N], I32, name="wa_raw")
-        nc.sync.dma_start(wa_raw[:], wa_words.rearrange("a p n i -> p a (n i)").bitcast(I32))
-        edge_w = keep.tile([P, J], F32, name="edge_w")
-        nc.sync.dma_start(edge_w[:], wgo)
 
+        def load_weight_scales(w, q):
+            first = QUAD * q + ROWS * w
+            nc.sync.dma_start(
+                w_sc_raw[first : first + ROWS, :, :].bitcast(I32),
+                (wa_scales, wc_scales)[w][:, ROWS * q : ROWS * (q + 1), :].rearrange("a r n -> r a n").bitcast(I32),
+            )
+
+        scale_loads = [(w, q) for w in range(2) for q in range(QUADS)]
+        for w, q in scale_loads[:6]:
+            load_weight_scales(w, q)
+        nc.sync.dma_start(wb_raw[1][:], wb_rows[1])
+
+        edge_sc = keep.tile([P, HALVES, PASSES, LISTS, HALF], U8, name="edge_sc", align_bytes=64)
+        nc.gpsimd.memset(edge_sc[:].bitcast(I32), 0)
         wc_sc = keep.tile([P, PASSES, N], U8, name="wc_sc", tag="gate1", align_bytes=64)
         nc.gpsimd.memset(wc_sc[:].bitcast(I32), 0)
-        edge_sc = keep.tile([P, PASSES, LISTS, J], U8, name="edge_sc", align_bytes=64)
-        nc.gpsimd.memset(edge_sc[:].bitcast(I32), 0)
         windows = [keep.tile([P, T], F32, name="window%d" % t) for t in range(PACK - 1)]
         for window in windows:
             nc.gpsimd.memset(window[:], 0.0)
 
-        picked_sc = keep.tile([P, LISTS, J], U8, name="picked_sc", align_bytes=64)
-        picked = [
-            [keep.tile([P, PASSES, 2 * HALF], U8, name="picked%d_%d" % (l, h), align_bytes=64) for h in range(HALVES)]
-            for l in range(LISTS)
-        ]
+        picked = {}
 
-        def gather_scales():
-            for l in range(LISTS):
-                nc.vector.tensor_copy(picked_sc[:, l, :], tab_sc[:].indirect(lists[l][:]))
+        def offsets(l, h):
+            return lists[l][:, h * HALF // 16 : (h + 1) * HALF // 16]
+
+        def gather_scales(h, first, picked_sc):
+            count = picked_sc.shape[1]
+            for l in range(count):
+                nc.vector.tensor_copy(picked_sc[:, l, :], tab_sc[:].indirect(offsets(first + l, h)))
             for a in range(PASSES):
                 shift = SPARE + ROWS * a
-                nc.sync.dma_start(edge_sc[0 : P - shift, a, :, :].bitcast(I32), picked_sc[shift:P, :, :].bitcast(I32))
-
-        def gather_words(h):
-            pairs = []
-            for l in range(LISTS):
-                tag = "pair%d" % l if h == 0 else "stage%d" % l
-                pair = keep.tile([P, HALF], U32, name="pair%d_%d" % (l, h), tag=tag, align_bytes=64)
-                offsets = lists[l][:, h * HALF // 16 : (h + 1) * HALF // 16]
-                nc.vector.tensor_copy(pair[:], tab_w[:].bitcast(U32).indirect(offsets))
-                pairs.append(pair)
-            for l in range(LISTS):
-                nc.vector.tensor_copy(
-                    picked[l][h][:].bitcast(U16), pairs[l][:].bitcast(U16).rearrange("p (j a) -> p a j", a=PASSES)
+                nc.sync.dma_start(
+                    edge_sc[0 : P - shift, h, a, first : first + count, :].bitcast(I32), picked_sc[shift:P].bitcast(I32)
                 )
+
+        def part(l, h, tag):
+            picked[l, h] = keep.tile([P, PASSES, 2 * HALF], U8, name="picked", tag=tag, align_bytes=64)
+            nc.vector.tensor_copy(
+                picked[l, h][:].bitcast(U16), pairs[l, h][:].bitcast(U16).rearrange("p (j a) -> p a j", a=PASSES)
+            )
+
+        wa_raw = keep.tile([P, PASSES, N], I32, name="wa_raw", align_bytes=64)
+        nc.sync.dma_start(wa_raw[:], wa_words.rearrange("a p n i -> p a (n i)").bitcast(I32))
+        for w, q in scale_loads[6:]:
+            load_weight_scales(w, q)
+        wc_raw = keep.tile([P, PASSES, 2 * N], U8, name="wc_raw", align_bytes=64)
+        nc.sync.dma_start(wc_raw[:].bitcast(I32), wc_words.rearrange("a p b -> p a b").bitcast(I32))
+        gather_scales(0, 0, keep.tile([P, LISTS, HALF], U8, name="early_sc", align_bytes=64))
+        edge_w = keep.tile([P, J], F32, name="edge_w")
+        nc.sync.dma_start(edge_w[:], wgo)
+
+        pairs = {}
+        for h in range(HALVES):
+            for l in range(LISTS):
+                pairs[l, h] = laid.tile([P, HALF], U32, name="pair", offset=4 * HALF * (LISTS * h + l), align_bytes=64)
+                nc.vector.tensor_copy(pairs[l, h][:], tab_w[:].bitcast(U32).indirect(offsets(l, h)))
 
         wa_q = keep.tile([P, PASSES, N], I32, name="wa_q", align_bytes=64)
         wa_sc = keep.tile([P, PASSES, N], U8, name="wa_sc", align_bytes=64)
@@ -124,14 +135,14 @@ def tile_list_rgg_reluP_kernel(
             nc.vector.tensor_copy(
                 wa_sc[:].rearrange("p a (t m) -> p a t m", t=PACK), w_sc_raw[:].rearrange("p a (m t) -> p a t m", t=PACK)
             )
-            nc.sync.dma_start(wc_sc[0 : P - ROWS, :, :].bitcast(I32), wa_sc[ROWS:P, :, :].bitcast(I32))
-            nc.vector.tensor_copy(
-                wc_q[:].bitcast(U16).rearrange("p a (t m) -> p a t m", t=PACK),
-                wc_raw[:].bitcast(U16).rearrange("p a (m t) -> p a t m", t=PACK),
-            )
+            nc.sync.dma_start(wc_sc[0:MOVED].bitcast(I32), wa_sc[ROWS : ROWS + MOVED].bitcast(I32))
             nc.vector.tensor_copy(
                 wa_q[:].rearrange("p a (t m e) -> p a m t e", t=PACK, e=LINE),
                 wa_raw[:].rearrange("p a (m e t) -> p a m t e", t=PACK, e=LINE),
+            )
+            nc.vector.tensor_copy(
+                wc_q[:].bitcast(U16).rearrange("p a (t m) -> p a t m", t=PACK),
+                wc_raw[:].bitcast(U16).rearrange("p a (m t) -> p a t m", t=PACK),
             )
 
         def quantise_wb():
@@ -143,30 +154,31 @@ def tile_list_rgg_reluP_kernel(
                 )
                 nc.vector.quantize_mx(out=wb_q[a][:].bitcast(FP8X4), scales=wb_sc[a][:], in_=grouped[:])
 
-        gather_scales()
-        gather_words(0)
+        for l in range(LISTS):
+            part(l, 0, "picked%d" % l)
         deal_packed_weights()
         quantise_wb()
-        gather_words(1)
-        last_window = keep.tile([P, T], F32, name="window3", tag="stage1", align_bytes=64)
+        for l in range(LISTS):
+            part(l, 1, ("wa_raw", "wc_raw")[l])
+        for l in range(LISTS):
+            gather_scales(1, l, laid.tile([P, 1, HALF], U8, name="late_sc", offset=4 * HALF * (LISTS + l), align_bytes=64))
+        last_window = laid.tile([P, T], F32, name="window3", offset=4 * HALF * (LISTS + 1) + 2 * HALF, align_bytes=64)
         nc.gpsimd.memset(last_window[:], 0.0)
         windows.append(last_window)
 
         def moving(l, h, a):
-            return dict(rhs=picked[l][h][:, a, :].bitcast(FP4X4), rhs_scale=edge_sc[:, a, l, h * HALF : (h + 1) * HALF])
+            return dict(rhs=picked[l, h][:, a, :].bitcast(FP4X4), rhs_scale=edge_sc[:, h, a, l, :])
 
         def gate(t, h):
             m = slice(t * P, (t + 1) * P)
             za = psum.tile([P, HALF], F32, name="za", bufs=BANKS)
-            for a in range(PASSES):
+            terms = [(wa_q[:, a, m], wa_sc[:, a, m], 1, a) for a in range(PASSES)]
+            from_wb = [(wb_q[a][:, m], wb_sc[a][:, m], 0, a) for a in range(PASSES)]
+            terms = terms + from_wb if h == 0 else from_wb + terms
+            for i, (words, scales, l, a) in enumerate(terms):
                 nc.tensor.matmul_mx(
-                    out=za[:], lhsT=wa_q[:, a, m].bitcast(FP8X4), lhsT_scale=wa_sc[:, a, m],
-                    start=(a == 0), stop=False, **moving(1, h, a),
-                )
-            for a in range(PASSES):
-                nc.tensor.matmul_mx(
-                    out=za[:], lhsT=wb_q[a][:, m].bitcast(FP8X4), lhsT_scale=wb_sc[a][:, m],
-                    start=False, stop=(a == PASSES - 1), **moving(0, h, a),
+                    out=za[:], lhsT=words.bitcast(FP8X4), lhsT_scale=scales,
+                    start=(i == 0), stop=(i == len(terms) - 1), **moving(l, h, a),
                 )
             eta = keep.tile([P, HALF], F32, name="eta", tag="eta%d_%d" % (t, h), align_bytes=64)
             nc.scalar.activation(eta[:], za[:], SIGMOID)
@@ -190,19 +202,21 @@ def tile_list_rgg_reluP_kernel(
         values = [keep.tile([P, J], F32, name="values%d" % t) for t in range(PACK)]
         for i, (t, h) in enumerate(steps):
             js = slice(h * HALF, (h + 1) * HALF)
-            eta = gate(t, h)
-            ms = message(t, h)
             tag = {1: "eta0_0", last_step: "gate3"}.get(i, "weighted%d" % i)
             weighted = keep.tile([P, HALF], F32, name="weighted", tag=tag, align_bytes=64)
             if i == 0:
+                eta = gate(t, h)
+                ms = message(t, h)
                 nc.vector.tensor_tensor(weighted[:], eta[:], edge_w[:, js], MULT)
                 nc.vector.scalar_tensor_tensor(values[t][:, js], ms[:], 0.0, weighted[:], MAX, MULT)
             else:
+                ms = message(t, h)
                 tag = "gate2" if i == last_step else "kept%d" % i
                 kept = keep.tile([P, HALF], F32, name="kept", tag=tag, align_bytes=64)
                 nc.scalar.activation(kept[:], ms[:], RELU)
-                nc.gpsimd.tensor_tensor(weighted[:], eta[:], edge_w[:, js], MULT)
-                nc.gpsimd.tensor_tensor(values[t][:, js], weighted[:], kept[:], MULT)
+                eta = gate(t, h)
+                nc.gpsimd.tensor_tensor(weighted[:], kept[:], edge_w[:, js], MULT)
+                nc.gpsimd.tensor_tensor(values[t][:, js], weighted[:], eta[:], MULT)
 
         y_bf = [
             keep.tile([P, CHUNK, PACK], BF16, name="y_bf%d" % c, tag="gate%d" % c, align_bytes=64) for c in range(CHUNKS)

@@ -15,6 +15,7 @@ FP8X4 = mybir.dt.float8_e4m3fn_x4
 FP4X4 = mybir.dt.float4_e2m1fn_x4
 MULT = mybir.AluOpType.mult
 MAX = mybir.AluOpType.max
+ADD = mybir.AluOpType.add
 SIGMOID = mybir.ActivationFunctionType.Sigmoid
 RELU = mybir.ActivationFunctionType.Relu
 
@@ -44,16 +45,16 @@ def tile_list_rgg_reluP_kernel(
         held = ctx.enter_context(tc.tile_pool(name="held", bufs=1))
         keep = ctx.enter_context(tc.tile_pool(name="keep", bufs=1))
         laid = ctx.enter_context(tc.tile_pool(name="laid", bufs=1))
+        late = ctx.enter_context(tc.tile_pool(name="late", bufs=1))
         psum = ctx.enter_context(tc.psum_pool(name="psum", bufs=1))
 
         src_list = held.tile([P, J // 16], U16, name="src_list")
         dst_list = held.tile([P, J // 16], U16, name="dst_list")
         lists = (src_list, dst_list)
         nc.sync.dma_start(src_list[:], offs)
-        nc.sync.dma_start(dst_list[:], offs2)
 
         w_sc_raw = keep.tile([P, PASSES, N], U8, name="w_sc_raw")
-        nc.gpsimd.memset(w_sc_raw[:].bitcast(I32), 0)
+        nc.vector.memset(w_sc_raw[:].bitcast(I32), 0)
         tab_sc = keep.tile([P, T], U8, name="tab_sc", align_bytes=64)
         for q in range(QUADS):
             nc.gpsimd.memset(tab_sc[QUAD * q : QUAD * q + SPARE, :].bitcast(I32), 0)
@@ -61,6 +62,7 @@ def tile_list_rgg_reluP_kernel(
                 tab_sc[QUAD * q + SPARE : QUAD * (q + 1), :].bitcast(I32),
                 tab_scales[:, ROWS * q : ROWS * (q + 1), :].bitcast(I32),
             )
+        nc.sync.dma_start(dst_list[:], offs2)
         tab_w = keep.tile([P, T], I32, name="tab_w", align_bytes=64)
 
         nc.sync.dma_start(tab_w[:], tab_words[0].rearrange("p t i -> p (t i)").bitcast(I32))
@@ -83,7 +85,7 @@ def tile_list_rgg_reluP_kernel(
         edge_sc = keep.tile([P, HALVES, PASSES, LISTS, HALF], U8, name="edge_sc", align_bytes=64)
         nc.gpsimd.memset(edge_sc[:].bitcast(I32), 0)
         wc_sc = keep.tile([P, PASSES, N], U8, name="wc_sc", tag="gate1", align_bytes=64)
-        nc.gpsimd.memset(wc_sc[:].bitcast(I32), 0)
+        nc.vector.memset(wc_sc[:].bitcast(I32), 0)
         windows = [keep.tile([P, T], F32, name="window%d" % t) for t in range(PACK - 1)]
         for window in windows:
             nc.gpsimd.memset(window[:], 0.0)
@@ -103,27 +105,29 @@ def tile_list_rgg_reluP_kernel(
                     edge_sc[0 : P - shift, h, a, first : first + count, :].bitcast(I32), picked_sc[shift:P].bitcast(I32)
                 )
 
-        def part(l, h, tag):
-            picked[l, h] = keep.tile([P, PASSES, 2 * HALF], U8, name="picked", tag=tag, align_bytes=64)
+        def part(l, h, target):
+            picked[l, h] = target[:]
             nc.vector.tensor_copy(
-                picked[l, h][:].bitcast(U16), pairs[l, h][:].bitcast(U16).rearrange("p (j a) -> p a j", a=PASSES)
+                target[:].bitcast(U16), pairs[l, h][:].bitcast(U16).rearrange("p (j a) -> p a j", a=PASSES)
             )
 
         wa_raw = keep.tile([P, PASSES, N], I32, name="wa_raw", align_bytes=64)
         nc.sync.dma_start(wa_raw[:], wa_words.rearrange("a p n i -> p a (n i)").bitcast(I32))
         for w, q in scale_loads[6:]:
             load_weight_scales(w, q)
-        wc_raw = keep.tile([P, PASSES, 2 * N], U8, name="wc_raw", align_bytes=64)
+        wc_raw = late.tile([P, PASSES, 2 * N], U8, name="wc_raw", offset=0, align_bytes=64)
         nc.sync.dma_start(wc_raw[:].bitcast(I32), wc_words.rearrange("a p b -> p a b").bitcast(I32))
         gather_scales(0, 0, keep.tile([P, LISTS, HALF], U8, name="early_sc", align_bytes=64))
         edge_w = keep.tile([P, J], F32, name="edge_w")
         nc.sync.dma_start(edge_w[:], wgo)
 
         pairs = {}
-        for h in range(HALVES):
-            for l in range(LISTS):
-                pairs[l, h] = laid.tile([P, HALF], U32, name="pair", offset=4 * HALF * (LISTS * h + l), align_bytes=64)
-                nc.vector.tensor_copy(pairs[l, h][:], tab_w[:].bitcast(U32).indirect(offsets(l, h)))
+        early_pairs = keep.tile([P, LISTS, HALF], U32, name="early_pairs", align_bytes=64)
+        for l in range(LISTS):
+            nc.vector.tensor_copy(early_pairs[:, l, :], tab_w[:].bitcast(U32).indirect(offsets(l, 0)))
+        for l in range(LISTS):
+            pairs[l, 1] = laid.tile([P, HALF], U32, name="pair", offset=4 * HALF * (LISTS + l), align_bytes=64)
+            nc.vector.tensor_copy(pairs[l, 1][:], tab_w[:].bitcast(U32).indirect(offsets(l, 1)))
 
         wa_q = keep.tile([P, PASSES, N], I32, name="wa_q", align_bytes=64)
         wa_sc = keep.tile([P, PASSES, N], U8, name="wa_sc", align_bytes=64)
@@ -147,22 +151,27 @@ def tile_list_rgg_reluP_kernel(
 
         def quantise_wb():
             for a in range(PASSES):
-                grouped = keep.tile([P, N * PACK], BF16, name="wb_grouped%d" % a, tag="stage%d" % a, align_bytes=64)
+                grouped = late.tile([P, N * PACK], BF16, name="wb_grouped%d" % a, offset=(12 * HALF, 4 * HALF)[a], align_bytes=64)
                 nc.scalar.copy(
                     grouped[:].rearrange("p (t m i) -> p m t i", t=PACK, i=PACK),
                     wb_raw[a][:].rearrange("p i (m t) -> p m t i", t=PACK),
                 )
                 nc.vector.quantize_mx(out=wb_q[a][:].bitcast(FP8X4), scales=wb_sc[a][:], in_=grouped[:])
 
+        early_picked = keep.tile([P, LISTS, PASSES, 2 * HALF], U8, name="early_picked", align_bytes=64)
+        nc.vector.tensor_copy(
+            early_picked[:].bitcast(U16), early_pairs[:].bitcast(U16).rearrange("p l (j a) -> p l a j", a=PASSES)
+        )
         for l in range(LISTS):
-            part(l, 0, "picked%d" % l)
+            picked[l, 0] = early_picked[:, l]
         deal_packed_weights()
         quantise_wb()
-        for l in range(LISTS):
-            part(l, 1, ("wa_raw", "wc_raw")[l])
+        part(0, 1, keep.tile([P, PASSES, 2 * HALF], U8, name="picked2", tag="wa_raw", align_bytes=64))
+        part(1, 1, late.tile([P, PASSES, 2 * HALF], U8, name="picked3", offset=2 * HALF, align_bytes=64))
+        last_pair = 4 * HALF * (LISTS + 1)
         for l in range(LISTS):
             gather_scales(1, l, laid.tile([P, 1, HALF], U8, name="late_sc", offset=4 * HALF * (LISTS + l), align_bytes=64))
-        last_window = laid.tile([P, T], F32, name="window3", offset=4 * HALF * (LISTS + 1) + 2 * HALF, align_bytes=64)
+        last_window = laid.tile([P, T], F32, name="window3", offset=last_pair + 3 * HALF, align_bytes=64)
         nc.gpsimd.memset(last_window[:], 0.0)
         windows.append(last_window)
 
@@ -237,7 +246,11 @@ def tile_list_rgg_reluP_kernel(
                 if t == PACK - 1 and c < SHARED:
                     nc.vector.tensor_copy(y_bf[c][:, :, t], part)
                 elif t < 2 and c >= SHARED:
-                    nc.gpsimd.tensor_copy(y_bf[c][:, :, t], part)
+                    nc.gpsimd.tensor_scalar(y_bf[c][:, :, t], part, 1.0, -0.0, MULT, ADD)
+                elif t == 2 and c == CHUNKS - 1:
+                    nc.gpsimd.tensor_scalar(
+                        y_bf[c][:, :, 2:4], part.unsqueeze(2).to_broadcast([P, CHUNK, 2]), 1.0, -0.0, MULT, ADD
+                    )
                 elif t == 2 and c < SHARED:
                     nc.scalar.copy(y_bf[c][:, :, 2:4], part.unsqueeze(2).to_broadcast([P, CHUNK, 2]))
                 else:

@@ -14,7 +14,6 @@ U8 = mybir.dt.uint8
 FP8X4 = mybir.dt.float8_e4m3fn_x4
 FP4X4 = mybir.dt.float4_e2m1fn_x4
 MULT = mybir.AluOpType.mult
-MAX = mybir.AluOpType.max
 ADD = mybir.AluOpType.add
 SIGMOID = mybir.ActivationFunctionType.Sigmoid
 RELU = mybir.ActivationFunctionType.Relu
@@ -28,13 +27,14 @@ HALVES = J // HALF
 QUAD = 32
 QUADS = P // QUAD
 ROWS = 4
-SPARE = QUAD - PASSES * ROWS
-MOVED = 112
+SIDE = P // 2
+TAB_FIRST = 48
+WC_ROWS = (4, 36, 60, 92)
 LINE = 4
 CHUNK = 512
 CHUNKS = T // CHUNK
-SHARED = CHUNKS // 2
-BANKS = 4
+BANKS = 3
+KB = 1024
 
 
 def tile_list_rgg_reluP_kernel(
@@ -45,7 +45,6 @@ def tile_list_rgg_reluP_kernel(
         held = ctx.enter_context(tc.tile_pool(name="held", bufs=1))
         keep = ctx.enter_context(tc.tile_pool(name="keep", bufs=1))
         laid = ctx.enter_context(tc.tile_pool(name="laid", bufs=1))
-        late = ctx.enter_context(tc.tile_pool(name="late", bufs=1))
         psum = ctx.enter_context(tc.psum_pool(name="psum", bufs=1))
 
         src_list = held.tile([P, J // 16], U16, name="src_list")
@@ -54,147 +53,132 @@ def tile_list_rgg_reluP_kernel(
         nc.sync.dma_start(src_list[:], offs)
 
         w_sc_raw = keep.tile([P, PASSES, N], U8, name="w_sc_raw")
-        nc.vector.memset(w_sc_raw[:].bitcast(I32), 0)
+        nc.gpsimd.memset(w_sc_raw[:].bitcast(I32), 0)
         tab_sc = keep.tile([P, T], U8, name="tab_sc", align_bytes=64)
-        for q in range(QUADS):
-            nc.gpsimd.memset(tab_sc[QUAD * q : QUAD * q + SPARE, :].bitcast(I32), 0)
-            nc.sync.dma_start(
-                tab_sc[QUAD * q + SPARE : QUAD * (q + 1), :].bitcast(I32),
-                tab_scales[:, ROWS * q : ROWS * (q + 1), :].bitcast(I32),
-            )
+        for first, last in ((0, TAB_FIRST), (SIDE, TAB_FIRST + QUAD), (3 * QUAD, P)):
+            nc.gpsimd.memset(tab_sc[first:last, :].bitcast(I32), 0)
+        sc_rows = tab_scales.rearrange("a (h e r) t -> e (a h) r t", e=2, r=ROWS)
+        for e in range(2):
+            first = TAB_FIRST + QUAD * e
+            nc.sync.dma_start(tab_sc[first : first + 16, :].bitcast(I32), sc_rows[e].bitcast(I32))
         nc.sync.dma_start(dst_list[:], offs2)
         tab_w = keep.tile([P, T], I32, name="tab_w", align_bytes=64)
-
         nc.sync.dma_start(tab_w[:], tab_words[0].rearrange("p t i -> p (t i)").bitcast(I32))
-        wb_raw = [keep.tile([P, PACK, N], F32, name="wb_raw%d" % a) for a in range(PASSES)]
-        wb_rows = wb.rearrange("(a p i) n -> a p i n", p=P, i=PACK)
-        nc.sync.dma_start(wb_raw[0][:], wb_rows[0])
 
         def load_weight_scales(w, q):
-            first = QUAD * q + ROWS * w
+            first = (QUAD * q, WC_ROWS[q])[w]
             nc.sync.dma_start(
                 w_sc_raw[first : first + ROWS, :, :].bitcast(I32),
                 (wa_scales, wc_scales)[w][:, ROWS * q : ROWS * (q + 1), :].rearrange("a r n -> r a n").bitcast(I32),
             )
 
         scale_loads = [(w, q) for w in range(2) for q in range(QUADS)]
-        for w, q in scale_loads[:6]:
+        wb_raw = [keep.tile([P, PACK, N], F32, name="wb_raw%d" % a) for a in range(PASSES)]
+        wb_rows = wb.rearrange("(a p i) n -> a p i n", p=P, i=PACK)
+        for w, q in scale_loads[:3]:
+            load_weight_scales(w, q)
+        nc.sync.dma_start(wb_raw[0][:], wb_rows[0])
+        for w, q in scale_loads[3:]:
             load_weight_scales(w, q)
         nc.sync.dma_start(wb_raw[1][:], wb_rows[1])
+        wa_raw = keep.tile([P, PASSES, N], I32, name="wa_raw", align_bytes=64)
+        nc.sync.dma_start(wa_raw[:], wa_words.rearrange("a p n i -> p a (n i)").bitcast(I32))
+        wc_raw = laid.tile([P, PASSES, 2 * N], U8, name="wc_raw", offset=4 * KB, align_bytes=64)
+        nc.sync.dma_start(wc_raw[:].bitcast(I32), wc_words.rearrange("a p b -> p a b").bitcast(I32))
 
-        edge_sc = keep.tile([P, HALVES, PASSES, LISTS, HALF], U8, name="edge_sc", align_bytes=64)
-        nc.gpsimd.memset(edge_sc[:].bitcast(I32), 0)
-        wc_sc = keep.tile([P, PASSES, N], U8, name="wc_sc", tag="gate1", align_bytes=64)
-        nc.vector.memset(wc_sc[:].bitcast(I32), 0)
-        windows = [keep.tile([P, T], F32, name="window%d" % t) for t in range(PACK - 1)]
-        for window in windows:
+        windows = [keep.tile([P, T], F32, name="window%d" % t) for t in range(PACK)]
+        nc.vector.memset(windows[0][:, : T // 2 + 1], 0.0)
+        nc.vector.memset(windows[0][:, T // 2 + 1 :], 0.0)
+        for window in windows[1:]:
             nc.gpsimd.memset(window[:], 0.0)
-
-        picked = {}
 
         def offsets(l, h):
             return lists[l][:, h * HALF // 16 : (h + 1) * HALF // 16]
 
-        def gather_scales(h, first, picked_sc):
-            count = picked_sc.shape[1]
-            for l in range(count):
-                nc.vector.tensor_copy(picked_sc[:, l, :], tab_sc[:].indirect(offsets(first + l, h)))
+        edge_sc = [keep.tile([P, PASSES, LISTS, HALF], U8, name="edge_sc%d" % h, align_bytes=64) for h in range(HALVES)]
+
+        def gather_scales(h, picked_sc):
+            for l in range(LISTS):
+                nc.vector.tensor_copy(picked_sc[:, l, :], tab_sc[:].indirect(offsets(l, h)))
             for a in range(PASSES):
-                shift = SPARE + ROWS * a
-                nc.sync.dma_start(
-                    edge_sc[0 : P - shift, h, a, first : first + count, :].bitcast(I32), picked_sc[shift:P].bitcast(I32)
-                )
+                for s in range(2):
+                    first = TAB_FIRST + ROWS * (2 * a + s)
+                    nc.sync.dma_start(
+                        edge_sc[h][SIDE * s : SIDE * (s + 1), a].bitcast(I32), picked_sc[first : first + SIDE].bitcast(I32)
+                    )
 
-        def part(l, h, target):
-            picked[l, h] = target[:]
-            nc.vector.tensor_copy(
-                target[:].bitcast(U16), pairs[l, h][:].bitcast(U16).rearrange("p (j a) -> p a j", a=PASSES)
-            )
-
-        wa_raw = keep.tile([P, PASSES, N], I32, name="wa_raw", align_bytes=64)
-        nc.sync.dma_start(wa_raw[:], wa_words.rearrange("a p n i -> p a (n i)").bitcast(I32))
-        for w, q in scale_loads[6:]:
-            load_weight_scales(w, q)
-        wc_raw = late.tile([P, PASSES, 2 * N], U8, name="wc_raw", offset=0, align_bytes=64)
-        nc.sync.dma_start(wc_raw[:].bitcast(I32), wc_words.rearrange("a p b -> p a b").bitcast(I32))
-        gather_scales(0, 0, keep.tile([P, LISTS, HALF], U8, name="early_sc", align_bytes=64))
+        gather_scales(0, keep.tile([P, LISTS, HALF], U8, name="early_sc", align_bytes=64))
         edge_w = keep.tile([P, J], F32, name="edge_w")
         nc.sync.dma_start(edge_w[:], wgo)
 
-        pairs = {}
-        early_pairs = keep.tile([P, LISTS, HALF], U32, name="early_pairs", align_bytes=64)
+        pairs = laid.tile([P, LISTS, J], U32, name="pairs", offset=20 * KB, align_bytes=64)
         for l in range(LISTS):
-            nc.vector.tensor_copy(early_pairs[:, l, :], tab_w[:].bitcast(U32).indirect(offsets(l, 0)))
-        for l in range(LISTS):
-            pairs[l, 1] = laid.tile([P, HALF], U32, name="pair", offset=4 * HALF * (LISTS + l), align_bytes=64)
-            nc.vector.tensor_copy(pairs[l, 1][:], tab_w[:].bitcast(U32).indirect(offsets(l, 1)))
+            nc.vector.tensor_copy(pairs[:, l, :], tab_w[:].bitcast(U32).indirect(lists[l][:]))
 
-        wa_q = keep.tile([P, PASSES, N], I32, name="wa_q", align_bytes=64)
+        def part(h, target):
+            nc.vector.tensor_copy(
+                target[:].bitcast(U16),
+                pairs[:, :, h * HALF : (h + 1) * HALF].bitcast(U16).rearrange("p l (j a) -> p l a j", a=PASSES),
+            )
+            return target
+
+        picked = [part(0, keep.tile([P, LISTS, PASSES, 2 * HALF], U8, name="picked0", align_bytes=64))]
+
         wa_sc = keep.tile([P, PASSES, N], U8, name="wa_sc", align_bytes=64)
-        wc_q = keep.tile([P, PASSES, 2 * N], U8, name="wc_q", tag="gate0", align_bytes=64)
+        wc_sc = keep.tile([P, PASSES, N], U8, name="wc_sc", align_bytes=64)
+        nc.vector.tensor_copy(
+            wa_sc[:].rearrange("p a (t m) -> p a t m", t=PACK), w_sc_raw[:].rearrange("p a (m t) -> p a t m", t=PACK)
+        )
+        for s in range(2):
+            first = WC_ROWS[2 * s]
+            nc.sync.dma_start(wc_sc[SIDE * s : SIDE * (s + 1)].bitcast(I32), wa_sc[first : first + SIDE].bitcast(I32))
+
         wb_q = [keep.tile([P, N], U32, name="wb_q%d" % a, align_bytes=64) for a in range(PASSES)]
         wb_sc = [keep.tile([P, N], U8, name="wb_sc%d" % a, align_bytes=64) for a in range(PASSES)]
 
-        def deal_packed_weights():
-            nc.vector.tensor_copy(
-                wa_sc[:].rearrange("p a (t m) -> p a t m", t=PACK), w_sc_raw[:].rearrange("p a (m t) -> p a t m", t=PACK)
+        def quantise_wb(a):
+            grouped = laid.tile([P, N * PACK], BF16, name="wb_grouped%d" % a, offset=(28 * KB, 0)[a], align_bytes=64)
+            nc.scalar.copy(
+                grouped[:].rearrange("p (t m i) -> p m t i", t=PACK, i=PACK),
+                wb_raw[a][:].rearrange("p i (m t) -> p m t i", t=PACK),
             )
-            nc.sync.dma_start(wc_sc[0:MOVED].bitcast(I32), wa_sc[ROWS : ROWS + MOVED].bitcast(I32))
-            nc.vector.tensor_copy(
-                wa_q[:].rearrange("p a (t m e) -> p a m t e", t=PACK, e=LINE),
-                wa_raw[:].rearrange("p a (m e t) -> p a m t e", t=PACK, e=LINE),
-            )
-            nc.vector.tensor_copy(
-                wc_q[:].bitcast(U16).rearrange("p a (t m) -> p a t m", t=PACK),
-                wc_raw[:].bitcast(U16).rearrange("p a (m t) -> p a t m", t=PACK),
-            )
+            nc.vector.quantize_mx(out=wb_q[a][:].bitcast(FP8X4), scales=wb_sc[a][:], in_=grouped[:])
 
-        def quantise_wb():
-            for a in range(PASSES):
-                grouped = late.tile([P, N * PACK], BF16, name="wb_grouped%d" % a, offset=(12 * HALF, 4 * HALF)[a], align_bytes=64)
-                nc.scalar.copy(
-                    grouped[:].rearrange("p (t m i) -> p m t i", t=PACK, i=PACK),
-                    wb_raw[a][:].rearrange("p i (m t) -> p m t i", t=PACK),
-                )
-                nc.vector.quantize_mx(out=wb_q[a][:].bitcast(FP8X4), scales=wb_sc[a][:], in_=grouped[:])
-
-        early_picked = keep.tile([P, LISTS, PASSES, 2 * HALF], U8, name="early_picked", align_bytes=64)
+        quantise_wb(0)
+        wa_q = laid.tile([P, PASSES, N], I32, name="wa_q", offset=8 * KB, align_bytes=64)
         nc.vector.tensor_copy(
-            early_picked[:].bitcast(U16), early_pairs[:].bitcast(U16).rearrange("p l (j a) -> p l a j", a=PASSES)
+            wa_q[:].rearrange("p a (t m e) -> p a m t e", t=PACK, e=LINE),
+            wa_raw[:].rearrange("p a (m e t) -> p a m t e", t=PACK, e=LINE),
         )
-        for l in range(LISTS):
-            picked[l, 0] = early_picked[:, l]
-        deal_packed_weights()
-        quantise_wb()
-        part(0, 1, keep.tile([P, PASSES, 2 * HALF], U8, name="picked2", tag="wa_raw", align_bytes=64))
-        part(1, 1, late.tile([P, PASSES, 2 * HALF], U8, name="picked3", offset=2 * HALF, align_bytes=64))
-        last_pair = 4 * HALF * (LISTS + 1)
-        for l in range(LISTS):
-            gather_scales(1, l, laid.tile([P, 1, HALF], U8, name="late_sc", offset=4 * HALF * (LISTS + l), align_bytes=64))
-        last_window = laid.tile([P, T], F32, name="window3", offset=last_pair + 3 * HALF, align_bytes=64)
-        nc.gpsimd.memset(last_window[:], 0.0)
-        windows.append(last_window)
+        quantise_wb(1)
+        wc_q = laid.tile([P, PASSES, 2 * N], U8, name="wc_q", offset=0, align_bytes=64)
+        nc.vector.tensor_copy(
+            wc_q[:].bitcast(U16).rearrange("p a (t m) -> p a t m", t=PACK),
+            wc_raw[:].bitcast(U16).rearrange("p a (m t) -> p a t m", t=PACK),
+        )
+        picked.append(part(1, laid.tile([P, LISTS, PASSES, 2 * HALF], U8, name="picked1", offset=4 * KB, align_bytes=64)))
+        gather_scales(1, laid.tile([P, LISTS, HALF], U8, name="late_sc", offset=20 * KB, align_bytes=64))
 
         def moving(l, h, a):
-            return dict(rhs=picked[l, h][:, a, :].bitcast(FP4X4), rhs_scale=edge_sc[:, h, a, l, :])
+            return dict(rhs=picked[h][:, l, a, :].bitcast(FP4X4), rhs_scale=edge_sc[h][:, a, l, :])
 
         def gate(t, h):
             m = slice(t * P, (t + 1) * P)
-            za = psum.tile([P, HALF], F32, name="za", bufs=BANKS)
-            terms = [(wa_q[:, a, m], wa_sc[:, a, m], 1, a) for a in range(PASSES)]
+            za = psum.tile([P, HALF], F32, name="za%d_%d" % (t, h), offset=2 * KB * ((PACK * h + t) % BANKS))
+            from_wa = [(wa_q[:, a, m], wa_sc[:, a, m], 1, a) for a in range(PASSES)]
             from_wb = [(wb_q[a][:, m], wb_sc[a][:, m], 0, a) for a in range(PASSES)]
-            terms = terms + from_wb if h == 0 else from_wb + terms
+            terms = from_wb[:1] + from_wa + from_wb[1:] if h == 0 else from_wb + from_wa
             for i, (words, scales, l, a) in enumerate(terms):
                 nc.tensor.matmul_mx(
                     out=za[:], lhsT=words.bitcast(FP8X4), lhsT_scale=scales,
                     start=(i == 0), stop=(i == len(terms) - 1), **moving(l, h, a),
                 )
-            eta = keep.tile([P, HALF], F32, name="eta", tag="eta%d_%d" % (t, h), align_bytes=64)
+            eta = keep.tile([P, HALF], F32, name="eta%d_%d" % (t, h), align_bytes=64)
             nc.scalar.activation(eta[:], za[:], SIGMOID)
             return eta
 
         def message(t, h):
-            ms = psum.tile([P, HALF], F32, name="ms", bufs=BANKS)
+            ms = psum.tile([P, HALF], F32, name="ms%d_%d" % (t, h), offset=2 * KB * ((PACK * h + t + 1) % BANKS))
             for a in range(PASSES):
                 nc.tensor.matmul_mx(
                     out=ms[:],
@@ -204,32 +188,27 @@ def tile_list_rgg_reluP_kernel(
                     stop=(a == PASSES - 1),
                     **moving(0, h, a),
                 )
-            return ms
+            kept = keep.tile([P, HALF], F32, name="kept%d_%d" % (t, h), align_bytes=64)
+            nc.scalar.activation(kept[:], ms[:], RELU)
+            return kept
 
         steps = [(t, h) for h in range(HALVES) for t in range(2)] + [(t, h) for t in range(2, PACK) for h in range(HALVES)]
-        last_step = len(steps) - 1
         values = [keep.tile([P, J], F32, name="values%d" % t) for t in range(PACK)]
+        factors = {}
+        for h in range(HALVES):
+            for t in range(PACK):
+                if (t, h) == (0, 0):
+                    factors[t, h] = (gate(t, h), message(t, h))
+                else:
+                    factors[t, h] = (message(t, h), gate(t, h))
         for i, (t, h) in enumerate(steps):
             js = slice(h * HALF, (h + 1) * HALF)
-            tag = {1: "eta0_0", last_step: "gate3"}.get(i, "weighted%d" % i)
-            weighted = keep.tile([P, HALF], F32, name="weighted", tag=tag, align_bytes=64)
-            if i == 0:
-                eta = gate(t, h)
-                ms = message(t, h)
-                nc.vector.tensor_tensor(weighted[:], eta[:], edge_w[:, js], MULT)
-                nc.vector.scalar_tensor_tensor(values[t][:, js], ms[:], 0.0, weighted[:], MAX, MULT)
-            else:
-                ms = message(t, h)
-                tag = "gate2" if i == last_step else "kept%d" % i
-                kept = keep.tile([P, HALF], F32, name="kept", tag=tag, align_bytes=64)
-                nc.scalar.activation(kept[:], ms[:], RELU)
-                eta = gate(t, h)
-                nc.gpsimd.tensor_tensor(weighted[:], kept[:], edge_w[:, js], MULT)
-                nc.gpsimd.tensor_tensor(values[t][:, js], weighted[:], eta[:], MULT)
+            weighted = laid.tile([P, HALF], F32, name="weighted%d" % i, offset=(12 + 2 * (i % 2)) * KB, align_bytes=64)
+            first, second = factors[t, h]
+            nc.gpsimd.tensor_tensor(weighted[:], first[:], edge_w[:, js], MULT)
+            nc.gpsimd.tensor_tensor(values[t][:, js], weighted[:], second[:], MULT)
 
-        y_bf = [
-            keep.tile([P, CHUNK, PACK], BF16, name="y_bf%d" % c, tag="gate%d" % c, align_bytes=64) for c in range(CHUNKS)
-        ]
+        y_bf = [laid.tile([P, CHUNK, PACK], BF16, name="y_bf%d" % c, offset=4 * KB * c, align_bytes=64) for c in range(CHUNKS)]
         y_sc = keep.tile([P, T], U8, name="y_sc", align_bytes=64)
         out_rows = out_0.rearrange("(p t) c -> t p c", t=PACK)
         out_words = out_1[0].rearrange("p c i -> p (c i)").bitcast(I32)
@@ -242,19 +221,18 @@ def tile_list_rgg_reluP_kernel(
                 continue
             nc.sync.dma_start(out_rows[t], window[:])
             for c in range(CHUNKS):
-                part = window[:, c * CHUNK : (c + 1) * CHUNK]
-                if t == PACK - 1 and c < SHARED:
-                    nc.vector.tensor_copy(y_bf[c][:, :, t], part)
-                elif t < 2 and c >= SHARED:
-                    nc.gpsimd.tensor_scalar(y_bf[c][:, :, t], part, 1.0, -0.0, MULT, ADD)
+                piece = window[:, c * CHUNK : (c + 1) * CHUNK]
+                both = piece.unsqueeze(2).to_broadcast([P, CHUNK, 2])
+                if t == PACK - 1 and c < 2:
+                    nc.vector.tensor_copy(y_bf[c][:, :, t], piece)
+                elif t < 2 and c == CHUNKS - 1:
+                    nc.gpsimd.tensor_scalar(y_bf[c][:, :, t], piece, 1.0, -0.0, MULT, ADD)
                 elif t == 2 and c == CHUNKS - 1:
-                    nc.gpsimd.tensor_scalar(
-                        y_bf[c][:, :, 2:4], part.unsqueeze(2).to_broadcast([P, CHUNK, 2]), 1.0, -0.0, MULT, ADD
-                    )
-                elif t == 2 and c < SHARED:
-                    nc.scalar.copy(y_bf[c][:, :, 2:4], part.unsqueeze(2).to_broadcast([P, CHUNK, 2]))
+                    nc.gpsimd.tensor_scalar(y_bf[c][:, :, 2:4], both, 1.0, -0.0, MULT, ADD)
+                elif t == 2 and c < 2:
+                    nc.scalar.copy(y_bf[c][:, :, 2:4], both)
                 else:
-                    nc.scalar.copy(y_bf[c][:, :, t], part)
+                    nc.scalar.copy(y_bf[c][:, :, t], piece)
 
         codes = keep.tile([P, T], I32, name="y_codes", align_bytes=64)
         for c in range(CHUNKS):

@@ -15,6 +15,7 @@ FP8X4 = mybir.dt.float8_e4m3fn_x4
 FP4X4 = mybir.dt.float4_e2m1fn_x4
 MULT = mybir.AluOpType.mult
 ADD = mybir.AluOpType.add
+MAX = mybir.AluOpType.max
 SIGMOID = mybir.ActivationFunctionType.Sigmoid
 RELU = mybir.ActivationFunctionType.Relu
 
@@ -52,7 +53,7 @@ def tile_list_rgg_reluP_kernel(
         lists = (src_list, dst_list)
         nc.sync.dma_start(src_list[:], offs)
 
-        w_sc_raw = keep.tile([P, PASSES, N], U8, name="w_sc_raw")
+        w_sc_raw = laid.tile([P, PASSES, N], U8, name="w_sc_raw", offset=12 * KB, align_bytes=64)
         nc.gpsimd.memset(w_sc_raw[:].bitcast(I32), 0)
         tab_sc = keep.tile([P, T], U8, name="tab_sc", align_bytes=64)
         for first, last in ((0, TAB_FIRST), (SIDE, TAB_FIRST + QUAD), (3 * QUAD, P)):
@@ -122,9 +123,8 @@ def tile_list_rgg_reluP_kernel(
             )
             return target
 
-        picked = [part(0, keep.tile([P, LISTS, PASSES, 2 * HALF], U8, name="picked0", align_bytes=64))]
 
-        wa_sc = keep.tile([P, PASSES, N], U8, name="wa_sc", align_bytes=64)
+        wa_sc = laid.tile([P, PASSES, N], U8, name="wa_sc", offset=0, align_bytes=64)
         wc_sc = keep.tile([P, PASSES, N], U8, name="wc_sc", align_bytes=64)
         nc.vector.tensor_copy(
             wa_sc[:].rearrange("p a (t m) -> p a t m", t=PACK), w_sc_raw[:].rearrange("p a (m t) -> p a t m", t=PACK)
@@ -133,11 +133,12 @@ def tile_list_rgg_reluP_kernel(
             first = WC_ROWS[2 * s]
             nc.sync.dma_start(wc_sc[SIDE * s : SIDE * (s + 1)].bitcast(I32), wa_sc[first : first + SIDE].bitcast(I32))
 
+        picked = [part(0, laid.tile([P, LISTS, PASSES, 2 * HALF], U8, name="picked0", offset=12 * KB, align_bytes=64))]
         wb_q = [keep.tile([P, N], U32, name="wb_q%d" % a, align_bytes=64) for a in range(PASSES)]
         wb_sc = [keep.tile([P, N], U8, name="wb_sc%d" % a, align_bytes=64) for a in range(PASSES)]
 
         def quantise_wb(a):
-            grouped = laid.tile([P, N * PACK], BF16, name="wb_grouped%d" % a, offset=(28 * KB, 0)[a], align_bytes=64)
+            grouped = laid.tile([P, N * PACK], BF16, name="wb_grouped%d" % a, offset=(32, 36)[a] * KB, align_bytes=64)
             nc.scalar.copy(
                 grouped[:].rearrange("p (t m i) -> p m t i", t=PACK, i=PACK),
                 wb_raw[a][:].rearrange("p i (m t) -> p m t i", t=PACK),
@@ -151,7 +152,7 @@ def tile_list_rgg_reluP_kernel(
             wa_raw[:].rearrange("p a (m e t) -> p a m t e", t=PACK, e=LINE),
         )
         quantise_wb(1)
-        wc_q = laid.tile([P, PASSES, 2 * N], U8, name="wc_q", offset=0, align_bytes=64)
+        wc_q = laid.tile([P, PASSES, 2 * N], U8, name="wc_q", offset=36 * KB, align_bytes=64)
         nc.vector.tensor_copy(
             wc_q[:].bitcast(U16).rearrange("p a (t m) -> p a t m", t=PACK),
             wc_raw[:].bitcast(U16).rearrange("p a (m t) -> p a t m", t=PACK),
@@ -162,9 +163,19 @@ def tile_list_rgg_reluP_kernel(
         def moving(l, h, a):
             return dict(rhs=picked[h][:, l, a, :].bitcast(FP4X4), rhs_scale=edge_sc[h][:, a, l, :])
 
+        sums = [(t, h) for h in range(HALVES) for t in range(PACK)]
+        eta = [keep.tile([P, J], F32, name="eta%d" % t) for t in range(PACK)]
+        kept = [keep.tile([P, J], F32, name="kept%d" % t) for t in range(PACK)]
+
+        def bank(t, h, is_gate):
+            k = sums.index((t, h))
+            if k == 0:
+                return 0 if is_gate else 2 * KB * BANKS
+            return 2 * KB * ((k - is_gate) % BANKS)
+
         def gate(t, h):
             m = slice(t * P, (t + 1) * P)
-            za = psum.tile([P, HALF], F32, name="za%d_%d" % (t, h), offset=2 * KB * ((PACK * h + t) % BANKS))
+            za = psum.tile([P, HALF], F32, name="za%d_%d" % (t, h), offset=bank(t, h, 1))
             from_wa = [(wa_q[:, a, m], wa_sc[:, a, m], 1, a) for a in range(PASSES)]
             from_wb = [(wb_q[a][:, m], wb_sc[a][:, m], 0, a) for a in range(PASSES)]
             terms = from_wb[:1] + from_wa + from_wb[1:] if h == 0 else from_wb + from_wa
@@ -173,12 +184,10 @@ def tile_list_rgg_reluP_kernel(
                     out=za[:], lhsT=words.bitcast(FP8X4), lhsT_scale=scales,
                     start=(i == 0), stop=(i == len(terms) - 1), **moving(l, h, a),
                 )
-            eta = keep.tile([P, HALF], F32, name="eta%d_%d" % (t, h), align_bytes=64)
-            nc.scalar.activation(eta[:], za[:], SIGMOID)
-            return eta
+            nc.scalar.activation(eta[t][:, h * HALF : (h + 1) * HALF], za[:], SIGMOID)
 
         def message(t, h):
-            ms = psum.tile([P, HALF], F32, name="ms%d_%d" % (t, h), offset=2 * KB * ((PACK * h + t + 1) % BANKS))
+            ms = psum.tile([P, HALF], F32, name="ms%d_%d" % (t, h), offset=bank(t, h, 0))
             for a in range(PASSES):
                 nc.tensor.matmul_mx(
                     out=ms[:],
@@ -188,27 +197,34 @@ def tile_list_rgg_reluP_kernel(
                     stop=(a == PASSES - 1),
                     **moving(0, h, a),
                 )
-            kept = keep.tile([P, HALF], F32, name="kept%d_%d" % (t, h), align_bytes=64)
-            nc.scalar.activation(kept[:], ms[:], RELU)
-            return kept
+            if (t, h) != (0, 0):
+                nc.scalar.activation(kept[t][:, h * HALF : (h + 1) * HALF], ms[:], RELU)
+            return ms
 
         steps = [(t, h) for h in range(HALVES) for t in range(2)] + [(t, h) for t in range(2, PACK) for h in range(HALVES)]
         values = [keep.tile([P, J], F32, name="values%d" % t) for t in range(PACK)]
-        factors = {}
-        for h in range(HALVES):
-            for t in range(PACK):
-                if (t, h) == (0, 0):
-                    factors[t, h] = (gate(t, h), message(t, h))
-                else:
-                    factors[t, h] = (message(t, h), gate(t, h))
-        for i, (t, h) in enumerate(steps):
-            js = slice(h * HALF, (h + 1) * HALF)
-            weighted = laid.tile([P, HALF], F32, name="weighted%d" % i, offset=(12 + 2 * (i % 2)) * KB, align_bytes=64)
-            first, second = factors[t, h]
-            nc.gpsimd.tensor_tensor(weighted[:], first[:], edge_w[:, js], MULT)
-            nc.gpsimd.tensor_tensor(values[t][:, js], weighted[:], second[:], MULT)
+        gate(0, 0)
+        first_ms = message(0, 0)
+        for t, h in sums[1:]:
+            message(t, h)
+            gate(t, h)
+        groups = [(t, h * HALF, HALF, HALF) for t, h in steps[:4]] + [(2, 0, J, HALF), (3, 0, J, J)]
+        for i, (t, j, width, share) in enumerate(groups):
+            weighted = laid.tile([P, width], F32, name="weighted%d" % i, offset=(24 + 2 * (i % 2) * (width < J)) * KB, align_bytes=64)
+            first, second = (eta, kept) if i == 0 else (kept, eta)
+            nc.gpsimd.tensor_tensor(weighted[:], first[t][:, j : j + width], edge_w[:, j : j + width], MULT)
+            if i == 0:
+                nc.vector.scalar_tensor_tensor(values[t][:, :HALF], first_ms[:], 0.0, weighted[:], MAX, MULT)
+                continue
+            for o in range(0, width, share):
+                js = slice(j + o, j + o + share)
+                nc.gpsimd.tensor_tensor(values[t][:, js], weighted[:, o : o + share], second[t][:, js], MULT)
 
-        y_bf = [laid.tile([P, CHUNK, PACK], BF16, name="y_bf%d" % c, offset=4 * KB * c, align_bytes=64) for c in range(CHUNKS)]
+        spans = ((0, 2 * CHUNK), (2 * CHUNK, CHUNK), (3 * CHUNK, CHUNK))
+        y_bf = [
+            laid.tile([P, width, PACK], BF16, name="y_bf%d" % c, offset=(0, 8, 24)[c] * KB, align_bytes=64)
+            for c, (first, width) in enumerate(spans)
+        ]
         y_sc = keep.tile([P, T], U8, name="y_sc", align_bytes=64)
         out_rows = out_0.rearrange("(p t) c -> t p c", t=PACK)
         out_words = out_1[0].rearrange("p c i -> p (c i)").bitcast(I32)
@@ -220,30 +236,28 @@ def tile_list_rgg_reluP_kernel(
             if j + width < J:
                 continue
             nc.sync.dma_start(out_rows[t], window[:])
-            for c in range(CHUNKS):
-                piece = window[:, c * CHUNK : (c + 1) * CHUNK]
-                both = piece.unsqueeze(2).to_broadcast([P, CHUNK, 2])
-                if t == PACK - 1 and c < 2:
+            for c in (1, 0, 2):
+                first, count = spans[c]
+                piece = window[:, first : first + count]
+                both = piece.unsqueeze(2).to_broadcast([P, count, 2])
+                if t == PACK - 1 and c == 0:
                     nc.vector.tensor_copy(y_bf[c][:, :, t], piece)
-                elif t < 2 and c == CHUNKS - 1:
+                elif t < 2 and c == 2:
                     nc.gpsimd.tensor_scalar(y_bf[c][:, :, t], piece, 1.0, -0.0, MULT, ADD)
-                elif t == 2 and c == CHUNKS - 1:
+                elif t == 2 and c == 2:
                     nc.gpsimd.tensor_scalar(y_bf[c][:, :, 2:4], both, 1.0, -0.0, MULT, ADD)
-                elif t == 2 and c < 2:
+                elif t == 2 and c == 0:
                     nc.scalar.copy(y_bf[c][:, :, 2:4], both)
                 else:
                     nc.scalar.copy(y_bf[c][:, :, t], piece)
 
         codes = keep.tile([P, T], I32, name="y_codes", align_bytes=64)
-        for c in range(CHUNKS):
+        for c in (1, 0, 2):
+            cols = slice(spans[c][0], spans[c][0] + spans[c][1])
             nc.vector.quantize_mx(
-                out=codes[:, c * CHUNK : (c + 1) * CHUNK].bitcast(FP8X4),
-                scales=y_sc[:, c * CHUNK : (c + 1) * CHUNK],
-                in_=y_bf[c][:].rearrange("p c i -> p (c i)"),
+                out=codes[:, cols].bitcast(FP8X4), scales=y_sc[:, cols], in_=y_bf[c][:].rearrange("p c i -> p (c i)")
             )
-            if c > 0:
-                first = 0 if c == 1 else c * CHUNK
-                nc.sync.dma_start(out_words[:, first : (c + 1) * CHUNK], codes[:, first : (c + 1) * CHUNK])
+            nc.sync.dma_start(out_words[:, cols], codes[:, cols])
         for q in range(QUADS):
             (nc.scalar if q % 2 else nc.sync).dma_start(
                 out_2[0, ROWS * q : ROWS * (q + 1), :].bitcast(I32), y_sc[QUAD * q : QUAD * q + ROWS, :].bitcast(I32)

@@ -96,19 +96,20 @@ def tile_list_rgg_reluP_kernel(
         def offsets(l, h):
             return lists[l][:, h * HALF // 16 : (h + 1) * HALF // 16]
 
-        edge_sc = [keep.tile([P, PASSES, LISTS, HALF], U8, name="edge_sc%d" % h, align_bytes=64) for h in range(HALVES)]
-
-        def gather_scales(h, picked_sc):
-            for l in range(LISTS):
-                nc.vector.tensor_copy(picked_sc[:, l, :], tab_sc[:].indirect(offsets(l, h)))
+        def gather_scales(h, which, picked_sc):
+            moved = keep.tile([P, PASSES, len(which), HALF], U8, name="edge_sc%d_%d" % (h, which[0]), align_bytes=64)
+            for i, l in enumerate(which):
+                nc.vector.tensor_copy(picked_sc[:, i, :], tab_sc[:].indirect(offsets(l, h)))
+                edge_sc[l, h] = [moved[:, a, i, :] for a in range(PASSES)]
             for a in range(PASSES):
                 for s in range(2):
                     first = TAB_FIRST + ROWS * (2 * a + s)
                     nc.sync.dma_start(
-                        edge_sc[h][SIDE * s : SIDE * (s + 1), a].bitcast(I32), picked_sc[first : first + SIDE].bitcast(I32)
+                        moved[SIDE * s : SIDE * (s + 1), a].bitcast(I32), picked_sc[first : first + SIDE].bitcast(I32)
                     )
 
-        gather_scales(0, keep.tile([P, LISTS, HALF], U8, name="early_sc", align_bytes=64))
+        edge_sc = {}
+        gather_scales(0, (0, 1), keep.tile([P, LISTS, HALF], U8, name="early_sc", align_bytes=64))
         edge_w = keep.tile([P, J], F32, name="edge_w")
         nc.sync.dma_start(edge_w[:], wgo)
 
@@ -158,20 +159,21 @@ def tile_list_rgg_reluP_kernel(
             wc_raw[:].bitcast(U16).rearrange("p a (m t) -> p a t m", t=PACK),
         )
         picked.append(part(1, laid.tile([P, LISTS, PASSES, 2 * HALF], U8, name="picked1", offset=4 * KB, align_bytes=64)))
-        gather_scales(1, laid.tile([P, LISTS, HALF], U8, name="late_sc", offset=20 * KB, align_bytes=64))
+        for l in range(LISTS):
+            gather_scales(1, (l,), laid.tile([P, 1, HALF], U8, name="late_sc%d" % l, offset=20 * KB + l * HALF, align_bytes=64))
 
         def moving(l, h, a):
-            return dict(rhs=picked[h][:, l, a, :].bitcast(FP4X4), rhs_scale=edge_sc[h][:, a, l, :])
+            return dict(rhs=picked[h][:, l, a, :].bitcast(FP4X4), rhs_scale=edge_sc[l, h][a])
 
-        sums = [(t, h) for h in range(HALVES) for t in range(PACK)]
+        sums = [(0, 0), (1, 0), (2, 0), (0, 1), (1, 1), (3, 0), (2, 1), (3, 1)]
         eta = [keep.tile([P, J], F32, name="eta%d" % t) for t in range(PACK)]
         kept = [keep.tile([P, J], F32, name="kept%d" % t) for t in range(PACK)]
 
         def bank(t, h, is_gate):
             k = sums.index((t, h))
-            if k == 0:
-                return 0 if is_gate else 2 * KB * BANKS
-            return 2 * KB * ((k - is_gate) % BANKS)
+            if k < 3:
+                return 2 * KB * ((3, 0), (1, 1), (0, 0))[k][is_gate]
+            return 2 * KB * (1 + (2 * k + is_gate + 1) % BANKS)
 
         def gate(t, h):
             m = slice(t * P, (t + 1) * P)
@@ -201,39 +203,53 @@ def tile_list_rgg_reluP_kernel(
                 nc.scalar.activation(kept[t][:, h * HALF : (h + 1) * HALF], ms[:], RELU)
             return ms
 
-        steps = [(t, h) for h in range(HALVES) for t in range(2)] + [(t, h) for t in range(2, PACK) for h in range(HALVES)]
-        values = [keep.tile([P, J], F32, name="values%d" % t) for t in range(PACK)]
         gate(0, 0)
         first_ms = message(0, 0)
         for t, h in sums[1:]:
             message(t, h)
             gate(t, h)
-        groups = [(t, h * HALF, HALF, HALF) for t, h in steps[:4]] + [(2, 0, J, HALF), (3, 0, J, J)]
-        for i, (t, j, width, share) in enumerate(groups):
-            weighted = laid.tile([P, width], F32, name="weighted%d" % i, offset=(24 + 2 * (i % 2) * (width < J)) * KB, align_bytes=64)
-            first, second = (eta, kept) if i == 0 else (kept, eta)
-            nc.gpsimd.tensor_tensor(weighted[:], first[t][:, j : j + width], edge_w[:, j : j + width], MULT)
-            if i == 0:
-                nc.vector.scalar_tensor_tensor(values[t][:, :HALF], first_ms[:], 0.0, weighted[:], MAX, MULT)
-                continue
-            for o in range(0, width, share):
-                js = slice(j + o, j + o + share)
-                nc.gpsimd.tensor_tensor(values[t][:, js], weighted[:, o : o + share], second[t][:, js], MULT)
+
+        def edges(h):
+            return slice(h * HALF, (h + 1) * HALF)
+
+        def weigh(factor, t, js, offset):
+            weighted = laid.tile([P, js.stop - js.start], F32, name="weighted%d_%d" % (t, js.start), offset=offset * KB, align_bytes=64)
+            nc.gpsimd.tensor_tensor(weighted[:], factor[t][:, js], edge_w[:, js], MULT)
+            return weighted
+
+        ready = []
+
+        def finish(t, js, weighted, values=None):
+            if values is None:
+                values = keep.tile([P, js.stop - js.start], F32, name="values%d_%d" % (t, js.start))
+            nc.gpsimd.tensor_tensor(values[:], weighted[:], eta[t][:, js], MULT)
+            ready.append((t, js, values))
+
+        first_values = keep.tile([P, HALF], F32, name="first_values")
+        nc.vector.scalar_tensor_tensor(first_values[:], first_ms[:], 0.0, weigh(eta, 0, edges(0), 24)[:], MAX, MULT)
+        ready.append((0, edges(0), first_values))
+        second_weighted = weigh(kept, 1, edges(0), 26)
+        early_weighted = weigh(kept, 2, edges(0), 28)
+        finish(1, edges(0), second_weighted)
+        for t in range(2):
+            finish(t, edges(1), weigh(kept, t, edges(1), 26))
+        finish(2, edges(0), early_weighted, laid.tile([P, HALF], F32, name="values2_0", offset=26 * KB, align_bytes=64))
+        finish(2, edges(1), weigh(kept, 2, edges(1), 28))
+        finish(3, slice(0, J), weigh(kept, 3, slice(0, J), 28))
 
         spans = ((0, 2 * CHUNK), (2 * CHUNK, CHUNK), (3 * CHUNK, CHUNK))
         y_bf = [
-            laid.tile([P, width, PACK], BF16, name="y_bf%d" % c, offset=(0, 8, 24)[c] * KB, align_bytes=64)
+            laid.tile([P, width, PACK], BF16, name="y_bf%d" % c, offset=(0, 8, 28)[c] * KB, align_bytes=64)
             for c, (first, width) in enumerate(spans)
         ]
         y_sc = keep.tile([P, T], U8, name="y_sc", align_bytes=64)
         out_rows = out_0.rearrange("(p t) c -> t p c", t=PACK)
         out_words = out_1[0].rearrange("p c i -> p (c i)").bitcast(I32)
 
-        pieces = [(t, h * HALF, HALF) for t, h in steps[:-HALVES]] + [(PACK - 1, 0, J)]
-        for t, j, width in pieces:
+        for t, js, values in ready:
             window = windows[t]
-            nc.vector.tensor_copy(window[:].indirect(dst_list[:, j // 16 : (j + width) // 16]), values[t][:, j : j + width])
-            if j + width < J:
+            nc.vector.tensor_copy(window[:].indirect(dst_list[:, js.start // 16 : js.stop // 16]), values[:])
+            if js.stop < J:
                 continue
             nc.sync.dma_start(out_rows[t], window[:])
             for c in (1, 0, 2):
@@ -252,10 +268,12 @@ def tile_list_rgg_reluP_kernel(
                     nc.scalar.copy(y_bf[c][:, :, t], piece)
 
         codes = keep.tile([P, T], I32, name="y_codes", align_bytes=64)
-        for c in (1, 0, 2):
-            cols = slice(spans[c][0], spans[c][0] + spans[c][1])
+        for c, o in ((1, 0), (0, 0), (0, CHUNK), (2, 0)):
+            cols = slice(spans[c][0] + o, spans[c][0] + o + CHUNK)
             nc.vector.quantize_mx(
-                out=codes[:, cols].bitcast(FP8X4), scales=y_sc[:, cols], in_=y_bf[c][:].rearrange("p c i -> p (c i)")
+                out=codes[:, cols].bitcast(FP8X4),
+                scales=y_sc[:, cols],
+                in_=y_bf[c][:, o : o + CHUNK].rearrange("p c i -> p (c i)"),
             )
             nc.sync.dma_start(out_words[:, cols], codes[:, cols])
         for q in range(QUADS):

@@ -237,9 +237,9 @@ def tile_list_rgg_reluP_kernel(
         finish(2, edges(1), weigh(kept, 2, edges(1), 28))
         finish(3, slice(0, J), weigh(kept, 3, slice(0, J), 28))
 
-        spans = ((0, 2 * CHUNK), (2 * CHUNK, CHUNK), (3 * CHUNK, CHUNK))
+        spans = ((0, 2 * CHUNK), (2 * CHUNK, CHUNK // 2), (5 * CHUNK // 2, 3 * CHUNK // 2))
         y_bf = [
-            laid.tile([P, width, PACK], BF16, name="y_bf%d" % c, offset=(0, 8, 28)[c] * KB, align_bytes=64)
+            laid.tile([P, width, PACK], BF16, name="y_bf%d" % c, offset=(0, 8, 26)[c] * KB, align_bytes=64)
             for c, (first, width) in enumerate(spans)
         ]
         y_sc = keep.tile([P, T], U8, name="y_sc", align_bytes=64)
@@ -264,16 +264,19 @@ def tile_list_rgg_reluP_kernel(
                     nc.gpsimd.tensor_scalar(y_bf[c][:, :, 2:4], both, 1.0, -0.0, MULT, ADD)
                 elif t == 2 and c == 0:
                     nc.scalar.copy(y_bf[c][:, :, 2:4], both)
+                elif c == 2:
+                    for cols in (slice(0, CHUNK), slice(CHUNK, count)):
+                        nc.scalar.copy(y_bf[c][:, cols, t], piece[:, cols])
                 else:
                     nc.scalar.copy(y_bf[c][:, :, t], piece)
 
         codes = keep.tile([P, T], I32, name="y_codes", align_bytes=64)
-        for c, o in ((1, 0), (0, 0), (0, CHUNK), (2, 0)):
-            cols = slice(spans[c][0] + o, spans[c][0] + o + CHUNK)
+        for c, o, width in ((1, 0, CHUNK // 2), (0, 0, CHUNK), (0, CHUNK, CHUNK), (2, 0, CHUNK), (2, CHUNK, CHUNK // 2)):
+            cols = slice(spans[c][0] + o, spans[c][0] + o + width)
             nc.vector.quantize_mx(
                 out=codes[:, cols].bitcast(FP8X4),
                 scales=y_sc[:, cols],
-                in_=y_bf[c][:, o : o + CHUNK].rearrange("p c i -> p (c i)"),
+                in_=y_bf[c][:, o : o + width].rearrange("p c i -> p (c i)"),
             )
             nc.sync.dma_start(out_words[:, cols], codes[:, cols])
         for q in range(QUADS):

@@ -159,28 +159,27 @@ def tile_list_rgg_reluP_kernel(
             wc_raw[:].bitcast(U16).rearrange("p a (m t) -> p a t m", t=PACK),
         )
         picked.append(part(1, laid.tile([P, LISTS, PASSES, 2 * HALF], U8, name="picked1", offset=4 * KB, align_bytes=64)))
-        for l in range(LISTS):
-            gather_scales(1, (l,), laid.tile([P, 1, HALF], U8, name="late_sc%d" % l, offset=20 * KB + l * HALF, align_bytes=64))
+        gather_scales(1, (0, 1), laid.tile([P, LISTS, HALF], U8, name="late_sc", offset=20 * KB, align_bytes=64))
 
         def moving(l, h, a):
             return dict(rhs=picked[h][:, l, a, :].bitcast(FP4X4), rhs_scale=edge_sc[l, h][a])
 
-        sums = [(0, 0), (1, 0), (2, 0), (0, 1), (1, 1), (3, 0), (2, 1), (3, 1)]
+        sums = [(t, h) for h in range(HALVES) for t in range(PACK)]
         eta = [keep.tile([P, J], F32, name="eta%d" % t) for t in range(PACK)]
         kept = [keep.tile([P, J], F32, name="kept%d" % t) for t in range(PACK)]
 
         def bank(t, h, is_gate):
             k = sums.index((t, h))
             if k < 3:
-                return 2 * KB * ((3, 0), (1, 1), (0, 0))[k][is_gate]
-            return 2 * KB * (1 + (2 * k + is_gate + 1) % BANKS)
+                return 2 * KB * ((3, 0), (1, 2), (0, 2))[k][is_gate]
+            return 2 * KB * (1, 0, 2)[(2 * k + is_gate) % BANKS]
 
         def gate(t, h):
             m = slice(t * P, (t + 1) * P)
             za = psum.tile([P, HALF], F32, name="za%d_%d" % (t, h), offset=bank(t, h, 1))
             from_wa = [(wa_q[:, a, m], wa_sc[:, a, m], 1, a) for a in range(PASSES)]
             from_wb = [(wb_q[a][:, m], wb_sc[a][:, m], 0, a) for a in range(PASSES)]
-            terms = from_wb[:1] + from_wa + from_wb[1:] if h == 0 else from_wb + from_wa
+            terms = from_wb[:1] + from_wa + from_wb[1:] if (t, h) == (0, 0) else from_wb[::-1] + from_wa
             for i, (words, scales, l, a) in enumerate(terms):
                 nc.tensor.matmul_mx(
                     out=za[:], lhsT=words.bitcast(FP8X4), lhsT_scale=scales,
@@ -204,8 +203,10 @@ def tile_list_rgg_reluP_kernel(
             return ms
 
         gate(0, 0)
+        gate(1, 0)
         first_ms = message(0, 0)
-        for t, h in sums[1:]:
+        message(1, 0)
+        for t, h in sums[2:]:
             message(t, h)
             gate(t, h)
 
@@ -219,23 +220,22 @@ def tile_list_rgg_reluP_kernel(
 
         ready = []
 
-        def finish(t, js, weighted, values=None):
-            if values is None:
-                values = keep.tile([P, js.stop - js.start], F32, name="values%d_%d" % (t, js.start))
-            nc.gpsimd.tensor_tensor(values[:], weighted[:], eta[t][:, js], MULT)
+        def finish(factor, t, js, weighted):
+            values = keep.tile([P, js.stop - js.start], F32, name="values%d_%d" % (t, js.start))
+            nc.gpsimd.tensor_tensor(values[:], weighted[:], factor[t][:, js], MULT)
             ready.append((t, js, values))
 
         first_values = keep.tile([P, HALF], F32, name="first_values")
         nc.vector.scalar_tensor_tensor(first_values[:], first_ms[:], 0.0, weigh(eta, 0, edges(0), 24)[:], MAX, MULT)
         ready.append((0, edges(0), first_values))
-        second_weighted = weigh(kept, 1, edges(0), 26)
-        early_weighted = weigh(kept, 2, edges(0), 28)
-        finish(1, edges(0), second_weighted)
-        for t in range(2):
-            finish(t, edges(1), weigh(kept, t, edges(1), 26))
-        finish(2, edges(0), early_weighted, laid.tile([P, HALF], F32, name="values2_0", offset=26 * KB, align_bytes=64))
-        finish(2, edges(1), weigh(kept, 2, edges(1), 28))
-        finish(3, slice(0, J), weigh(kept, 3, slice(0, J), 28))
+        finish(kept, 1, edges(0), weigh(eta, 1, edges(0), 26))
+        finish(eta, 2, edges(0), weigh(kept, 2, edges(0), 26))
+        waiting = weigh(kept, 0, edges(1), 26)
+        for t in range(PACK - 1):
+            ahead = weigh(kept, t + 1, edges(1), (28, 26)[t]) if t < 2 else weigh(kept, 3, slice(0, J), 28)
+            finish(eta, t, edges(1), waiting)
+            waiting = ahead
+        finish(eta, 3, slice(0, J), waiting)
 
         spans = ((0, 2 * CHUNK), (2 * CHUNK, CHUNK // 2), (5 * CHUNK // 2, 3 * CHUNK // 2))
         y_bf = [

@@ -74,16 +74,22 @@ def tile_list_rgg_reluP_kernel(
             )
 
         scale_loads = [(w, q) for w in range(2) for q in range(QUADS)]
-        wb_raw = [keep.tile([P, PACK, N], F32, name="wb_raw%d" % a) for a in range(PASSES)]
-        wb_rows = wb.rearrange("(a p i) n -> a p i n", p=P, i=PACK)
+        wb_raw = [[keep.tile([P, PACK, N // 2], F32, name="wb_raw%d_%d" % (a, s)) for s in range(2)] for a in range(PASSES)]
+        wb_rows = wb.rearrange("(a p i) (s n) -> a s p i n", p=P, i=PACK, s=2)
+
+        def load_wb(a):
+            for s in range(2):
+                nc.sync.dma_start(wb_raw[a][s][:], wb_rows[a, s])
+
         for w, q in scale_loads[:3]:
             load_weight_scales(w, q)
-        nc.sync.dma_start(wb_raw[0][:], wb_rows[0])
+        load_wb(0)
         for w, q in scale_loads[3:]:
             load_weight_scales(w, q)
-        nc.sync.dma_start(wb_raw[1][:], wb_rows[1])
-        wa_raw = keep.tile([P, PASSES, N], I32, name="wa_raw", align_bytes=64)
+        nc.sync.dma_start(wb_raw[1][0][:], wb_rows[1, 0])
+        wa_raw = laid.tile([P, PASSES, N], I32, name="wa_raw", offset=42 * KB, align_bytes=64)
         nc.sync.dma_start(wa_raw[:], wa_words.rearrange("a p n i -> p a (n i)").bitcast(I32))
+        nc.sync.dma_start(wb_raw[1][1][:], wb_rows[1, 1])
         wc_raw = laid.tile([P, PASSES, 2 * N], U8, name="wc_raw", offset=4 * KB, align_bytes=64)
         nc.sync.dma_start(wc_raw[:].bitcast(I32), wc_words.rearrange("a p b -> p a b").bitcast(I32))
 
@@ -135,15 +141,14 @@ def tile_list_rgg_reluP_kernel(
             nc.sync.dma_start(wc_sc[SIDE * s : SIDE * (s + 1)].bitcast(I32), wa_sc[first : first + SIDE].bitcast(I32))
 
         picked = [part(0, laid.tile([P, LISTS, PASSES, 2 * HALF], U8, name="picked0", offset=12 * KB, align_bytes=64))]
-        wb_q = [keep.tile([P, N], U32, name="wb_q%d" % a, align_bytes=64) for a in range(PASSES)]
+        wb_q = [laid.tile([P, N], U32, name="wb_q%d" % a, offset=(40, 42)[a] * KB, align_bytes=64) for a in range(PASSES)]
         wb_sc = [keep.tile([P, N], U8, name="wb_sc%d" % a, align_bytes=64) for a in range(PASSES)]
 
         def quantise_wb(a):
             grouped = laid.tile([P, N * PACK], BF16, name="wb_grouped%d" % a, offset=(32, 36)[a] * KB, align_bytes=64)
-            nc.scalar.copy(
-                grouped[:].rearrange("p (t m i) -> p m t i", t=PACK, i=PACK),
-                wb_raw[a][:].rearrange("p i (m t) -> p m t i", t=PACK),
-            )
+            by_column = grouped[:].rearrange("p (t s m i) -> p s m t i", t=PACK, s=2, i=PACK)
+            for s in range(2):
+                nc.scalar.copy(by_column[:, s], wb_raw[a][s][:].rearrange("p i (m t) -> p m t i", t=PACK))
             nc.vector.quantize_mx(out=wb_q[a][:].bitcast(FP8X4), scales=wb_sc[a][:], in_=grouped[:])
 
         quantise_wb(0)
@@ -153,7 +158,7 @@ def tile_list_rgg_reluP_kernel(
             wa_raw[:].rearrange("p a (m e t) -> p a m t e", t=PACK, e=LINE),
         )
         quantise_wb(1)
-        wc_q = laid.tile([P, PASSES, 2 * N], U8, name="wc_q", offset=36 * KB, align_bytes=64)
+        wc_q = laid.tile([P, PASSES, 2 * N], U8, name="wc_q", offset=44 * KB, align_bytes=64)
         nc.vector.tensor_copy(
             wc_q[:].bitcast(U16).rearrange("p a (t m) -> p a t m", t=PACK),
             wc_raw[:].bitcast(U16).rearrange("p a (m t) -> p a t m", t=PACK),

@@ -33,9 +33,8 @@ TAB_FIRST = 48
 WC_ROWS = (4, 36, 60, 92)
 LINE = 4
 CHUNK = 512
-CHUNKS = T // CHUNK
-BANKS = 3
 KB = 1024
+BANK = 2 * KB
 
 
 def tile_list_rgg_reluP_kernel(
@@ -54,10 +53,10 @@ def tile_list_rgg_reluP_kernel(
         nc.sync.dma_start(src_list[:], offs)
 
         w_sc_raw = laid.tile([P, PASSES, N], U8, name="w_sc_raw", offset=12 * KB, align_bytes=64)
-        nc.gpsimd.memset(w_sc_raw[:].bitcast(I32), 0)
         tab_sc = keep.tile([P, T], U8, name="tab_sc", align_bytes=64)
         for first, last in ((0, TAB_FIRST), (SIDE, TAB_FIRST + QUAD), (3 * QUAD, P)):
             nc.gpsimd.memset(tab_sc[first:last, :].bitcast(I32), 0)
+        nc.gpsimd.memset(w_sc_raw[:].bitcast(I32), 0)
         sc_rows = tab_scales.rearrange("a (h e r) t -> e (a h) r t", e=2, r=ROWS)
         for e in range(2):
             first = TAB_FIRST + QUAD * e
@@ -74,16 +73,18 @@ def tile_list_rgg_reluP_kernel(
             )
 
         scale_loads = [(w, q) for w in range(2) for q in range(QUADS)]
-        wb_raw = [[keep.tile([P, PACK, N // 2], F32, name="wb_raw%d_%d" % (a, s)) for s in range(2)] for a in range(PASSES)]
+        wb_raw = [
+            [
+                laid.tile([P, PACK, N // 2], F32, name="wb_raw%d_%d" % (a, s), offset=(46 + 10 * a + 4 * s) * KB, align_bytes=64)
+                for s in range(2)
+            ]
+            for a in range(PASSES)
+        ]
         wb_rows = wb.rearrange("(a p i) (s n) -> a s p i n", p=P, i=PACK, s=2)
-
-        def load_wb(a):
-            for s in range(2):
-                nc.sync.dma_start(wb_raw[a][s][:], wb_rows[a, s])
-
         for w, q in scale_loads[:3]:
             load_weight_scales(w, q)
-        load_wb(0)
+        for s in range(2):
+            nc.sync.dma_start(wb_raw[0][s][:], wb_rows[0, s])
         for w, q in scale_loads[3:]:
             load_weight_scales(w, q)
         nc.sync.dma_start(wb_raw[1][0][:], wb_rows[1, 0])
@@ -102,20 +103,19 @@ def tile_list_rgg_reluP_kernel(
         def offsets(l, h):
             return lists[l][:, h * HALF // 16 : (h + 1) * HALF // 16]
 
-        def gather_scales(h, which, picked_sc):
-            moved = keep.tile([P, PASSES, len(which), HALF], U8, name="edge_sc%d_%d" % (h, which[0]), align_bytes=64)
-            for i, l in enumerate(which):
-                nc.vector.tensor_copy(picked_sc[:, i, :], tab_sc[:].indirect(offsets(l, h)))
-                edge_sc[l, h] = [moved[:, a, i, :] for a in range(PASSES)]
+        def gather_scales(h, picked_sc):
+            moved = keep.tile([P, PASSES, LISTS, HALF], U8, name="edge_sc%d_0" % h, align_bytes=64)
+            for l in range(LISTS):
+                nc.vector.tensor_copy(picked_sc[:, l, :], tab_sc[:].indirect(offsets(l, h)))
             for a in range(PASSES):
                 for s in range(2):
                     first = TAB_FIRST + ROWS * (2 * a + s)
                     nc.sync.dma_start(
                         moved[SIDE * s : SIDE * (s + 1), a].bitcast(I32), picked_sc[first : first + SIDE].bitcast(I32)
                     )
+            return moved
 
-        edge_sc = {}
-        gather_scales(0, (0, 1), keep.tile([P, LISTS, HALF], U8, name="early_sc", align_bytes=64))
+        edge_sc = [gather_scales(0, keep.tile([P, LISTS, HALF], U8, name="early_sc", align_bytes=64))]
         edge_w = keep.tile([P, J], F32, name="edge_w")
         nc.sync.dma_start(edge_w[:], wgo)
 
@@ -130,7 +130,6 @@ def tile_list_rgg_reluP_kernel(
             )
             return target
 
-
         wa_sc = laid.tile([P, PASSES, N], U8, name="wa_sc", offset=0, align_bytes=64)
         wc_sc = keep.tile([P, PASSES, N], U8, name="wc_sc", align_bytes=64)
         nc.vector.tensor_copy(
@@ -140,17 +139,21 @@ def tile_list_rgg_reluP_kernel(
             first = WC_ROWS[2 * s]
             nc.sync.dma_start(wc_sc[SIDE * s : SIDE * (s + 1)].bitcast(I32), wa_sc[first : first + SIDE].bitcast(I32))
 
-        picked = [part(0, laid.tile([P, LISTS, PASSES, 2 * HALF], U8, name="picked0", offset=12 * KB, align_bytes=64))]
-        wb_q = [laid.tile([P, N], U32, name="wb_q%d" % a, offset=(40, 42)[a] * KB, align_bytes=64) for a in range(PASSES)]
+        wb_q = [keep.tile([P, N], U32, name="wb_q%d" % a, align_bytes=64) for a in range(PASSES)]
         wb_sc = [keep.tile([P, N], U8, name="wb_sc%d" % a, align_bytes=64) for a in range(PASSES)]
 
-        def quantise_wb(a):
+        def round_wb(a):
             grouped = laid.tile([P, N * PACK], BF16, name="wb_grouped%d" % a, offset=(32, 36)[a] * KB, align_bytes=64)
             by_column = grouped[:].rearrange("p (t s m i) -> p s m t i", t=PACK, s=2, i=PACK)
             for s in range(2):
                 nc.scalar.copy(by_column[:, s], wb_raw[a][s][:].rearrange("p i (m t) -> p m t i", t=PACK))
-            nc.vector.quantize_mx(out=wb_q[a][:].bitcast(FP8X4), scales=wb_sc[a][:], in_=grouped[:])
+            return grouped
 
+        def quantise_wb(a):
+            nc.vector.quantize_mx(out=wb_q[a][:].bitcast(FP8X4), scales=wb_sc[a][:], in_=wb_grouped[a][:])
+
+        wb_grouped = [round_wb(a) for a in range(PASSES)]
+        picked = [part(0, laid.tile([P, LISTS, PASSES, 2 * HALF], U8, name="picked0", offset=50 * KB, align_bytes=64))]
         quantise_wb(0)
         wa_q = laid.tile([P, PASSES, N], I32, name="wa_q", offset=8 * KB, align_bytes=64)
         nc.vector.tensor_copy(
@@ -158,26 +161,31 @@ def tile_list_rgg_reluP_kernel(
             wa_raw[:].rearrange("p a (m e t) -> p a m t e", t=PACK, e=LINE),
         )
         quantise_wb(1)
-        wc_q = laid.tile([P, PASSES, 2 * N], U8, name="wc_q", offset=44 * KB, align_bytes=64)
+        wc_q = laid.tile([P, PASSES, 2 * N], U8, name="wc_q", offset=60 * KB, align_bytes=64)
         nc.vector.tensor_copy(
             wc_q[:].bitcast(U16).rearrange("p a (t m) -> p a t m", t=PACK),
             wc_raw[:].bitcast(U16).rearrange("p a (m t) -> p a t m", t=PACK),
         )
-        picked.append(part(1, laid.tile([P, LISTS, PASSES, 2 * HALF], U8, name="picked1", offset=4 * KB, align_bytes=64)))
-        gather_scales(1, (0, 1), laid.tile([P, LISTS, HALF], U8, name="late_sc", offset=20 * KB, align_bytes=64))
+        picked.append(part(1, laid.tile([P, LISTS, PASSES, 2 * HALF], U8, name="picked1", offset=63 * KB, align_bytes=64)))
+        edge_sc.append(gather_scales(1, laid.tile([P, LISTS, HALF], U8, name="late_sc", offset=62 * KB, align_bytes=64)))
 
         def moving(l, h, a):
-            return dict(rhs=picked[h][:, l, a, :].bitcast(FP4X4), rhs_scale=edge_sc[l, h][a])
+            return dict(rhs=picked[h][:, l, a, :].bitcast(FP4X4), rhs_scale=edge_sc[h][:, a, l, :])
 
-        sums = [(t, h) for h in range(HALVES) for t in range(PACK)]
+        steps = [(t, h) for h in range(HALVES) for t in range(PACK)]
         eta = [keep.tile([P, J], F32, name="eta%d" % t) for t in range(PACK)]
         kept = [keep.tile([P, J], F32, name="kept%d" % t) for t in range(PACK)]
 
+        def edges(h):
+            return slice(h * HALF, (h + 1) * HALF)
+
         def bank(t, h, is_gate):
-            k = sums.index((t, h))
-            if k < 3:
-                return 2 * KB * ((3, 0), (1, 2), (0, 2))[k][is_gate]
-            return 2 * KB * (1, 0, 2)[(2 * k + is_gate) % BANKS]
+            k = steps.index((t, h))
+            first_steps = ((3, 0), (1, 2), (0, 2))
+            if k < len(first_steps):
+                return BANK * first_steps[k][is_gate]
+            in_turn = (1, 0, 2)
+            return BANK * in_turn[(2 * k + is_gate) % len(in_turn)]
 
         def gate(t, h):
             m = slice(t * P, (t + 1) * P)
@@ -190,7 +198,7 @@ def tile_list_rgg_reluP_kernel(
                     out=za[:], lhsT=words.bitcast(FP8X4), lhsT_scale=scales,
                     start=(i == 0), stop=(i == len(terms) - 1), **moving(l, h, a),
                 )
-            nc.scalar.activation(eta[t][:, h * HALF : (h + 1) * HALF], za[:], SIGMOID)
+            nc.scalar.activation(eta[t][:, edges(h)], za[:], SIGMOID)
 
         def message(t, h):
             ms = psum.tile([P, HALF], F32, name="ms%d_%d" % (t, h), offset=bank(t, h, 0))
@@ -203,23 +211,22 @@ def tile_list_rgg_reluP_kernel(
                     stop=(a == PASSES - 1),
                     **moving(0, h, a),
                 )
-            if (t, h) != (0, 0):
-                nc.scalar.activation(kept[t][:, h * HALF : (h + 1) * HALF], ms[:], RELU)
             return ms
+
+        def kept_message(t, h):
+            nc.scalar.activation(kept[t][:, edges(h)], message(t, h)[:], RELU)
 
         gate(0, 0)
         gate(1, 0)
         first_ms = message(0, 0)
-        message(1, 0)
-        for t, h in sums[2:]:
-            message(t, h)
+        kept_message(1, 0)
+        for t, h in steps[2:]:
+            kept_message(t, h)
             gate(t, h)
 
-        def edges(h):
-            return slice(h * HALF, (h + 1) * HALF)
-
         def weigh(factor, t, js, offset):
-            weighted = laid.tile([P, js.stop - js.start], F32, name="weighted%d_%d" % (t, js.start), offset=offset * KB, align_bytes=64)
+            name = "weighted%d_%d" % (t, js.start)
+            weighted = laid.tile([P, js.stop - js.start], F32, name=name, offset=offset, align_bytes=64)
             nc.gpsimd.tensor_tensor(weighted[:], factor[t][:, js], edge_w[:, js], MULT)
             return weighted
 
@@ -230,21 +237,23 @@ def tile_list_rgg_reluP_kernel(
             nc.gpsimd.tensor_tensor(values[:], weighted[:], factor[t][:, js], MULT)
             ready.append((t, js, values))
 
+        place = (24 * KB, 26 * KB, 28 * KB)
         first_values = keep.tile([P, HALF], F32, name="first_values")
-        nc.vector.scalar_tensor_tensor(first_values[:], first_ms[:], 0.0, weigh(eta, 0, edges(0), 24)[:], MAX, MULT)
+        nc.vector.scalar_tensor_tensor(first_values[:], first_ms[:], 0.0, weigh(eta, 0, edges(0), place[0])[:], MAX, MULT)
         ready.append((0, edges(0), first_values))
-        finish(kept, 1, edges(0), weigh(eta, 1, edges(0), 26))
-        finish(eta, 2, edges(0), weigh(kept, 2, edges(0), 26))
-        waiting = weigh(kept, 0, edges(1), 26)
-        for t in range(PACK - 1):
-            ahead = weigh(kept, t + 1, edges(1), (28, 26)[t]) if t < 2 else weigh(kept, 3, slice(0, J), 28)
-            finish(eta, t, edges(1), waiting)
+        finish(kept, 1, edges(0), weigh(eta, 1, edges(0), place[1]))
+        finish(eta, 2, edges(0), weigh(kept, 2, edges(0), place[1]))
+        later = [(t, edges(1)) for t in range(PACK - 1)] + [(PACK - 1, slice(0, J))]
+        waiting = weigh(kept, *later[0], place[1])
+        for i, (t, js) in enumerate(later[:-1]):
+            ahead = weigh(kept, *later[i + 1], place[2 - i % 2])
+            finish(eta, t, js, waiting)
             waiting = ahead
-        finish(eta, 3, slice(0, J), waiting)
+        finish(eta, *later[-1], waiting)
 
         spans = ((0, 2 * CHUNK), (2 * CHUNK, CHUNK // 2), (5 * CHUNK // 2, 3 * CHUNK // 2))
         y_bf = [
-            laid.tile([P, width, PACK], BF16, name="y_bf%d" % c, offset=(0, 8, 26)[c] * KB, align_bytes=64)
+            laid.tile([P, width, PACK], BF16, name="y_bf%d" % c, offset=(0, 8 * KB, place[1])[c], align_bytes=64)
             for c, (first, width) in enumerate(spans)
         ]
         y_sc = keep.tile([P, T], U8, name="y_sc", align_bytes=64)
@@ -266,9 +275,9 @@ def tile_list_rgg_reluP_kernel(
                 elif t < 2 and c == 2:
                     nc.gpsimd.tensor_scalar(y_bf[c][:, :, t], piece, 1.0, -0.0, MULT, ADD)
                 elif t == 2 and c == 2:
-                    nc.gpsimd.tensor_scalar(y_bf[c][:, :, 2:4], both, 1.0, -0.0, MULT, ADD)
+                    nc.gpsimd.tensor_scalar(y_bf[c][:, :, t:], both, 1.0, -0.0, MULT, ADD)
                 elif t == 2 and c == 0:
-                    nc.scalar.copy(y_bf[c][:, :, 2:4], both)
+                    nc.scalar.copy(y_bf[c][:, :, t:], both)
                 elif c == 2:
                     for cols in (slice(0, CHUNK), slice(CHUNK, count)):
                         nc.scalar.copy(y_bf[c][:, cols, t], piece[:, cols])

@@ -33,6 +33,7 @@ TAB_FIRST = 48
 WC_ROWS = (4, 36, 60, 92)
 LINE = 4
 CHUNK = 512
+OWN = 928
 KB = 1024
 BANK = 2 * KB
 
@@ -50,7 +51,6 @@ def tile_list_rgg_reluP_kernel(
         src_list = held.tile([P, J // 16], U16, name="src_list")
         dst_list = held.tile([P, J // 16], U16, name="dst_list")
         lists = (src_list, dst_list)
-        nc.sync.dma_start(src_list[:], offs)
 
         w_sc_raw = laid.tile([P, PASSES, N], U8, name="w_sc_raw", offset=12 * KB, align_bytes=64)
         tab_sc = keep.tile([P, T], U8, name="tab_sc", align_bytes=64)
@@ -61,6 +61,7 @@ def tile_list_rgg_reluP_kernel(
         for e in range(2):
             first = TAB_FIRST + QUAD * e
             nc.sync.dma_start(tab_sc[first : first + 16, :].bitcast(I32), sc_rows[e].bitcast(I32))
+        nc.sync.dma_start(src_list[:], offs)
         nc.sync.dma_start(dst_list[:], offs2)
         tab_w = keep.tile([P, T], I32, name="tab_w", align_bytes=64)
         nc.sync.dma_start(tab_w[:], tab_words[0].rearrange("p t i -> p (t i)").bitcast(I32))
@@ -87,10 +88,10 @@ def tile_list_rgg_reluP_kernel(
             nc.sync.dma_start(wb_raw[0][s][:], wb_rows[0, s])
         for w, q in scale_loads[3:]:
             load_weight_scales(w, q)
-        nc.sync.dma_start(wb_raw[1][0][:], wb_rows[1, 0])
+        for s in range(2):
+            nc.sync.dma_start(wb_raw[1][s][:], wb_rows[1, s])
         wa_raw = laid.tile([P, PASSES, N], I32, name="wa_raw", offset=42 * KB, align_bytes=64)
         nc.sync.dma_start(wa_raw[:], wa_words.rearrange("a p n i -> p a (n i)").bitcast(I32))
-        nc.sync.dma_start(wb_raw[1][1][:], wb_rows[1, 1])
         wc_raw = laid.tile([P, PASSES, 2 * N], U8, name="wc_raw", offset=4 * KB, align_bytes=64)
         nc.sync.dma_start(wc_raw[:].bitcast(I32), wc_words.rearrange("a p b -> p a b").bitcast(I32))
 
@@ -237,7 +238,7 @@ def tile_list_rgg_reluP_kernel(
             nc.gpsimd.tensor_tensor(values[:], weighted[:], factor[t][:, js], MULT)
             ready.append((t, js, values))
 
-        place = (24 * KB, 26 * KB, 28 * KB)
+        place = (24 * KB, 26 * KB, 28 * KB, 30 * KB)
         first_values = keep.tile([P, HALF], F32, name="first_values")
         nc.vector.scalar_tensor_tensor(first_values[:], first_ms[:], 0.0, weigh(eta, 0, edges(0), place[0])[:], MAX, MULT)
         ready.append((0, edges(0), first_values))
@@ -246,7 +247,7 @@ def tile_list_rgg_reluP_kernel(
         later = [(t, edges(1)) for t in range(PACK - 1)] + [(PACK - 1, slice(0, J))]
         waiting = weigh(kept, *later[0], place[1])
         for i, (t, js) in enumerate(later[:-1]):
-            ahead = weigh(kept, *later[i + 1], place[2 - i % 2])
+            ahead = weigh(kept, *later[i + 1], place[(2, 0, 3)[i]])
             finish(eta, t, js, waiting)
             waiting = ahead
         finish(eta, *later[-1], waiting)
@@ -256,7 +257,6 @@ def tile_list_rgg_reluP_kernel(
             laid.tile([P, width, PACK], BF16, name="y_bf%d" % c, offset=(0, 8 * KB, place[1])[c], align_bytes=64)
             for c, (first, width) in enumerate(spans)
         ]
-        y_sc = keep.tile([P, T], U8, name="y_sc", align_bytes=64)
         out_rows = out_0.rearrange("(p t) c -> t p c", t=PACK)
         out_words = out_1[0].rearrange("p c i -> p (c i)").bitcast(I32)
 
@@ -271,7 +271,8 @@ def tile_list_rgg_reluP_kernel(
                 piece = window[:, first : first + count]
                 both = piece.unsqueeze(2).to_broadcast([P, count, 2])
                 if t == PACK - 1 and c == 0:
-                    nc.vector.tensor_copy(y_bf[c][:, :, t], piece)
+                    nc.vector.tensor_copy(y_bf[c][:, :OWN, t], piece[:, :OWN])
+                    nc.scalar.copy(y_bf[c][:, OWN:, t], piece[:, OWN:])
                 elif t < 2 and c == 2:
                     nc.gpsimd.tensor_scalar(y_bf[c][:, :, t], piece, 1.0, -0.0, MULT, ADD)
                 elif t == 2 and c == 2:
@@ -285,15 +286,22 @@ def tile_list_rgg_reluP_kernel(
                     nc.scalar.copy(y_bf[c][:, :, t], piece)
 
         codes = keep.tile([P, T], I32, name="y_codes", align_bytes=64)
-        for c, o, width in ((1, 0, CHUNK // 2), (0, 0, CHUNK), (0, CHUNK, CHUNK), (2, 0, CHUNK), (2, CHUNK, CHUNK // 2)):
-            cols = slice(spans[c][0] + o, spans[c][0] + o + width)
-            nc.vector.quantize_mx(
-                out=codes[:, cols].bitcast(FP8X4),
-                scales=y_sc[:, cols],
-                in_=y_bf[c][:, o : o + width].rearrange("p c i -> p (c i)"),
-            )
+        y_sc = keep.tile([P, CHUNK], U8, name="y_sc", align_bytes=64)
+        width = CHUNK // 2
+        for pieces in ((4,), (1, 0), (3, 2), (5, 6), (7,)):
+            for u in pieces:
+                first = u * width
+                c = max(i for i in range(len(spans)) if spans[i][0] <= first)
+                o = first - spans[c][0]
+                nc.vector.quantize_mx(
+                    out=codes[:, first : first + width].bitcast(FP8X4),
+                    scales=y_sc[ROWS * (u // 2) :, u % 2 * width : (u % 2 + 1) * width],
+                    in_=y_bf[c][:, o : o + width].rearrange("p c i -> p (c i)"),
+                )
+            cols = slice(min(pieces) * width, (max(pieces) + 1) * width)
             nc.sync.dma_start(out_words[:, cols], codes[:, cols])
+        out_scales = out_2[0].rearrange("(q r) (g c) -> q g r c", r=ROWS, c=CHUNK)
         for q in range(QUADS):
             (nc.scalar if q % 2 else nc.sync).dma_start(
-                out_2[0, ROWS * q : ROWS * (q + 1), :].bitcast(I32), y_sc[QUAD * q : QUAD * q + ROWS, :].bitcast(I32)
+                out_scales[q].bitcast(I32), y_sc[QUAD * q : QUAD * q + 16, :].bitcast(I32)
             )

@@ -52,11 +52,15 @@ def tile_list_rgg_reluP_kernel(
         dst_list = held.tile([P, J // 16], U16, name="dst_list")
         lists = (src_list, dst_list)
 
+        warm = keep.tile([P, 2], F32, name="warm")
+        nc.gpsimd.memset(warm[:, :1], 0.0)
+        nc.scalar.activation(warm[:, 1:], warm[:, :1], SIGMOID)
+
         w_sc_raw = laid.tile([P, PASSES, N], U8, name="w_sc_raw", offset=12 * KB, align_bytes=64)
         tab_sc = keep.tile([P, T], U8, name="tab_sc", align_bytes=64)
+        nc.gpsimd.memset(w_sc_raw[:].bitcast(I32), 0)
         for first, last in ((0, TAB_FIRST), (SIDE, TAB_FIRST + QUAD), (3 * QUAD, P)):
             nc.gpsimd.memset(tab_sc[first:last, :].bitcast(I32), 0)
-        nc.gpsimd.memset(w_sc_raw[:].bitcast(I32), 0)
         sc_rows = tab_scales.rearrange("a (h e r) t -> e (a h) r t", e=2, r=ROWS)
         for e in range(2):
             first = TAB_FIRST + QUAD * e
@@ -76,7 +80,7 @@ def tile_list_rgg_reluP_kernel(
         scale_loads = [(w, q) for w in range(2) for q in range(QUADS)]
         wb_raw = [
             [
-                laid.tile([P, PACK, N // 2], F32, name="wb_raw%d_%d" % (a, s), offset=(46 + 10 * a + 4 * s) * KB, align_bytes=64)
+                laid.tile([P, PACK, N // 2], F32, name="wb_raw%d_%d" % (a, s), offset=(46 + 14 * a + 4 * s) * KB, align_bytes=64)
                 for s in range(2)
             ]
             for a in range(PASSES)
@@ -90,10 +94,6 @@ def tile_list_rgg_reluP_kernel(
             load_weight_scales(w, q)
         for s in range(2):
             nc.sync.dma_start(wb_raw[1][s][:], wb_rows[1, s])
-        wa_raw = laid.tile([P, PASSES, N], I32, name="wa_raw", offset=42 * KB, align_bytes=64)
-        nc.sync.dma_start(wa_raw[:], wa_words.rearrange("a p n i -> p a (n i)").bitcast(I32))
-        wc_raw = laid.tile([P, PASSES, 2 * N], U8, name="wc_raw", offset=4 * KB, align_bytes=64)
-        nc.sync.dma_start(wc_raw[:].bitcast(I32), wc_words.rearrange("a p b -> p a b").bitcast(I32))
 
         windows = [keep.tile([P, T], F32, name="window%d" % t) for t in range(PACK)]
         nc.vector.memset(windows[0][:, : T // 2 + 1], 0.0)
@@ -116,19 +116,21 @@ def tile_list_rgg_reluP_kernel(
                     )
             return moved
 
-        edge_sc = [gather_scales(0, keep.tile([P, LISTS, HALF], U8, name="early_sc", align_bytes=64))]
-        edge_w = keep.tile([P, J], F32, name="edge_w")
+        edge_sc = [gather_scales(0, laid.tile([P, LISTS, HALF], U8, name="early_sc", offset=70 * KB, align_bytes=64))]
+        wa_raw = laid.tile([P, PASSES, N], I32, name="wa_raw", offset=42 * KB, align_bytes=64)
+        nc.sync.dma_start(wa_raw[:], wa_words.rearrange("a p n i -> p a (n i)").bitcast(I32))
+        wc_raw = laid.tile([P, PASSES, 2 * N], U8, name="wc_raw", offset=4 * KB, align_bytes=64)
+        nc.sync.dma_start(wc_raw[:].bitcast(I32), wc_words.rearrange("a p b -> p a b").bitcast(I32))
+        edge_w = laid.tile([P, J], F32, name="edge_w", offset=70 * KB, align_bytes=64)
         nc.sync.dma_start(edge_w[:], wgo)
+        early_pairs = laid.tile([P, HALF + J], U32, name="early_pairs", offset=20 * KB, align_bytes=64)
+        table = tab_w[:].bitcast(U32)
+        nc.vector.tensor_copy(early_pairs[:, HALF:], table.indirect(src_list[:]))
+        nc.vector.tensor_copy(early_pairs[:, :HALF], table.indirect(offsets(1, 0)))
 
-        pairs = laid.tile([P, LISTS, J], U32, name="pairs", offset=20 * KB, align_bytes=64)
-        for l in range(LISTS):
-            nc.vector.tensor_copy(pairs[:, l, :], tab_w[:].bitcast(U32).indirect(lists[l][:]))
-
-        def part(h, target):
-            nc.vector.tensor_copy(
-                target[:].bitcast(U16),
-                pairs[:, :, h * HALF : (h + 1) * HALF].bitcast(U16).rearrange("p l (j a) -> p l a j", a=PASSES),
-            )
+        def part(pairs, name, offset):
+            target = laid.tile([P, PASSES, 2 * pairs.shape[1]], U8, name=name, offset=offset, align_bytes=64)
+            nc.vector.tensor_copy(target[:].bitcast(U16), pairs.bitcast(U16).rearrange("p (j a) -> p a j", a=PASSES))
             return target
 
         wa_sc = laid.tile([P, PASSES, N], U8, name="wa_sc", offset=0, align_bytes=64)
@@ -154,24 +156,26 @@ def tile_list_rgg_reluP_kernel(
             nc.vector.quantize_mx(out=wb_q[a][:].bitcast(FP8X4), scales=wb_sc[a][:], in_=wb_grouped[a][:])
 
         wb_grouped = [round_wb(a) for a in range(PASSES)]
-        picked = [part(0, laid.tile([P, LISTS, PASSES, 2 * HALF], U8, name="picked0", offset=50 * KB, align_bytes=64))]
         quantise_wb(0)
-        wa_q = laid.tile([P, PASSES, N], I32, name="wa_q", offset=8 * KB, align_bytes=64)
-        nc.vector.tensor_copy(
-            wa_q[:].rearrange("p a (t m e) -> p a m t e", t=PACK, e=LINE),
-            wa_raw[:].rearrange("p a (m e t) -> p a m t e", t=PACK, e=LINE),
-        )
+        early = part(early_pairs[:, :J], "early", 52 * KB)
         quantise_wb(1)
-        wc_q = laid.tile([P, PASSES, 2 * N], U8, name="wc_q", offset=60 * KB, align_bytes=64)
-        nc.vector.tensor_copy(
+        late_pairs = laid.tile([P, HALF], U32, name="late_pairs", offset=64 * KB, align_bytes=64)
+        nc.vector.tensor_copy(late_pairs[:], table.indirect(offsets(1, 1)))
+        wa_q = laid.tile([P, PASSES, N], U32, name="wa_q", offset=8 * KB, align_bytes=64)
+        nc.scalar.copy(
+            wa_q[:].rearrange("p a (t m e) -> p a m t e", t=PACK, e=LINE),
+            wa_raw[:].bitcast(U32).rearrange("p a (m e t) -> p a m t e", t=PACK, e=LINE),
+        )
+        wc_q = laid.tile([P, PASSES, 2 * N], U8, name="wc_q", offset=14 * KB, align_bytes=64)
+        nc.scalar.copy(
             wc_q[:].bitcast(U16).rearrange("p a (t m) -> p a t m", t=PACK),
             wc_raw[:].bitcast(U16).rearrange("p a (m t) -> p a t m", t=PACK),
         )
-        picked.append(part(1, laid.tile([P, LISTS, PASSES, 2 * HALF], U8, name="picked1", offset=63 * KB, align_bytes=64)))
-        edge_sc.append(gather_scales(1, laid.tile([P, LISTS, HALF], U8, name="late_sc", offset=62 * KB, align_bytes=64)))
+        late = (part(early_pairs[:, J:], "late0", 67 * KB), part(late_pairs[:], "late1", 56 * KB))
 
         def moving(l, h, a):
-            return dict(rhs=picked[h][:, l, a, :].bitcast(FP4X4), rhs_scale=edge_sc[h][:, a, l, :])
+            words = late[l][:, a, :] if h else early[:, a, 2 * HALF * (1 - l) : 2 * HALF * (2 - l)]
+            return dict(rhs=words.bitcast(FP4X4), rhs_scale=edge_sc[h][:, a, l, :])
 
         steps = [(t, h) for h in range(HALVES) for t in range(PACK)]
         eta = [keep.tile([P, J], F32, name="eta%d" % t) for t in range(PACK)]
@@ -182,10 +186,10 @@ def tile_list_rgg_reluP_kernel(
 
         def bank(t, h, is_gate):
             k = steps.index((t, h))
-            first_steps = ((3, 0), (1, 2), (0, 2))
+            first_steps = ((3, 0), (0, 1))
             if k < len(first_steps):
                 return BANK * first_steps[k][is_gate]
-            in_turn = (1, 0, 2)
+            in_turn = (0, 1, 2)
             return BANK * in_turn[(2 * k + is_gate) % len(in_turn)]
 
         def gate(t, h):
@@ -193,7 +197,7 @@ def tile_list_rgg_reluP_kernel(
             za = psum.tile([P, HALF], F32, name="za%d_%d" % (t, h), offset=bank(t, h, 1))
             from_wa = [(wa_q[:, a, m], wa_sc[:, a, m], 1, a) for a in range(PASSES)]
             from_wb = [(wb_q[a][:, m], wb_sc[a][:, m], 0, a) for a in range(PASSES)]
-            terms = from_wb[:1] + from_wa + from_wb[1:] if (t, h) == (0, 0) else from_wb[::-1] + from_wa
+            terms = from_wa + from_wb if (t, h) in ((1, 0), (2, 0)) else from_wb + from_wa
             for i, (words, scales, l, a) in enumerate(terms):
                 nc.tensor.matmul_mx(
                     out=za[:], lhsT=words.bitcast(FP8X4), lhsT_scale=scales,
@@ -217,9 +221,10 @@ def tile_list_rgg_reluP_kernel(
         def kept_message(t, h):
             nc.scalar.activation(kept[t][:, edges(h)], message(t, h)[:], RELU)
 
+        edge_sc.append(gather_scales(1, laid.tile([P, LISTS, HALF], U8, name="late_sc", offset=66 * KB, align_bytes=64)))
         gate(0, 0)
-        gate(1, 0)
         first_ms = message(0, 0)
+        gate(1, 0)
         kept_message(1, 0)
         for t, h in steps[2:]:
             kept_message(t, h)
@@ -240,7 +245,7 @@ def tile_list_rgg_reluP_kernel(
 
         place = (24 * KB, 26 * KB, 28 * KB, 30 * KB)
         first_values = keep.tile([P, HALF], F32, name="first_values")
-        nc.vector.scalar_tensor_tensor(first_values[:], first_ms[:], 0.0, weigh(eta, 0, edges(0), place[0])[:], MAX, MULT)
+        nc.vector.scalar_tensor_tensor(first_values[:], first_ms[:], 0.0, weigh(eta, 0, edges(0), 64 * KB)[:], MAX, MULT)
         ready.append((0, edges(0), first_values))
         finish(kept, 1, edges(0), weigh(eta, 1, edges(0), place[1]))
         finish(eta, 2, edges(0), weigh(kept, 2, edges(0), place[1]))

@@ -34,6 +34,7 @@ WC_ROWS = (4, 36, 60, 92)
 LINE = 4
 CHUNK = 512
 OWN = 928
+EARLY = 768
 KB = 1024
 BANK = 2 * KB
 
@@ -53,7 +54,7 @@ def tile_list_rgg_reluP_kernel(
         lists = (src_list, dst_list)
 
         warm = keep.tile([P, 2], F32, name="warm")
-        nc.gpsimd.memset(warm[:, :1], 0.0)
+        nc.vector.memset(warm[:, :1], 0.0)
         nc.scalar.activation(warm[:, 1:], warm[:, :1], SIGMOID)
 
         w_sc_raw = laid.tile([P, PASSES, N], U8, name="w_sc_raw", offset=12 * KB, align_bytes=64)
@@ -104,19 +105,23 @@ def tile_list_rgg_reluP_kernel(
         def offsets(l, h):
             return lists[l][:, h * HALF // 16 : (h + 1) * HALF // 16]
 
-        def gather_scales(h, picked_sc):
-            moved = keep.tile([P, PASSES, LISTS, HALF], U8, name="edge_sc%d_0" % h, align_bytes=64)
-            for l in range(LISTS):
-                nc.vector.tensor_copy(picked_sc[:, l, :], tab_sc[:].indirect(offsets(l, h)))
+        edge_sc = keep.tile([P, PASSES, 2 * J], U8, name="edge_sc", align_bytes=64)
+
+        def gather_scales(picked_sc, first_column, runs):
+            at = 0
+            for l, first, last in runs:
+                nc.vector.tensor_copy(picked_sc[:, at : at + last - first], tab_sc[:].indirect(lists[l][:, first // 16 : last // 16]))
+                at = at + last - first
             for a in range(PASSES):
                 for s in range(2):
                     first = TAB_FIRST + ROWS * (2 * a + s)
                     nc.sync.dma_start(
-                        moved[SIDE * s : SIDE * (s + 1), a].bitcast(I32), picked_sc[first : first + SIDE].bitcast(I32)
+                        edge_sc[SIDE * s : SIDE * (s + 1), a, first_column : first_column + at].bitcast(I32),
+                        picked_sc[first : first + SIDE].bitcast(I32),
                     )
-            return moved
 
-        edge_sc = [gather_scales(0, laid.tile([P, LISTS, HALF], U8, name="early_sc", offset=70 * KB, align_bytes=64))]
+        early_sc = laid.tile([P, HALF + EARLY], U8, name="early_sc", offset=70 * KB, align_bytes=64)
+        gather_scales(early_sc, 0, ((1, 0, HALF), (0, 0, EARLY)))
         wa_raw = laid.tile([P, PASSES, N], I32, name="wa_raw", offset=42 * KB, align_bytes=64)
         nc.sync.dma_start(wa_raw[:], wa_words.rearrange("a p n i -> p a (n i)").bitcast(I32))
         wc_raw = laid.tile([P, PASSES, 2 * N], U8, name="wc_raw", offset=4 * KB, align_bytes=64)
@@ -147,9 +152,9 @@ def tile_list_rgg_reluP_kernel(
 
         def round_wb(a):
             grouped = laid.tile([P, N * PACK], BF16, name="wb_grouped%d" % a, offset=(32, 36)[a] * KB, align_bytes=64)
-            by_column = grouped[:].rearrange("p (t s m i) -> p s m t i", t=PACK, s=2, i=PACK)
+            by_column = grouped[:].rearrange("p (t s m i) -> p s m i t", t=PACK, s=2, i=PACK)
             for s in range(2):
-                nc.scalar.copy(by_column[:, s], wb_raw[a][s][:].rearrange("p i (m t) -> p m t i", t=PACK))
+                nc.scalar.copy(by_column[:, s], wb_raw[a][s][:].rearrange("p i (m t) -> p m i t", t=PACK))
             return grouped
 
         def quantise_wb(a):
@@ -161,11 +166,16 @@ def tile_list_rgg_reluP_kernel(
         quantise_wb(1)
         late_pairs = laid.tile([P, HALF], U32, name="late_pairs", offset=64 * KB, align_bytes=64)
         nc.vector.tensor_copy(late_pairs[:], table.indirect(offsets(1, 1)))
-        wa_q = laid.tile([P, PASSES, N], U32, name="wa_q", offset=8 * KB, align_bytes=64)
-        nc.scalar.copy(
-            wa_q[:].rearrange("p a (t m e) -> p a m t e", t=PACK, e=LINE),
-            wa_raw[:].bitcast(U32).rearrange("p a (m e t) -> p a m t e", t=PACK, e=LINE),
-        )
+        wa_q = []
+
+        def deal_wa(u, offset):
+            wa_q.append(laid.tile([P, PASSES, 2 * P], U32, name="wa_q%d" % u, offset=offset, align_bytes=64))
+            nc.scalar.copy(
+                wa_q[u][:].rearrange("p a (t m e) -> p a m t e", t=2, e=LINE),
+                wa_raw[:].bitcast(U32).rearrange("p a (m e t) -> p a m t e", t=PACK, e=LINE)[:, :, :, 2 * u : 2 * u + 2, :],
+            )
+
+        deal_wa(0, 16 * KB)
         wc_q = laid.tile([P, PASSES, 2 * N], U8, name="wc_q", offset=14 * KB, align_bytes=64)
         nc.scalar.copy(
             wc_q[:].bitcast(U16).rearrange("p a (t m) -> p a t m", t=PACK),
@@ -175,10 +185,11 @@ def tile_list_rgg_reluP_kernel(
 
         def moving(l, h, a):
             words = late[l][:, a, :] if h else early[:, a, 2 * HALF * (1 - l) : 2 * HALF * (2 - l)]
-            return dict(rhs=words.bitcast(FP4X4), rhs_scale=edge_sc[h][:, a, l, :])
+            return dict(rhs=words.bitcast(FP4X4), rhs_scale=edge_sc[:, a, HALF * (3 * h if l else 1 + h) :][:, :HALF])
 
-        steps = [(t, h) for h in range(HALVES) for t in range(PACK)]
+        steps = [(t, h) for h in range(HALVES) for t in range(PACK - 1)] + [(PACK - 1, h) for h in range(HALVES)]
         eta = [keep.tile([P, J], F32, name="eta%d" % t) for t in range(PACK)]
+        first_eta = laid.tile([P, HALF], F32, name="first_eta", offset=9 * KB, align_bytes=64)
         kept = [keep.tile([P, J], F32, name="kept%d" % t) for t in range(PACK)]
 
         def edges(h):
@@ -195,7 +206,7 @@ def tile_list_rgg_reluP_kernel(
         def gate(t, h):
             m = slice(t * P, (t + 1) * P)
             za = psum.tile([P, HALF], F32, name="za%d_%d" % (t, h), offset=bank(t, h, 1))
-            from_wa = [(wa_q[:, a, m], wa_sc[:, a, m], 1, a) for a in range(PASSES)]
+            from_wa = [(wa_q[t // 2][:, a, t % 2 * P : (t % 2 + 1) * P], wa_sc[:, a, m], 1, a) for a in range(PASSES)]
             from_wb = [(wb_q[a][:, m], wb_sc[a][:, m], 0, a) for a in range(PASSES)]
             terms = from_wa + from_wb if (t, h) in ((1, 0), (2, 0)) else from_wb + from_wa
             for i, (words, scales, l, a) in enumerate(terms):
@@ -203,7 +214,7 @@ def tile_list_rgg_reluP_kernel(
                     out=za[:], lhsT=words.bitcast(FP8X4), lhsT_scale=scales,
                     start=(i == 0), stop=(i == len(terms) - 1), **moving(l, h, a),
                 )
-            nc.scalar.activation(eta[t][:, edges(h)], za[:], SIGMOID)
+            nc.scalar.activation(first_eta[:] if (t, h) == (0, 0) else eta[t][:, edges(h)], za[:], SIGMOID)
 
         def message(t, h):
             ms = psum.tile([P, HALF], F32, name="ms%d_%d" % (t, h), offset=bank(t, h, 0))
@@ -221,11 +232,15 @@ def tile_list_rgg_reluP_kernel(
         def kept_message(t, h):
             nc.scalar.activation(kept[t][:, edges(h)], message(t, h)[:], RELU)
 
-        edge_sc.append(gather_scales(1, laid.tile([P, LISTS, HALF], U8, name="late_sc", offset=66 * KB, align_bytes=64)))
+        late_sc = laid.tile([P, J - EARLY + HALF], U8, name="late_sc", offset=66 * KB, align_bytes=64)
+        gather_scales(late_sc, HALF + EARLY, ((0, EARLY, J), (1, HALF, J)))
         gate(0, 0)
         first_ms = message(0, 0)
         gate(1, 0)
         kept_message(1, 0)
+        first_weighted = laid.tile([P, HALF], F32, name="first_weighted", offset=64 * KB, align_bytes=64)
+        nc.gpsimd.tensor_tensor(first_weighted[:], first_eta[:], edge_w[:, edges(0)], MULT)
+        deal_wa(1, 8 * KB)
         for t, h in steps[2:]:
             kept_message(t, h)
             gate(t, h)
@@ -245,7 +260,7 @@ def tile_list_rgg_reluP_kernel(
 
         place = (24 * KB, 26 * KB, 28 * KB, 30 * KB)
         first_values = keep.tile([P, HALF], F32, name="first_values")
-        nc.vector.scalar_tensor_tensor(first_values[:], first_ms[:], 0.0, weigh(eta, 0, edges(0), 64 * KB)[:], MAX, MULT)
+        nc.vector.scalar_tensor_tensor(first_values[:], first_ms[:], 0.0, first_weighted[:], MAX, MULT)
         ready.append((0, edges(0), first_values))
         finish(kept, 1, edges(0), weigh(eta, 1, edges(0), place[1]))
         finish(eta, 2, edges(0), weigh(kept, 2, edges(0), place[1]))

@@ -30,7 +30,7 @@ QUADS = P // QUAD
 ROWS = 4
 SIDE = P // 2
 TAB_FIRST = 48
-WC_ROWS = (4, 36, 60, 92)
+W_FIRST = (32, 48)
 LINE = 4
 CHUNK = 512
 OWN = 928
@@ -71,14 +71,10 @@ def tile_list_rgg_reluP_kernel(
         tab_w = keep.tile([P, T], I32, name="tab_w", align_bytes=64)
         nc.sync.dma_start(tab_w[:], tab_words[0].rearrange("p t i -> p (t i)").bitcast(I32))
 
-        def load_weight_scales(w, q):
-            first = (QUAD * q, WC_ROWS[q])[w]
+        for w, scales in enumerate((wa_scales, wc_scales)):
             nc.sync.dma_start(
-                w_sc_raw[first : first + ROWS, :, :].bitcast(I32),
-                (wa_scales, wc_scales)[w][:, ROWS * q : ROWS * (q + 1), :].rearrange("a r n -> r a n").bitcast(I32),
+                w_sc_raw[W_FIRST[w] : W_FIRST[w] + 16].bitcast(I32), scales.rearrange("a r n -> r a n").bitcast(I32)
             )
-
-        scale_loads = [(w, q) for w in range(2) for q in range(QUADS)]
         wb_raw = [
             [
                 laid.tile([P, PACK, N // 2], F32, name="wb_raw%d_%d" % (a, s), offset=(46 + 14 * a + 4 * s) * KB, align_bytes=64)
@@ -87,14 +83,9 @@ def tile_list_rgg_reluP_kernel(
             for a in range(PASSES)
         ]
         wb_rows = wb.rearrange("(a p i) (s n) -> a s p i n", p=P, i=PACK, s=2)
-        for w, q in scale_loads[:3]:
-            load_weight_scales(w, q)
-        for s in range(2):
-            nc.sync.dma_start(wb_raw[0][s][:], wb_rows[0, s])
-        for w, q in scale_loads[3:]:
-            load_weight_scales(w, q)
-        for s in range(2):
-            nc.sync.dma_start(wb_raw[1][s][:], wb_rows[1, s])
+        for a in range(PASSES):
+            for s in range(2):
+                nc.sync.dma_start(wb_raw[a][s][:], wb_rows[a, s])
 
         windows = [keep.tile([P, T], F32, name="window%d" % t) for t in range(PACK)]
         nc.vector.memset(windows[0][:, : T // 2 + 1], 0.0)
@@ -127,7 +118,6 @@ def tile_list_rgg_reluP_kernel(
         wc_raw = laid.tile([P, PASSES, 2 * N], U8, name="wc_raw", offset=4 * KB, align_bytes=64)
         nc.sync.dma_start(wc_raw[:].bitcast(I32), wc_words.rearrange("a p b -> p a b").bitcast(I32))
         edge_w = laid.tile([P, J], F32, name="edge_w", offset=70 * KB, align_bytes=64)
-        nc.sync.dma_start(edge_w[:], wgo)
         early_pairs = laid.tile([P, HALF + J], U32, name="early_pairs", offset=20 * KB, align_bytes=64)
         table = tab_w[:].bitcast(U32)
         nc.vector.tensor_copy(early_pairs[:, HALF:], table.indirect(src_list[:]))
@@ -137,15 +127,6 @@ def tile_list_rgg_reluP_kernel(
             target = laid.tile([P, PASSES, 2 * pairs.shape[1]], U8, name=name, offset=offset, align_bytes=64)
             nc.vector.tensor_copy(target[:].bitcast(U16), pairs.bitcast(U16).rearrange("p (j a) -> p a j", a=PASSES))
             return target
-
-        wa_sc = laid.tile([P, PASSES, N], U8, name="wa_sc", offset=0, align_bytes=64)
-        wc_sc = keep.tile([P, PASSES, N], U8, name="wc_sc", align_bytes=64)
-        nc.vector.tensor_copy(
-            wa_sc[:].rearrange("p a (t m) -> p a t m", t=PACK), w_sc_raw[:].rearrange("p a (m t) -> p a t m", t=PACK)
-        )
-        for s in range(2):
-            first = WC_ROWS[2 * s]
-            nc.sync.dma_start(wc_sc[SIDE * s : SIDE * (s + 1)].bitcast(I32), wa_sc[first : first + SIDE].bitcast(I32))
 
         wb_q = [keep.tile([P, N], U32, name="wb_q%d" % a, align_bytes=64) for a in range(PASSES)]
         wb_sc = [keep.tile([P, N], U8, name="wb_sc%d" % a, align_bytes=64) for a in range(PASSES)]
@@ -161,21 +142,30 @@ def tile_list_rgg_reluP_kernel(
             nc.vector.quantize_mx(out=wb_q[a][:].bitcast(FP8X4), scales=wb_sc[a][:], in_=wb_grouped[a][:])
 
         wb_grouped = [round_wb(a) for a in range(PASSES)]
+        dealt_sc = laid.tile([P, PASSES, N], U8, name="dealt_sc", offset=51 * KB, align_bytes=64)
+        nc.vector.tensor_copy(
+            dealt_sc[:].rearrange("p a (t m) -> p a t m", t=PACK), w_sc_raw[:].rearrange("p a (m t) -> p a t m", t=PACK)
+        )
+        wa_sc = laid.tile([P, PASSES, N], U8, name="wa_sc", offset=0, align_bytes=64)
+        wc_sc = keep.tile([P, PASSES, N], U8, name="wc_sc", align_bytes=64)
+        for w, target in enumerate((wa_sc, wc_sc)):
+            for q in range(QUADS):
+                first = W_FIRST[w] + ROWS * q
+                nc.sync.dma_start(
+                    target[QUAD * q : QUAD * (q + 1)].bitcast(I32), dealt_sc[first : first + QUAD].bitcast(I32)
+                )
+            if w == 0:
+                nc.sync.dma_start(edge_w[:], wgo)
         quantise_wb(0)
         early = part(early_pairs[:, :J], "early", 52 * KB)
         quantise_wb(1)
         late_pairs = laid.tile([P, HALF], U32, name="late_pairs", offset=64 * KB, align_bytes=64)
         nc.vector.tensor_copy(late_pairs[:], table.indirect(offsets(1, 1)))
-        wa_q = []
-
-        def deal_wa(u, offset):
-            wa_q.append(laid.tile([P, PASSES, 2 * P], U32, name="wa_q%d" % u, offset=offset, align_bytes=64))
-            nc.scalar.copy(
-                wa_q[u][:].rearrange("p a (t m e) -> p a m t e", t=2, e=LINE),
-                wa_raw[:].bitcast(U32).rearrange("p a (m e t) -> p a m t e", t=PACK, e=LINE)[:, :, :, 2 * u : 2 * u + 2, :],
-            )
-
-        deal_wa(0, 16 * KB)
+        wa_q = laid.tile([P, PASSES, N], U32, name="wa_q", offset=8 * KB, align_bytes=64)
+        nc.scalar.copy(
+            wa_q[:].rearrange("p a (t m e) -> p a m t e", t=PACK, e=LINE),
+            wa_raw[:].bitcast(U32).rearrange("p a (m e t) -> p a m t e", t=PACK, e=LINE),
+        )
         wc_q = laid.tile([P, PASSES, 2 * N], U8, name="wc_q", offset=14 * KB, align_bytes=64)
         nc.scalar.copy(
             wc_q[:].bitcast(U16).rearrange("p a (t m) -> p a t m", t=PACK),
@@ -187,9 +177,8 @@ def tile_list_rgg_reluP_kernel(
             words = late[l][:, a, :] if h else early[:, a, 2 * HALF * (1 - l) : 2 * HALF * (2 - l)]
             return dict(rhs=words.bitcast(FP4X4), rhs_scale=edge_sc[:, a, HALF * (3 * h if l else 1 + h) :][:, :HALF])
 
-        steps = [(t, h) for h in range(HALVES) for t in range(PACK - 1)] + [(PACK - 1, h) for h in range(HALVES)]
+        steps = [(t, h) for h in range(HALVES) for t in range(PACK)]
         eta = [keep.tile([P, J], F32, name="eta%d" % t) for t in range(PACK)]
-        first_eta = laid.tile([P, HALF], F32, name="first_eta", offset=9 * KB, align_bytes=64)
         kept = [keep.tile([P, J], F32, name="kept%d" % t) for t in range(PACK)]
 
         def edges(h):
@@ -200,13 +189,13 @@ def tile_list_rgg_reluP_kernel(
             first_steps = ((3, 0), (0, 1))
             if k < len(first_steps):
                 return BANK * first_steps[k][is_gate]
-            in_turn = (0, 1, 2)
+            in_turn = (0, 1, 3)
             return BANK * in_turn[(2 * k + is_gate) % len(in_turn)]
 
         def gate(t, h):
             m = slice(t * P, (t + 1) * P)
             za = psum.tile([P, HALF], F32, name="za%d_%d" % (t, h), offset=bank(t, h, 1))
-            from_wa = [(wa_q[t // 2][:, a, t % 2 * P : (t % 2 + 1) * P], wa_sc[:, a, m], 1, a) for a in range(PASSES)]
+            from_wa = [(wa_q[:, a, m], wa_sc[:, a, m], 1, a) for a in range(PASSES)]
             from_wb = [(wb_q[a][:, m], wb_sc[a][:, m], 0, a) for a in range(PASSES)]
             terms = from_wa + from_wb if (t, h) in ((1, 0), (2, 0)) else from_wb + from_wa
             for i, (words, scales, l, a) in enumerate(terms):
@@ -214,7 +203,7 @@ def tile_list_rgg_reluP_kernel(
                     out=za[:], lhsT=words.bitcast(FP8X4), lhsT_scale=scales,
                     start=(i == 0), stop=(i == len(terms) - 1), **moving(l, h, a),
                 )
-            nc.scalar.activation(first_eta[:] if (t, h) == (0, 0) else eta[t][:, edges(h)], za[:], SIGMOID)
+            nc.scalar.activation(eta[t][:, edges(h)], za[:], SIGMOID)
 
         def message(t, h):
             ms = psum.tile([P, HALF], F32, name="ms%d_%d" % (t, h), offset=bank(t, h, 0))
@@ -239,8 +228,7 @@ def tile_list_rgg_reluP_kernel(
         gate(1, 0)
         kept_message(1, 0)
         first_weighted = laid.tile([P, HALF], F32, name="first_weighted", offset=64 * KB, align_bytes=64)
-        nc.gpsimd.tensor_tensor(first_weighted[:], first_eta[:], edge_w[:, edges(0)], MULT)
-        deal_wa(1, 8 * KB)
+        nc.gpsimd.tensor_tensor(first_weighted[:], eta[0][:, edges(0)], edge_w[:, edges(0)], MULT)
         for t, h in steps[2:]:
             kept_message(t, h)
             gate(t, h)

@@ -68,6 +68,16 @@ def tile_list_rgg_reluP_kernel(
             nc.sync.dma_start(tab_sc[first : first + 16, :].bitcast(I32), sc_rows[e].bitcast(I32))
         nc.sync.dma_start(src_list[:], offs)
         nc.sync.dma_start(dst_list[:], offs2)
+        wb_rows = wb.rearrange("(a p i) n -> a p i n", p=P, i=PACK)
+        wb_raw = [[], []]
+
+        def load_wb(a, first, last):
+            offset = (46 + 14 * a) * KB + first * PACK * 4
+            raw = laid.tile([P, PACK, last - first], F32, name="wb_raw%d_%d" % (a, first), offset=offset, align_bytes=64)
+            nc.sync.dma_start(raw[:], wb_rows[a, :, :, first:last])
+            wb_raw[a].append((first, last, raw))
+
+        load_wb(0, 0, N // 4)
         tab_w = keep.tile([P, T], I32, name="tab_w", align_bytes=64)
         nc.sync.dma_start(tab_w[:], tab_words[0].rearrange("p t i -> p (t i)").bitcast(I32))
 
@@ -75,17 +85,8 @@ def tile_list_rgg_reluP_kernel(
             nc.sync.dma_start(
                 w_sc_raw[W_FIRST[w] : W_FIRST[w] + 16].bitcast(I32), scales.rearrange("a r n -> r a n").bitcast(I32)
             )
-        wb_raw = [
-            [
-                laid.tile([P, PACK, N // 2], F32, name="wb_raw%d_%d" % (a, s), offset=(46 + 14 * a + 4 * s) * KB, align_bytes=64)
-                for s in range(2)
-            ]
-            for a in range(PASSES)
-        ]
-        wb_rows = wb.rearrange("(a p i) (s n) -> a s p i n", p=P, i=PACK, s=2)
-        for a in range(PASSES):
-            for s in range(2):
-                nc.sync.dma_start(wb_raw[a][s][:], wb_rows[a, s])
+        for a, first, last in ((0, N // 4, N // 2), (0, N // 2, N), (1, 0, N // 2), (1, N // 2, N)):
+            load_wb(a, first, last)
 
         windows = [keep.tile([P, T], F32, name="window%d" % t) for t in range(PACK)]
         nc.vector.memset(windows[0][:, : T // 2 + 1], 0.0)
@@ -133,9 +134,9 @@ def tile_list_rgg_reluP_kernel(
 
         def round_wb(a):
             grouped = laid.tile([P, N * PACK], BF16, name="wb_grouped%d" % a, offset=(32, 36)[a] * KB, align_bytes=64)
-            by_column = grouped[:].rearrange("p (t s m i) -> p s m i t", t=PACK, s=2, i=PACK)
-            for s in range(2):
-                nc.scalar.copy(by_column[:, s], wb_raw[a][s][:].rearrange("p i (m t) -> p m i t", t=PACK))
+            by_column = grouped[:].rearrange("p (t m i) -> p m i t", t=PACK, i=PACK)
+            for first, last, raw in wb_raw[a]:
+                nc.scalar.copy(by_column[:, first // PACK : last // PACK], raw[:].rearrange("p i (m t) -> p m i t", t=PACK))
             return grouped
 
         def quantise_wb(a):

@@ -116,8 +116,6 @@ def tile_list_rgg_reluP_kernel(
         gather_scales(early_sc, 0, ((1, 0, HALF), (0, 0, EARLY)))
         wa_raw = laid.tile([P, PASSES, N], I32, name="wa_raw", offset=42 * KB, align_bytes=64)
         nc.sync.dma_start(wa_raw[:], wa_words.rearrange("a p n i -> p a (n i)").bitcast(I32))
-        wc_raw = laid.tile([P, PASSES, 2 * N], U8, name="wc_raw", offset=4 * KB, align_bytes=64)
-        nc.sync.dma_start(wc_raw[:].bitcast(I32), wc_words.rearrange("a p b -> p a b").bitcast(I32))
         edge_w = laid.tile([P, J], F32, name="edge_w", offset=70 * KB, align_bytes=64)
         early_pairs = laid.tile([P, HALF + J], U32, name="early_pairs", offset=20 * KB, align_bytes=64)
         table = tab_w[:].bitcast(U32)
@@ -156,17 +154,24 @@ def tile_list_rgg_reluP_kernel(
                     target[QUAD * q : QUAD * (q + 1)].bitcast(I32), dealt_sc[first : first + QUAD].bitcast(I32)
                 )
             if w == 0:
+                wc_raw = laid.tile([P, PASSES, 2 * N], U8, name="wc_raw", offset=11 * KB, align_bytes=64)
+                nc.sync.dma_start(wc_raw[:].bitcast(I32), wc_words.rearrange("a p b -> p a b").bitcast(I32))
                 nc.sync.dma_start(edge_w[:], wgo)
         quantise_wb(0)
         early = part(early_pairs[:, :J], "early", 52 * KB)
         quantise_wb(1)
         late_pairs = laid.tile([P, HALF], U32, name="late_pairs", offset=64 * KB, align_bytes=64)
         nc.vector.tensor_copy(late_pairs[:], table.indirect(offsets(1, 1)))
-        wa_q = laid.tile([P, PASSES, N], U32, name="wa_q", offset=8 * KB, align_bytes=64)
-        nc.scalar.copy(
-            wa_q[:].rearrange("p a (t m e) -> p a m t e", t=PACK, e=LINE),
-            wa_raw[:].bitcast(U32).rearrange("p a (m e t) -> p a m t e", t=PACK, e=LINE),
-        )
+        wa_q = []
+
+        def deal_wa(u, offset):
+            wa_q.append(laid.tile([P, PASSES, 2 * P], U32, name="wa_q%d" % u, offset=offset, align_bytes=64))
+            nc.scalar.copy(
+                wa_q[u][:].rearrange("p a (t m e) -> p a m t e", t=2, e=LINE),
+                wa_raw[:].bitcast(U32).rearrange("p a (m e t) -> p a m t e", t=PACK, e=LINE)[:, :, :, 2 * u : 2 * u + 2, :],
+            )
+
+        deal_wa(0, 16 * KB)
         wc_q = laid.tile([P, PASSES, 2 * N], U8, name="wc_q", offset=14 * KB, align_bytes=64)
         nc.scalar.copy(
             wc_q[:].bitcast(U16).rearrange("p a (t m) -> p a t m", t=PACK),
@@ -180,6 +185,7 @@ def tile_list_rgg_reluP_kernel(
 
         steps = [(t, h) for h in range(HALVES) for t in range(PACK)]
         eta = [keep.tile([P, J], F32, name="eta%d" % t) for t in range(PACK)]
+        first_eta = laid.tile([P, HALF], F32, name="first_eta", offset=8 * KB, align_bytes=64)
         kept = [keep.tile([P, J], F32, name="kept%d" % t) for t in range(PACK)]
 
         def edges(h):
@@ -196,7 +202,7 @@ def tile_list_rgg_reluP_kernel(
         def gate(t, h):
             m = slice(t * P, (t + 1) * P)
             za = psum.tile([P, HALF], F32, name="za%d_%d" % (t, h), offset=bank(t, h, 1))
-            from_wa = [(wa_q[:, a, m], wa_sc[:, a, m], 1, a) for a in range(PASSES)]
+            from_wa = [(wa_q[t // 2][:, a, t % 2 * P : (t % 2 + 1) * P], wa_sc[:, a, m], 1, a) for a in range(PASSES)]
             from_wb = [(wb_q[a][:, m], wb_sc[a][:, m], 0, a) for a in range(PASSES)]
             terms = from_wa + from_wb if (t, h) in ((1, 0), (2, 0)) else from_wb + from_wa
             for i, (words, scales, l, a) in enumerate(terms):
@@ -204,7 +210,7 @@ def tile_list_rgg_reluP_kernel(
                     out=za[:], lhsT=words.bitcast(FP8X4), lhsT_scale=scales,
                     start=(i == 0), stop=(i == len(terms) - 1), **moving(l, h, a),
                 )
-            nc.scalar.activation(eta[t][:, edges(h)], za[:], SIGMOID)
+            nc.scalar.activation(first_eta[:] if (t, h) == (0, 0) else eta[t][:, edges(h)], za[:], SIGMOID)
 
         def message(t, h):
             ms = psum.tile([P, HALF], F32, name="ms%d_%d" % (t, h), offset=bank(t, h, 0))
@@ -229,7 +235,8 @@ def tile_list_rgg_reluP_kernel(
         gate(1, 0)
         kept_message(1, 0)
         first_weighted = laid.tile([P, HALF], F32, name="first_weighted", offset=64 * KB, align_bytes=64)
-        nc.gpsimd.tensor_tensor(first_weighted[:], eta[0][:, edges(0)], edge_w[:, edges(0)], MULT)
+        nc.gpsimd.tensor_tensor(first_weighted[:], first_eta[:], edge_w[:, edges(0)], MULT)
+        deal_wa(1, 8 * KB)
         for t, h in steps[2:]:
             kept_message(t, h)
             gate(t, h)

from contextlib import ExitStack

import concourse.mybir as mybir

K, N, T, J = 1024, 512, 2048, 1024
FLOPS = 3 * 2 * K * N * J

F32 = mybir.dt.float32
BF16 = mybir.dt.bfloat16
I32 = mybir.dt.int32
U32 = mybir.dt.uint32
U16 = mybir.dt.uint16
U8 = mybir.dt.uint8
FP8X4 = mybir.dt.float8_e4m3fn_x4
FP4X4 = mybir.dt.float4_e2m1fn_x4
MULT = mybir.AluOpType.mult
ADD = mybir.AluOpType.add
MAX = mybir.AluOpType.max
SIGMOID = mybir.ActivationFunctionType.Sigmoid
RELU = mybir.ActivationFunctionType.Relu

P = 128
PACK = 4
PASSES = K // (P * PACK)
LISTS = 2
HALF = 512
HALVES = J // HALF
QUAD = 32
QUADS = P // QUAD
ROWS = 4
SIDE = P // 2
TAB_FIRST = 48
W_FIRST = (32, 48)
LINE = 4
CHUNK = 512
OWN = 928
EARLY = 768
KB = 1024
BANK = 2 * KB


def tile_list_rgg_reluP_kernel(
    tc, tab_words, tab_scales, wa_words, wa_scales, wb, wc_words, wc_scales, wgo, offs, offs2, out_0, out_1, out_2
):
    nc = tc.nc
    with ExitStack() as ctx:
        held = ctx.enter_context(tc.tile_pool(name="held", bufs=1))
        keep = ctx.enter_context(tc.tile_pool(name="keep", bufs=1))
        laid = ctx.enter_context(tc.tile_pool(name="laid", bufs=1))
        psum = ctx.enter_context(tc.psum_pool(name="psum", bufs=1))

        src_list = held.tile([P, J // 16], U16, name="src_list")
        dst_list = held.tile([P, J // 16], U16, name="dst_list")
        lists = (src_list, dst_list)

        warm = keep.tile([P, 2], F32, name="warm")
        nc.vector.memset(warm[:, :1], 0.0)
        nc.scalar.activation(warm[:, 1:], warm[:, :1], SIGMOID)

        w_sc_raw = laid.tile([P, PASSES, N], U8, name="w_sc_raw", offset=12 * KB, align_bytes=64)
        tab_sc = keep.tile([P, T], U8, name="tab_sc", align_bytes=64)
        nc.gpsimd.memset(w_sc_raw[:].bitcast(I32), 0)
        for first, last in ((0, TAB_FIRST), (SIDE, TAB_FIRST + QUAD), (3 * QUAD, P)):
            nc.gpsimd.memset(tab_sc[first:last, :].bitcast(I32), 0)
        sc_rows = tab_scales.rearrange("a (h e r) t -> e (a h) r t", e=2, r=ROWS)
        for e in range(2):
            first = TAB_FIRST + QUAD * e
            nc.sync.dma_start(tab_sc[first : first + 16, :].bitcast(I32), sc_rows[e].bitcast(I32))
        nc.sync.dma_start(src_list[:], offs)
        nc.sync.dma_start(dst_list[:], offs2)
        wb_rows = wb.rearrange("(a p i) n -> a p i n", p=P, i=PACK)
        wb_raw = [[], []]

        def load_wb(a, first, last):
            offset = (46 + 14 * a) * KB + first * PACK * 4
            raw = laid.tile([P, PACK, last - first], F32, name="wb_raw%d_%d" % (a, first), offset=offset, align_bytes=64)
            nc.sync.dma_start(raw[:], wb_rows[a, :, :, first:last])
            wb_raw[a].append((first, last, raw))

        load_wb(0, 0, N // 4)
        tab_w = keep.tile([P, T], I32, name="tab_w", align_bytes=64)
        nc.sync.dma_start(tab_w[:], tab_words[0].rearrange("p t i -> p (t i)").bitcast(I32))

        for w, scales in enumerate((wa_scales, wc_scales)):
            nc.sync.dma_start(
                w_sc_raw[W_FIRST[w] : W_FIRST[w] + 16].bitcast(I32), scales.rearrange("a r n -> r a n").bitcast(I32)
            )
        for a, first, last in ((0, N // 4, N // 2), (0, N // 2, N), (1, 0, N // 2), (1, N // 2, N)):
            load_wb(a, first, last)

        windows = [keep.tile([P, T], F32, name="window%d" % t) for t in range(PACK)]
        nc.vector.memset(windows[0][:, : T // 2 + 1], 0.0)
        nc.vector.memset(windows[0][:, T // 2 + 1 :], 0.0)
        for window in windows[1:]:
            nc.gpsimd.memset(window[:], 0.0)

        def offsets(l, h):
            return lists[l][:, h * HALF // 16 : (h + 1) * HALF // 16]

        edge_sc = keep.tile([P, PASSES, 2 * J], U8, name="edge_sc", align_bytes=64)

        def gather_scales(picked_sc, first_column, runs):
            at = 0
            for l, first, last in runs:
                nc.vector.tensor_copy(picked_sc[:, at : at + last - first], tab_sc[:].indirect(lists[l][:, first // 16 : last // 16]))
                at = at + last - first
            for a in range(PASSES):
                for s in range(2):
                    first = TAB_FIRST + ROWS * (2 * a + s)
                    nc.sync.dma_start(
                        edge_sc[SIDE * s : SIDE * (s + 1), a, first_column : first_column + at].bitcast(I32),
                        picked_sc[first : first + SIDE].bitcast(I32),
                    )

        early_sc = laid.tile([P, HALF + EARLY], U8, name="early_sc", offset=70 * KB, align_bytes=64)
        gather_scales(early_sc, 0, ((1, 0, HALF), (0, 0, EARLY)))
        wa_raw = laid.tile([P, PASSES, N], I32, name="wa_raw", offset=42 * KB, align_bytes=64)
        nc.sync.dma_start(wa_raw[:], wa_words.rearrange("a p n i -> p a (n i)").bitcast(I32))
        edge_w = laid.tile([P, J], F32, name="edge_w", offset=70 * KB, align_bytes=64)
        early_pairs = laid.tile([P, HALF + J], U32, name="early_pairs", offset=20 * KB, align_bytes=64)
        table = tab_w[:].bitcast(U32)
        nc.vector.tensor_copy(early_pairs[:, HALF:], table.indirect(src_list[:]))
        nc.vector.tensor_copy(early_pairs[:, :HALF], table.indirect(offsets(1, 0)))

        def part(pairs, name, offset):
            target = laid.tile([P, PASSES, 2 * pairs.shape[1]], U8, name=name, offset=offset, align_bytes=64)
            nc.vector.tensor_copy(target[:].bitcast(U16), pairs.bitcast(U16).rearrange("p (j a) -> p a j", a=PASSES))
            return target

        wb_q = [keep.tile([P, N], U32, name="wb_q%d" % a, align_bytes=64) for a in range(PASSES)]
        wb_sc = [keep.tile([P, N], U8, name="wb_sc%d" % a, align_bytes=64) for a in range(PASSES)]

        def round_wb(a):
            grouped = laid.tile([P, N * PACK], BF16, name="wb_grouped%d" % a, offset=(32, 36)[a] * KB, align_bytes=64)
            by_column = grouped[:].rearrange("p (t m i) -> p m i t", t=PACK, i=PACK)
            for first, last, raw in wb_raw[a]:
                nc.scalar.copy(by_column[:, first // PACK : last // PACK], raw[:].rearrange("p i (m t) -> p m i t", t=PACK))
            return grouped

        def quantise_wb(a):
            nc.vector.quantize_mx(out=wb_q[a][:].bitcast(FP8X4), scales=wb_sc[a][:], in_=wb_grouped[a][:])

        wb_grouped = [round_wb(a) for a in range(PASSES)]
        dealt_sc = laid.tile([P, PASSES, N], U8, name="dealt_sc", offset=51 * KB, align_bytes=64)
        nc.vector.tensor_copy(
            dealt_sc[:].rearrange("p a (t m) -> p a t m", t=PACK), w_sc_raw[:].rearrange("p a (m t) -> p a t m", t=PACK)
        )
        wa_sc = laid.tile([P, PASSES, N], U8, name="wa_sc", offset=0, align_bytes=64)
        wc_sc = keep.tile([P, PASSES, N], U8, name="wc_sc", align_bytes=64)
        for w, target in enumerate((wa_sc, wc_sc)):
            for q in range(QUADS):
                first = W_FIRST[w] + ROWS * q
                nc.sync.dma_start(
                    target[QUAD * q : QUAD * (q + 1)].bitcast(I32), dealt_sc[first : first + QUAD].bitcast(I32)
                )
            if w == 0:
                wc_raw = laid.tile([P, PASSES, 2 * N], U8, name="wc_raw", offset=11 * KB, align_bytes=64)
                nc.sync.dma_start(wc_raw[:].bitcast(I32), wc_words.rearrange("a p b -> p a b").bitcast(I32))
                nc.sync.dma_start(edge_w[:], wgo)
        quantise_wb(0)
        early = part(early_pairs[:, :J], "early", 52 * KB)
        quantise_wb(1)
        late_pairs = laid.tile([P, HALF], U32, name="late_pairs", offset=64 * KB, align_bytes=64)
        nc.vector.tensor_copy(late_pairs[:], table.indirect(offsets(1, 1)))
        wa_q = []

        def deal_wa(u, offset):
            wa_q.append(laid.tile([P, PASSES, 2 * P], U32, name="wa_q%d" % u, offset=offset, align_bytes=64))
            nc.scalar.copy(
                wa_q[u][:].rearrange("p a (t m e) -> p a m t e", t=2, e=LINE),
                wa_raw[:].bitcast(U32).rearrange("p a (m e t) -> p a m t e", t=PACK, e=LINE)[:, :, :, 2 * u : 2 * u + 2, :],
            )

        deal_wa(0, 16 * KB)
        wc_q = laid.tile([P, PASSES, 2 * N], U8, name="wc_q", offset=14 * KB, align_bytes=64)
        nc.scalar.copy(
            wc_q[:].bitcast(U16).rearrange("p a (t m) -> p a t m", t=PACK),
            wc_raw[:].bitcast(U16).rearrange("p a (m t) -> p a t m", t=PACK),
        )
        late = (part(early_pairs[:, J:], "late0", 67 * KB), part(late_pairs[:], "late1", 56 * KB))

        def moving(l, h, a):
            words = late[l][:, a, :] if h else early[:, a, 2 * HALF * (1 - l) : 2 * HALF * (2 - l)]
            return dict(rhs=words.bitcast(FP4X4), rhs_scale=edge_sc[:, a, HALF * (3 * h if l else 1 + h) :][:, :HALF])

        steps = [(t, h) for h in range(HALVES) for t in range(PACK)]
        eta = [keep.tile([P, J], F32, name="eta%d" % t) for t in range(PACK)]
        first_eta = laid.tile([P, HALF], F32, name="first_eta", offset=8 * KB, align_bytes=64)
        kept = [keep.tile([P, J], F32, name="kept%d" % t) for t in range(PACK)]

        def edges(h):
            return slice(h * HALF, (h + 1) * HALF)

        def bank(t, h, is_gate):
            k = steps.index((t, h))
            first_steps = ((3, 0), (0, 1))
            if k < len(first_steps):
                return BANK * first_steps[k][is_gate]
            in_turn = (0, 1, 3)
            return BANK * in_turn[(2 * k + is_gate) % len(in_turn)]

        def gate(t, h):
            m = slice(t * P, (t + 1) * P)
            za = psum.tile([P, HALF], F32, name="za%d_%d" % (t, h), offset=bank(t, h, 1))
            from_wa = [(wa_q[t // 2][:, a, t % 2 * P : (t % 2 + 1) * P], wa_sc[:, a, m], 1, a) for a in range(PASSES)]
            from_wb = [(wb_q[a][:, m], wb_sc[a][:, m], 0, a) for a in range(PASSES)]
            terms = from_wa + from_wb if (t, h) in ((1, 0), (2, 0)) else from_wb + from_wa
            for i, (words, scales, l, a) in enumerate(terms):
                nc.tensor.matmul_mx(
                    out=za[:], lhsT=words.bitcast(FP8X4), lhsT_scale=scales,
                    start=(i == 0), stop=(i == len(terms) - 1), **moving(l, h, a),
                )
            nc.scalar.activation(first_eta[:] if (t, h) == (0, 0) else eta[t][:, edges(h)], za[:], SIGMOID)

        def message(t, h):
            ms = psum.tile([P, HALF], F32, name="ms%d_%d" % (t, h), offset=bank(t, h, 0))
            for a in range(PASSES):
                nc.tensor.matmul_mx(
                    out=ms[:],
                    lhsT=wc_q[:, a, 2 * t * P : 2 * (t + 1) * P].bitcast(FP4X4),
                    lhsT_scale=wc_sc[:, a, t * P : (t + 1) * P],
                    start=(a == 0),
                    stop=(a == PASSES - 1),
                    **moving(0, h, a),
                )
            return ms

        def kept_message(t, h):
            nc.scalar.activation(kept[t][:, edges(h)], message(t, h)[:], RELU)

        late_sc = laid.tile([P, J - EARLY + HALF], U8, name="late_sc", offset=66 * KB, align_bytes=64)
        gather_scales(late_sc, HALF + EARLY, ((0, EARLY, J), (1, HALF, J)))
        gate(0, 0)
        first_ms = message(0, 0)
        gate(1, 0)
        kept_message(1, 0)
        first_weighted = laid.tile([P, HALF], F32, name="first_weighted", offset=64 * KB, align_bytes=64)
        nc.gpsimd.tensor_tensor(first_weighted[:], first_eta[:], edge_w[:, edges(0)], MULT)
        deal_wa(1, 8 * KB)
        for t, h in steps[2:]:
            kept_message(t, h)
            gate(t, h)

        def weigh(factor, t, js, offset):
            name = "weighted%d_%d" % (t, js.start)
            weighted = laid.tile([P, js.stop - js.start], F32, name=name, offset=offset, align_bytes=64)
            nc.gpsimd.tensor_tensor(weighted[:], factor[t][:, js], edge_w[:, js], MULT)
            return weighted

        ready = []

        def finish(factor, t, js, weighted):
            values = keep.tile([P, js.stop - js.start], F32, name="values%d_%d" % (t, js.start))
            nc.gpsimd.tensor_tensor(values[:], weighted[:], factor[t][:, js], MULT)
            ready.append((t, js, values))

        place = (24 * KB, 26 * KB, 28 * KB, 30 * KB)
        first_values = keep.tile([P, HALF], F32, name="first_values")
        nc.vector.scalar_tensor_tensor(first_values[:], first_ms[:], 0.0, first_weighted[:], MAX, MULT)
        ready.append((0, edges(0), first_values))
        finish(kept, 1, edges(0), weigh(eta, 1, edges(0), place[1]))
        finish(eta, 2, edges(0), weigh(kept, 2, edges(0), place[1]))
        later = [(t, edges(1)) for t in range(PACK - 1)] + [(PACK - 1, slice(0, J))]
        waiting = weigh(kept, *later[0], place[1])
        for i, (t, js) in enumerate(later[:-1]):
            ahead = weigh(kept, *later[i + 1], place[(2, 0, 3)[i]])
            finish(eta, t, js, waiting)
            waiting = ahead
        finish(eta, *later[-1], waiting)

        spans = ((0, 2 * CHUNK), (2 * CHUNK, CHUNK // 2), (5 * CHUNK // 2, 3 * CHUNK // 2))
        y_bf = [
            laid.tile([P, width, PACK], BF16, name="y_bf%d" % c, offset=(0, 8 * KB, place[1])[c], align_bytes=64)
            for c, (first, width) in enumerate(spans)
        ]
        out_rows = out_0.rearrange("(p t) c -> t p c", t=PACK)
        out_words = out_1[0].rearrange("p c i -> p (c i)").bitcast(I32)

        for t, js, values in ready:
            window = windows[t]
            nc.vector.tensor_copy(window[:].indirect(dst_list[:, js.start // 16 : js.stop // 16]), values[:])
            if js.stop < J:
                continue
            nc.sync.dma_start(out_rows[t], window[:])
            for c in (1, 0, 2):
                first, count = spans[c]
                piece = window[:, first : first + count]
                both = piece.unsqueeze(2).to_broadcast([P, count, 2])
                if t == PACK - 1 and c == 0:
                    nc.vector.tensor_copy(y_bf[c][:, :OWN, t], piece[:, :OWN])
                    nc.scalar.copy(y_bf[c][:, OWN:, t], piece[:, OWN:])
                elif t < 2 and c == 2:
                    nc.gpsimd.tensor_scalar(y_bf[c][:, :, t], piece, 1.0, -0.0, MULT, ADD)
                elif t == 2 and c == 2:
                    nc.gpsimd.tensor_scalar(y_bf[c][:, :, t:], both, 1.0, -0.0, MULT, ADD)
                elif t == 2 and c == 0:
                    nc.scalar.copy(y_bf[c][:, :, t:], both)
                elif c == 2:
                    for cols in (slice(0, CHUNK), slice(CHUNK, count)):
                        nc.scalar.copy(y_bf[c][:, cols, t], piece[:, cols])
                else:
                    nc.scalar.copy(y_bf[c][:, :, t], piece)

        codes = keep.tile([P, T], I32, name="y_codes", align_bytes=64)
        y_sc = keep.tile([P, CHUNK], U8, name="y_sc", align_bytes=64)
        width = CHUNK // 2
        for pieces in ((4,), (1, 0), (3, 2), (5, 6), (7,)):
            for u in pieces:
                first = u * width
                c = max(i for i in range(len(spans)) if spans[i][0] <= first)
                o = first - spans[c][0]
                nc.vector.quantize_mx(
                    out=codes[:, first : first + width].bitcast(FP8X4),
                    scales=y_sc[ROWS * (u // 2) :, u % 2 * width : (u % 2 + 1) * width],
                    in_=y_bf[c][:, o : o + width].rearrange("p c i -> p (c i)"),
                )
            cols = slice(min(pieces) * width, (max(pieces) + 1) * width)
            nc.sync.dma_start(out_words[:, cols], codes[:, cols])
        out_scales = out_2[0].rearrange("(q r) (g c) -> q g r c", r=ROWS, c=CHUNK)
        for q in range(QUADS):
            (nc.scalar if q % 2 else nc.sync).dma_start(
                out_scales[q].bitcast(I32), y_sc[QUAD * q : QUAD * q + 16, :].bitcast(I32)
            )
